import numpy as np, ml_dtypes
CORES = [8,9,10,11,12,13]
N = 6
BF = ml_dtypes.bfloat16
V, B, L, CAP, RO = 640, 768, 256, 48, 4
W, NB = N * V, N * B
def by_good(a):
    return np.ascontiguousarray(a.reshape(N, 8, 16, -1).transpose(1, 0, 3, 2)).reshape(8, -1, 16)
def by_rank(a):
    return np.ascontiguousarray(a.reshape(8, N, -1, 16).transpose(1, 0, 3, 2)).reshape(N, 128, -1)
def money(rng, lo, hi):
    return (0.5 + 0.5 * rng.random((8, NB, 16))) * np.exp2(rng.integers(lo, hi, (8, NB, 1)))
def rooms(rng):
    n = rng.choice(np.array([0, 1, 2, 3, 6, 16]), (8, W, 1), p=[0.1, 0.35, 0.25, 0.15, 0.1, 0.05])
    return np.argsort(rng.random((8, W, 16)), axis=-1) < n
def lodge(rng, room, stay, first, old, fixed=()):
    H = np.where(room, 0, NB + 1).astype(np.int64); hold = np.full((8, NB), W, np.int64)
    for g in range(8):
        h = H[g].reshape(-1).copy(); free = room[g].reshape(-1).copy(); st = stay[g].copy()
        for m, x, s, b, sign in fixed:
            if m == g: h[16 * x + s] = sign * (b + 1); free[16 * x + s] = False; st[b] = False; hold[g, b] = x
        key = np.where(free, rng.random(16 * W) + np.repeat(first[g], 16), 1e9)
        names = rng.permutation(np.flatnonzero(st)); n = min(len(names), int(np.count_nonzero(free)))
        names = names[:n]; pl = np.argsort(key)[:n]
        h[pl] = (names + 1) * np.where(rng.random(n) < old[g][pl // 16], -1, 1); hold[g, names] = pl // 16
        H[g] = h.reshape(W, 16)
    return H, hold
def parts(rng):
    n = W // 8; hot = np.argsort(rng.random((8, W)), axis=1)[:, :n]; F = rng.integers(0, W, (8, NB, 16)); first = np.ones((8, W))
    for g in range(8):
        F[g] = np.where(rng.random((NB, 16)) < 0.5, hot[g][rng.integers(0, n, (NB, 16))], F[g]); first[g, hot[g]] = 0.0
    U = rng.integers(1, 16, (8, NB, 16)); A = rng.random((8, W, 16), dtype=np.float32) * np.float32(0.75) + np.float32(0.25)
    return F, U, A, money(rng, -1, 2), rooms(rng), rng.random((8, NB)) < 0.42, first, rng.random((8, W))
def pack(F, U, M, A, H, hold):
    return {"ft": by_rank(F).astype(np.int32), "ut": by_rank(U).astype(np.float32).astype(BF), "mon": by_rank(M).astype(np.float32).astype(BF), "al": by_rank(A).astype(np.float32),
            "hn": by_rank(H).astype(np.int32), "hb": np.ascontiguousarray(hold.reshape(8, N, B).transpose(1, 0, 2)).astype(np.int32)}
def chain(n, k):
    c = np.float32(1.0)
    for i in range(n): c = c * np.float32(0.9375)
    return c if k == 0 else np.nextafter(c, np.float32(0.0 if k < 0 else 2.0))
def pair(rng, i):
    u = 2 ** int(rng.integers(0, 4)); c = (0.6 + 0.39 * rng.random(4096)).astype(np.float32); w = c.astype(np.float64)
    if i == 0:
        ux, uy = ((15, 13), (9, 15), (13, 11), (11, 9))[int(rng.integers(0, 4))]; lo, hi = 0.5 * max(ux, uy) + 0.01, min(ux, uy) - 0.01
        p = lo + (hi - lo) * rng.random(4096); a = (p * float(ux) ** -1.0).astype(np.float32); b = (p * float(uy) ** -1.0).astype(np.float32)
        k = np.flatnonzero((np.float32(ux) * a == np.float32(uy) * b) & (ux * a.astype(np.float64) < uy * b.astype(np.float64)))[:16]
        return ux, uy, a[k], b[k], False
    if i == 1:
        r = c * np.float32(0.9375); k = np.flatnonzero(r.astype(np.float64) > w * 0.9375)[:16]
        return u, u, c[k], r[k], True
    if i == 2:
        r = c * np.float32(0.9375) * np.float32(0.9375); k = np.flatnonzero(r > (w * 0.87890625).astype(np.float32))[:16]
        return u, u, c[k], r[k], True
    if i == 3:
        a = (rng.integers(2 ** 21, 2 ** 22, 16) * 2.0 ** -24).astype(np.float32)
        return u, u, a, np.nextafter(a, np.float32(1.0)), False
    if i == 4:
        j = rng.integers(3100000, 5500000, 16); a = (j * 2.0 ** -24).astype(np.float32); low = rng.permutation(16) >= int(rng.integers(8, 16))
        return 15, 5, np.where(low, a * np.float32(0.75), a), (3 * j * 2.0 ** -24).astype(np.float32), False
    a = c[:16].copy(); k = int(rng.integers(0, 16)); a[k] = np.nextafter(a[k], np.float32(0.0))
    return u, u, a, c[:16].copy(), False
def setup_inputs(rng):
    F, U, A, M, room, stay, first, old = parts(rng)
    H, hold = lodge(rng, room, stay, first, old)
    return pack(F, U, M, A, H, hold)
def setup_inputs_spread(rng):
    F, U, A, M, room, stay, first, old = parts(rng)
    A = np.clip(np.exp2(-1.5 * (rng.random((8, W, 1)) + rng.random((8, W, 16)))), 0.125, 1.0); M = money(rng, -1, 3)
    F = np.minimum((W * rng.random(F.shape) ** 3).astype(np.int64), W - 1); F[1::2] = W - 1 - F[1::2]
    U = np.minimum(np.exp2(4 * rng.random(U.shape)).astype(np.int64), 15)
    first = np.tile(np.arange(W) * (8.0 / W), (8, 1)); first[1::2] = first[1::2, ::-1]
    H, hold = lodge(rng, room, stay, first, old)
    return pack(F, U, M, A, H, hold)
def setup_inputs_ends(rng):
    F, U, A, M, room, stay, first, old = parts(rng)
    e = rng.random((8, N, B)) < 0.72; e[:, :, B - 1] = True
    F = np.where(e.reshape(8, NB, 1), (W - 1) * rng.integers(0, 2, F.shape), rng.integers(0, W, F.shape))
    U = 1 + 14 * rng.integers(0, 2, U.shape); A = np.where(rng.random(A.shape) < 0.5, 0.125, 1.0)
    A[::2, 0] = 1.0; A[::2, W - 1] = 1.0
    for i in range(16): A[:, W - 2 - i] = 0.125; A[:, W - 2 - i, i] = 1.0
    b = np.arange(7, NB, 32); F[:, b] = W - 2 - np.argsort(rng.random((8, len(b), 16)), axis=-1); U[:, b] = 15
    M = np.where(rng.random(M.shape) < 0.5, 0.25, 4.0)
    stay = rng.random((8, NB)) < 0.36; room[:, 0] = False; room[:, 0, :N] = True; fixed = []
    for g in range(8):
        z = (g % N) * V + V - 1; room[g, z] = False; room[g, z, 15] = True
        if g % 4 == 0: room[g, 0, N] = True; fixed.append((g, 0, N, NB - 1, 1))
        else: fixed.append((g, z, 15, NB - 1, -1))
        for q in range(N): fixed.append((g, 0, q, q * B, 1 if g % 4 == 0 else 1 - 2 * int(rng.integers(0, 2))))
    H, hold = lodge(rng, room, stay, first, old, fixed)
    return pack(F, U, M, A, H, hold)
def setup_inputs_corners(rng):
    F, U, A, M, room, stay, first, old = parts(rng)
    n = rng.choice(np.array([0, 1, 1, 2, 8, 15, 16]), (8, W, 1)); kind = rng.integers(0, 3, (8, W, 1)); i = np.arange(16)
    room = np.where(kind == 0, i < n, np.where(kind == 1, i >= 16 - n, np.argsort(rng.random((8, W, 16)), axis=-1) < n))
    first = 2.0 * n[:, :, 0]; old = rng.choice(np.array([0.0, 0.5, 1.0]), (8, W)); stay = np.ones((8, NB), bool)
    F = np.where(rng.random(F.shape) < 0.1, V * rng.integers(0, N, F.shape) + (V - 1) * rng.integers(0, 2, F.shape), F)
    sh = int(rng.integers(0, 8)); counts = [0, 1, 2, 3, L - 1, L, L + 1, B]
    for g in range(8):
        for q in range(N):
            hm = np.sort(rng.permutation(B)[:counts[(g + q + sh) % 8]]); stay[g, q * B + hm] = False
            lane = hm[:L]; o = (q + 1 + rng.permutation(N - 1)) % N; rest = np.append(o[3:], q)
            to = np.concatenate([np.repeat(o[0], CAP), np.repeat(o[1], CAP + 1), np.repeat(o[2], CAP - 1), rng.choice(rest, L - 3 * CAP)])
            to = rng.permutation(to[:len(lane)])
            v = rng.integers(0, V, (len(lane), 16))
            if g % 2: v = rng.integers(0, 24, v.shape) + (V - 24) * rng.integers(0, 2, v.shape)
            F[g, q * B + lane] = V * to[:, None] + v
    z = rng.random(M.shape)
    M = np.where(z < 0.5, 4.0, np.where(z < 0.7, 0.25, M))
    H, hold = lodge(rng, room, stay, first, old)
    return pack(F, U, M, A, H, hold)
def setup_inputs_crowd(rng):
    F, U, A, M, room, stay, first, old = parts(rng)
    for g, x, y, c in ((0, W - 1, 0, chain(RO - 1, -1)), (1, 0, W - 1, chain(RO - 1, 0)), (2, V, V - 1, chain(RO - 1, 1)), (3, W - 1, V // 2, chain(1, 0))):
        stay[g] = False; F[g] = x; F[g, :, 0] = y; U[g] = 15; A[g, x] = 1.0; A[g, y] = c; room[g, x] = False; room[g, y] = False
        if g == 3: room[g, x, 15] = True
        if g >= 2:
            for q in range(N):
                b = q * B + np.arange(int(rng.integers(0, L)), B, L); F[g, b] = rng.integers(0, W, (len(b), 16)); U[g, b] = rng.integers(1, 16, (len(b), 16))
    few = rng.permutation(W)[:4]; F[4] = few[rng.integers(0, 4, F[4].shape)]; first[4, few] = -1.0
    one = V * np.arange(N) + rng.integers(0, V, N); F[5] = one[rng.integers(0, N, F[5].shape)]; first[5, one] = -1.0
    owner = int(rng.integers(0, N)); home = (owner + 1 + int(rng.integers(0, N - 1))) % N
    pv = owner * V + rng.permutation(V); xs, rest = pv[:N * CAP], pv[N * CAP:]; sl = rng.integers(0, 16, N * CAP); held = home * B + CAP + rng.permutation(B - CAP)[:N * CAP]
    bs = (B * np.arange(N)[:, None] + np.arange(CAP)).reshape(-1)
    for g in (6, 7): stay[g, bs] = False; F[g, bs] = xs[:, None]; room[g, xs] = False
    room[7, rest[:N]] = False
    for q in range(N):
        b = q * B + np.arange(CAP, L); stay[7, b] = False
        F[7, b] = np.append(rng.permutation(np.delete(rest, q))[:L - CAP - 1], rest[q])[:, None]
    room[6, xs, sl] = True; fixed = [(6, int(xs[i]), int(sl[i]), int(held[i]), -1) for i in range(N * CAP)]
    H, hold = lodge(rng, room, stay, first, old, fixed)
    return pack(F, U, M, A, H, hold)
def setup_inputs_calm(rng):
    F, U, A, M, room, stay, first, old = parts(rng); ce = -(-L // N)
    for g in range(4):
        po = [o * V + rng.permutation(V) for o in range(N)]
        for o in range(N):
            sp = po[o][:N * ce]; room[g, sp] = False; room[g, sp, rng.integers(0, 16, len(sp))] = True; first[g, sp] = 50.0
        for q in range(N):
            hm = np.sort(rng.permutation(B)[:L + (g + q) % 4]); stay[g, q * B:(q + 1) * B] = True; stay[g, q * B + hm] = False
            for j in range(L): F[g, q * B + hm[j]] = po[(j + q) % N][q * ce + j // N]
            for r in range(len(hm) - L):
                x, y = po[(q + 1) % N][N * ce + 2 * r], po[(q + 1) % N][N * ce + 2 * r + 1]; b = q * B + hm[L + r]
                room[g, x] = False; room[g, y] = False; F[g, b] = x; F[g, b, 0] = y; U[g, b] = 15
                A[g, x] = 1.0; A[g, y] = chain(1 + (r + q + g) % (RO - 2), int(rng.integers(-1, 2)))
    lo = np.resize(np.array([0, 2, L, 1, 3, L - 1]), N); hi = np.resize(np.array([1, 3, 0, 2, B - L, B - L - 1]), N); S = 8 * (B // L + 1)
    for g in (4, 5):
        pv = np.argsort(rng.random((N, V)), axis=1); turn = rng.permutation(N); stay[g] = True
        for q in range(N):
            n, m = (int(lo[turn[q]]), B - L) if g == 4 else (L, int(hi[turn[q]]))
            b = np.concatenate([rng.permutation(L)[:n], L + rng.permutation(B - L)[:m]]); o = b % N; i = (b + 4) % L
            x = o * V + pv[o, np.where(i < 8, 1 + S * q + 8 * ((b + 4) // L) + i, 0)]
            stay[g, q * B + b] = False; F[g, q * B + b] = x[:, None]; room[g, x] = False
    home = int(rng.integers(0, N)); pv = np.argsort(rng.random((N, V)), axis=1); i = np.arange(B)
    goods = (i % N) * V + pv[i % N, i // N]; held = home * B + rng.permutation(B); sl = rng.integers(0, 16, B)
    stay[6, home * B:(home + 1) * B] = False; room[6, goods] = False; room[6, goods, sl] = True
    fixed = [(6, int(goods[j]), int(sl[j]), int(held[j]), -1) for j in range(B)]
    for j in range(N - 1):
        q = (home + 1 + j) % N; w = goods[j * L:(j + 1) * L]
        stay[6, q * B:q * B + L] = False; F[6, q * B + np.arange(len(w))] = w[:, None]
    xy = rng.permutation(W)[:N * 48].reshape(N, 24, 2); stay[7] = True; room[7, xy.reshape(-1)] = False; first[7, xy.reshape(-1)] = 50.0
    for q in range(N):
        hm = q * B + rng.permutation(B)[:24]; stay[7, hm] = False
        for j in range(24):
            x, y = int(xy[q, j, 0]), int(xy[q, j, 1]); b = int(hm[j]); ux, uy, ax, ay, shut = pair(rng, j % 6)
            F[7, b] = y; F[7, b, 0] = x; U[7, b] = uy; U[7, b, 0] = ux; A[7, x] = ax; A[7, y] = ay
            room[7, y, int(rng.integers(0, 16))] = True
            if not shut: room[7, x, int(rng.integers(0, 16))] = True
    H, hold = lodge(rng, room, stay, first, old, fixed)
    return pack(F, U, M, A, H, hold)
def check_ranges(d):
    bad = []
    for k, lo, hi in (("ft", 0, W - 1), ("ut", 1, 15), ("mon", 0.25, 4.0), ("al", 0.125, 1.0), ("hn", -NB, NB + 1), ("hb", 0, W)):
        v = np.asarray(d[k]).astype(np.float64)
        if not np.all((v >= lo) & (v <= hi)): bad.append("range of " + k)
    u = np.asarray(d["ut"]).astype(np.float64)
    if not np.all(u == np.rint(u)): bad.append("ut isn't whole")
    if not bad:
        H = np.abs(by_good(np.asarray(d["hn"])).astype(np.int64)); hb = np.asarray(d["hb"]).astype(np.int64).transpose(1, 0, 2).reshape(8, NB)
        for g in range(8):
            held = (H[g] > 0) & (H[g] <= NB); names = H[g][held] - 1; hold = np.full(NB, W, np.int64); hold[names] = np.nonzero(held)[0]
            if np.any(np.bincount(names, minlength=NB) > 1) or np.any(hold != hb[g]): bad.append("hn and hb of market %d" % g)
    return bad
def reference(ft, ut, mon, al, hn, hb):
    F = by_good(ft).astype(np.int64); U = by_good(ut).astype(np.float32); M = by_good(mon).astype(np.float64)
    A = by_good(al).astype(np.float32); H = by_good(hn).astype(np.int64)
    hold = np.ascontiguousarray(hb.transpose(1, 0, 2)).astype(np.int64).reshape(8, NB)
    for t in range(RO):
        order = (np.arange(B) + t * L) % B
        for g in range(8):
            goods, who, best = [], [], []
            for q in range(N):
                o = q * B + order; o = o[hold[g, o] == W][:L]; j = np.arange(len(o))
                fk = F[g, o]; e = U[g, o][:, :, None] * A[g][fk]
                top = e == np.max(e, axis=1, keepdims=True)
                k = np.argmax(np.add.reduce(top.astype(np.int64), axis=2), axis=1)
                x = fk[j, k]; to = ((x // V)[:, None] == np.arange(N)).astype(np.int64)
                ok = np.add.reduce(to * (np.add.accumulate(to, axis=0) - to), axis=1) < CAP
                goods.append(x[ok]); who.append(o[ok]); best.append(top[j, k][ok])
            x, at = np.unique(np.concatenate(goods), return_index=True)
            b = np.concatenate(who)[at]; m = np.concatenate(best)[at]; h = H[g, x]
            grade = np.where(h == 0, 0, np.where(h < 0, 16, 32)) + np.arange(16)
            s = np.argmin(grade, axis=1); fits = np.min(grade, axis=1) < 32
            r = np.flatnonzero(fits); out = h[r, s[r]]
            hold[g, -out[out < 0] - 1] = W
            h[r, s[r]] = b[r] + 1; hold[g, b[r]] = x[r]
            r = np.flatnonzero(~fits); h[r] = np.where(h[r] <= NB, -h[r], h[r])
            H[g, x] = h
            A[g, x[r]] = np.where(m[r], A[g, x[r]] * np.float32(0.9375), A[g, x[r]])
    P = np.stack([np.where((hold[g] < W)[:, None], M[g] * A[g][np.minimum(hold[g], W - 1)].astype(np.float64), 0.0) for g in range(8)])
    return {"yal": by_rank(A), "yh": by_rank(H).astype(np.float32), "yp": by_rank(P).astype(np.float32)}

def check_inputs(d):
    bad = list(check_ranges(d))
    if not bad:
        for name, y in reference(**d).items():
            for q in range(N):
                v = np.abs(np.asarray(y[q], np.float64)); s = np.sqrt(np.mean(v * v))
                if v.max() > 9 * s or s < 2.0 ** -3: bad.append('%s of rank %d is uneven or too small' % (name, q))
    return bad

@@ -1,0 +1,589 @@
+import math
+from concourse.bass import DstId, RemoteDMATransfer
+from concourse.mybir import AluOpType as A, ActivationFunctionType as F
+
+N, V, B, L, CAP, RO = 6, 640, 768, 256, 48, 4
+W = N * V
+SEG = (49, 33, 17)
+SB = (0, N * 49, N * 82)
+NE = N * 99
+f32, bf, i32, u16 = "float32", "bfloat16", "int32", "uint16"
+SCRATCH = {"ps": ("psum", [128, 4096], f32)}
+
+
+def _sb(dtype, **kw):
+    for k in kw:
+        SCRATCH[k] = ("sbuf", [128, kw[k]], dtype)
+
+
+for _t in range(2):
+    SCRATCH["aw%d" % _t] = ("sbuf", [128, W + 8], f32)
+    SCRATCH["ev%d" % _t] = ("sbuf", [128, 488], f32)
+    SCRATCH["tb%d" % _t] = ("sbuf", [128, N * CAP], f32)
+    SCRATCH["lb%d" % _t] = ("sbuf", [128, N * 24], u16)
+_sb(i32, fti=B, hni=V, hbi=B, pcol=4, ci=8, pk=B + 512, lw=2304, uti=L, xi=L, owi=L, pci=L, tgi=48, tg8=48)
+_sb(u16, offu=48, offc=48, gl=L, ku=16, bu=16, lu=24, tgu=48, finu=48)
+_sb(bf, utb=B, monb=B, ownb=B, lob=B, hib=B, idb=128, nid=128, bo=128, bo4=128, n2=128, m2=128, wn=128, wc=128,
+    d0=128, d1=128, d2=128, d3=128, sel=2048, x1=144, xe=144, xk=144, boz=128, bow=128, x8=144, x4=144, dc=48, jl=16,
+    h0=48, h1=48, cs=48, hd=48, hd1=48, ones=L, km=512, utl=L, pcb=L, top=4096, wv=L, ch=L, y2=L, ind=L, zz=L, zc=L,
+    tog=B, ka=V, kb=V, tgt=V, ntg=V, o1=V, r2=V)
+_sb(f32, cf=40, dm=128, tmp=128, tm2=128, crow=152, grow=128, r16=16, dg=16, pw=16, q16=16, z16=16, x1f=144, x4f=144,
+    x1g=128, c8=320, nam=2 * B, cpk=B, cdd=NE, eqb=NE, eqs=NE, mark=N * CAP, wc18=18, w18=18,
+    ag=4096, ms=4096, y1=L, xrow=264, sgn=L, vb=L, xb=1792, tw=1792, lsc=N * CAP, xg=B, xs=B, m48=48, t48=48, tg0=48,
+    tg1=48, tt=688, nab=80, hh=V, he=V, uu=V, tn=V, en=V, ff=V)
+SEMAPHORES = (["cv", "cs_", "cp", "cg"] + ["ld%d" % k for k in range(7)] + ["st%d" % k for k in range(4)]
+              + ["%s%d" % (p, t) for p in ("ab", "ae", "lt", "ll", "le") for t in range(RO)]
+              + ["%s%d" % (p, t) for p in ("aa", "la") for t in range(RO + 1)])
+MAGIC = 12582912.0
+LN = math.log(1.8)
+
+
+def rank_program(g, core, T, topo):
+    me = T.rank_of(core)
+    if me is None:
+        return
+    Q = {"v": g.vector, "s": g.scalar, "p": g.tensor, "g": g, "y": g.sync}
+    SEM = {"v": "cv", "s": "cs_", "p": "cp", "g": "cg"}
+    cnt = {"v": 0, "s": 0, "p": 0, "g": 0}
+    seen = {e: {} for e in Q}
+    wr, rd, ends = {}, {}, {}
+
+    def need(e, tok):
+        if tok[2] == "p" and e == "p":
+            return
+        if seen[e].get(tok[0], 0) < tok[1]:
+            Q[e].wait_ge(T.sem[tok[0]], tok[1])
+            seen[e][tok[0]] = tok[1]
+
+    def order(e, r, w):
+        for k in r:
+            if k in wr:
+                need(e, wr[k])
+            if k[0] == "P":
+                for tok in rd.get(k, []):
+                    if tok[2] != e:
+                        need(e, tok)
+        for k in w:
+            if k in wr:
+                need(e, wr[k])
+            for tok in rd.get(k, []):
+                need(e, tok)
+
+    def mark(tok, r, w):
+        for k in r:
+            rd.setdefault(k, []).append(tok)
+        for k in w:
+            wr[k] = tok
+            rd[k] = []
+
+    def op(e, fn, r, w, inc=True):
+        order(e, r, w)
+        ins = fn()
+        if inc:
+            cnt[e] += 1
+            ins.then_inc(T.sem[SEM[e]], 1)
+            mark((SEM[e], cnt[e], e), r, w)
+        else:
+            mark((SEM[e], cnt[e] + 1, e), r, w)
+
+    def dma(e, sem, out, in_, r, w):
+        order(e, r, w)
+        Q[e].dma_start(out, in_).then_inc(T.sem[sem], 16)
+        mark((sem, 16, "d"), r, w)
+        ends[sem] = 16
+
+    def ts(out, in0, s1, s2, o0, o1, r, w):
+        if o1 is None:
+            op("v", lambda: g.vector.tensor_scalar(out, in0, s1, None, o0), r, w)
+        else:
+            op("v", lambda: g.vector.tensor_scalar(out, in0, s1, s2, o0, o1), r, w)
+
+    def tt(out, a, b, o, r, w):
+        op("v", lambda: g.vector.tensor_tensor(out, a, b, o), r, w)
+
+    def cp(out, a, r, w):
+        op("v", lambda: g.vector.tensor_copy(out, a), r, w)
+
+    def ms(out, c, w):
+        op("v", lambda: g.vector.memset(out, c), [], w)
+
+    def scan(out, a, b, init, o0, o1, r, w):
+        op("v", lambda: g.vector.tensor_tensor_scan(out, a, b, init, o0, o1), r, w)
+
+    def act(out, a, func, r, w, bias=0.0, scale=1.0):
+        op("s", lambda: g.scalar.activation(out, a, func, bias=bias, scale=scale), r, w)
+
+    def mm(items, w, first=True, last=True):
+        for i, (o, l, x, r) in enumerate(items):
+            st, sp = first and i == 0, last and i == len(items) - 1
+            op("p", lambda: g.tensor.matmul(o, l, x, st, sp), r, w, inc=sp)
+
+    def iota(out, pat, base, mult, w, small=True):
+        if small:
+            op("g", lambda: g.iota(out, pat, base, mult, allow_small_or_imprecise_dtypes=True), [], w)
+        else:
+            op("g", lambda: g.iota(out, pat, base, mult), [], w)
+
+    others = [q for q in range(N) if q != me]
+
+    def did(q):
+        a = topo.addr(T.cores[q])
+        return DstId(rid=a[0], pnc=a[1])
+
+    def common(src):
+        return [e for e in topo.engines(T.cores[src], T.cores[(src + 1) % N])
+                if all(e in topo.engines(T.cores[src], T.cores[q]) for q in range(N) if q != src)]
+
+    def deal(src):
+        eng, dst = common(src), [q for q in range(N) if q != src]
+        n = {q: 1 for q in dst}
+        grow = True
+        while grow:
+            grow = False
+            for q in sorted(dst, key=lambda x: n[x]):
+                if sum(n.values()) + n[q] <= len(eng):
+                    n[q] *= 2
+                    grow = True
+                    break
+        out, at = {}, 0
+        for q in dst:
+            out[q] = eng[at:at + n[q]]
+            at += n[q]
+        return out
+
+    def bits(es):
+        return sum(1 << e for e in es)
+
+    def bcast(src, dst, rsem, lsem, r):
+        order("g", r, [])
+        es = common(me)
+        g.remote_dma_fused([RemoteDMATransfer(dst_ids=[did(q) for q in others], dma_engine_mask=bits(es),
+                                              remote_sem=T.sem[rsem], srcs=[src], dsts=[dst] * len(others))],
+                           local_sem=T.sem[lsem])
+        mark((lsem, len(es), "d"), r, [])
+        ends[lsem] = len(es)
+
+    nb = sum(len(common(q)) for q in others)
+
+    def arrive(key, sem, n):
+        wr[key] = (sem, n, "d")
+        ends[sem] = n
+
+    ps = T.ps
+    mine = slice(me * V, (me + 1) * V)
+
+    def col(j):
+        return T.cf[:, j:j + 1]
+
+    def sh(x, r):
+        return x[:, 15 - r:143 - r]
+
+    def wide(base, items, w):
+        for a, b, k in ((0, 512, w[0]), (512, V, w[1])):
+            mm([(ps[:, base + a:base + b], l, x[:, a:b], r) for (l, x, r) in items], [k])
+
+    def double(x, n, end, key):
+        while n < end:
+            m = min(n, end - n)
+            act(x[:, n:n + m], x[:, 0:m], F.Identity, [key], [key])
+            n += m
+
+    dma("y", "ld0", T.aw0[:, mine], T.al[:], [], ["aw0m"])
+    dma("s", "ld1", T.hbi[0:8, :], T.hb[:], [], ["hbi"])
+    dma("s", "ld2", T.fti[:], T.ft[:], [], ["fti"])
+    dma("y", "ld3", T.utb[:], T.ut[:], [], ["utb"])
+    dma("y", "ld4", T.hni[:], T.hn[:], [], ["hni"])
+    dma("y", "ld5", T.monb[:], T.mon[:], [], ["monb"])
+    iota(T.pcol[:, 0:1], [[0, 1]], 0, 1, ["pcol"], small=False)
+    iota(T.crow[:], [[1, 152]], 0, 0, ["crow"])
+    iota(T.dm[:], [[-1, 128]], 0, 1, ["dm"])
+    iota(T.grow[:], [[16, 8], [0, 16]], 0, 0, ["grow"])
+    iota(T.hib[:], [[1, 24], [0, 32]], 0, 0, ["hib"])
+    bcast(T.aw0[:, mine], T.aw0[:, mine], "aa0", "la0", ["aw0m"])
+    arrive("aw0r", "aa0", nb)
+    act(T.lob[:, 0:32], T.crow[:, 0:32], F.Identity, ["crow"], ["lob"])
+    double(T.lob, 32, B, "lob")
+    iota(T.mark[:], [[V, N], [1, CAP]], V + 1, 0, ["mark"])
+    iota(T.wc18[:], [[V, N], [0, 3]], 1001, 0, ["wc18"])
+    for c in range(3):
+        iota(T.cdd[:, SB[c]:SB[c] + N * SEG[c]], [[0, N], [1, SEG[c]]], 0, 0, ["cdd%d" % c])
+    iota(T.nam[:], [[0, 2], [1, B]], me * B + 1, 0, ["nam"])
+
+    (R, G16, O7, PF, UP, C15, NV, P15, RM1, EB, KW, EW, SS, NS, CA, CB, ZW, IW, R0, R1, NW, NC, WE, WO, S0, S1, T0, T1,
+     T2, T3, RH, NE_, D0, D1, D2) = range(35)
+
+    def lin(j, src, a, b):
+        act(col(j), col(src), F.Identity, ["c%d" % src], ["c%d" % j], bias=b, scale=a)
+
+    ts(T.ci[:, 0:1], T.pcol[:, 0:1], 15, None, A.bitwise_and, None, ["pcol"], ["ci0"])
+    ts(T.ci[:, 1:2], T.pcol[:, 0:1], 7, None, A.bitwise_and, None, ["pcol"], ["ci1"])
+    cp(col(PF), T.pcol[:, 0:1], ["pcol"], ["c3"])
+    ms(T.ones[:], 1.0, ["ones"])
+    cp(col(R), T.ci[:, 0:1], ["ci0"], ["c0"])
+    cp(col(O7), T.ci[:, 1:2], ["ci1"], ["c2"])
+    ts(col(P15), col(PF), 16.0, 15.0, A.mult, A.add, ["c3"], ["c7"])
+    ts(T.idb[:], T.dm[:], 0.0, None, A.is_equal, None, ["dm"], ["idb"])
+    tt(col(G16), col(PF), col(R), A.subtract, ["c3", "c0"], ["c1"])
+    ts(T.x4[:], T.crow[:, 0:144], col(P15), None, A.is_equal, None, ["crow", "c7"], ["x4"])
+    ts(T.dg[:], T.crow[:, 0:16], col(R), None, A.is_equal, None, ["crow", "c0"], ["dg"])
+    ts(T.bo[:], T.grow[:], col(G16), None, A.is_equal, None, ["grow", "c1"], ["bo"])
+    ts(T.tmp[:], T.dm[:], 0.0, -1.0, A.is_gt, A.mult, ["dm"], ["tmp"])
+    ts(T.tm2[:], T.dm[:], 0.0, col(R), A.is_equal, A.mult, ["dm", "c0"], ["tm2"])
+    ts(col(S0), col(R), 0.0, 524288.0, A.is_equal, A.mult, ["c0"], ["c24"])
+    ts(col(S1), col(R), 1.0, 524288.0, A.is_equal, A.mult, ["c0"], ["c25"])
+    ts(col(UP), col(R), 7.5, None, A.is_gt, None, ["c0"], ["c4"])
+    tt(T.tmp[:], T.tmp[:], T.bo[:], A.mult, ["tmp", "bo"], ["tmp"])
+    act(T.dc[:], T.crow[:, 0:48], F.Identity, ["crow"], ["dc"], bias=768.0, scale=16.0)
+    act(T.nid[:], T.idb[:], F.Identity, ["idb"], ["nid"], scale=-1.0)
+    lin(RM1, R, 1.0, -1.0)
+    act(T.d2[:], T.idb[:], F.Identity, ["idb"], ["d2"], scale=4096.0)
+    act(T.d3[:], T.idb[:], F.Identity, ["idb"], ["d3"], scale=65536.0)
+    act(T.d0[:], T.idb[:], F.Identity, ["idb", "c24"], ["d0"], scale=col(S0))
+    act(T.d1[:], T.idb[:], F.Identity, ["idb", "c25"], ["d1"], scale=col(S1))
+    lin(C15, G16, 1.0, 15.0)
+    for k in range(16):
+        act(T.sel[:, 128 * k:128 * k + 128], T.bo[:], F.Identity, ["bo", "dg"], ["sel%d" % k], scale=T.dg[:, k:k + 1])
+    ts(T.tog[0:8, :], T.hbi[0:8, :], float(W), None, A.is_equal, None, ["hbi"], ["tog"])
+    XL = ps[:, 3584:3632]
+    mm([(XL, T.x4[0:8, 15 - r:143 - r], T.tog[0:8, r:B:16], ["x4", "tog"]) for r in range(16)], ["P7"])
+    ts(T.xg[:], T.fti[:], 1.0 / V, -0.4992, A.mult, A.add, ["fti"], ["xg"])
+    tt(T.m2[:], T.tmp[:], T.tm2[:], A.subtract, ["tmp", "tm2"], ["m2"])
+    ts(T.ownb[:], T.xg[:], MAGIC, -MAGIC, A.add, A.add, ["xg"], ["ownb"])
+    for a, b, k in ((0, 512, "P0"), (512, B, "P1")):
+        mm([(ps[:, a:b], T.d0[:], T.lob[:, a:b], ["d0", "lob"]), (ps[:, a:b], T.d2[:], T.utb[:, a:b], ["d2", "utb"]),
+            (ps[:, a:b], T.d1[:], T.hib[:, a:b], ["d1", "hib"]), (ps[:, a:b], T.d3[:], T.ownb[:, a:b], ["d3", "ownb"])], [k])
+    ts(T.x1[:], T.crow[:, 0:144], col(C15), None, A.is_equal, None, ["crow", "c5"], ["x1"])
+    ts(col(T1), col(O7), 5.5, col(UP), A.is_lt, A.mult, ["c2", "c4"], ["c27"])
+    ts(col(T2), col(O7), 6.0, 1456.0, A.is_equal, A.mult, ["c2"], ["c28"])
+    ts(T.r16[:], T.crow[:, 0:16], col(R), None, A.is_gt, None, ["crow", "c0"], ["r16"])
+    ts(T.c8[:, 0:8], T.crow[:, 0:8], col(O7), None, A.is_gt, None, ["crow", "c2"], ["c8t"])
+    ts(T.z16[:, 0:8], T.crow[:, 0:8], col(O7), 16384.0, A.is_equal, A.mult, ["crow", "c2"], ["z16"])
+    ts(T.pw[:], T.dg[:], 8192.0, None, A.mult, None, ["dg"], ["pw"])
+    ms(T.h1[:], 0.0, ["h1"])
+    tt(T.c8[:, 0:8], T.c8[:, 0:8], T.z16[:, 0:8], A.add, ["c8t", "z16"], ["c8t"])
+    tt(T.cpk[:, 0:16], T.r16[:], T.pw[:], A.add, ["r16", "pw"], ["cpk"])
+    ts(T.c8[:, 7:8], T.c8[:, 7:8], -1.0 / 16384, None, A.mult, None, ["c8t"], ["c8t"])
+    ts(T.cpk[:, 15:16], T.cpk[:, 15:16], -1.0 / 8192, None, A.mult, None, ["cpk"], ["cpk"])
+    ms(T.lw[:, 0:L], W + (N << 16), ["lw"])
+
+    X2 = ps[:, 3072:3120]
+
+    def ranks_old():
+        mm([(X2, T.idb[:], T.dc[:], ["idb", "dc"]), (X2, T.nid[:], T.hd1[:], ["nid", "hd1"])], ["P6"], last=False)
+
+    def ranks():
+        tt(T.h0[:], T.h1[:], XL, A.add, ["h1", "P7"], ["h0"])
+        tt(T.hd[:], T.dc[:], XL, A.mult, ["dc", "P7"], ["hd"])
+        scan(T.cs[:], T.h1[:], XL, 0.0, A.add, A.add, ["h1", "P7"], ["cs"])
+        mm([(X2, T.m2[:], T.h0[:], ["m2", "h0"]), (X2, T.nid[:], T.hd[:], ["nid", "hd"]),
+            (X2, T.bo[:], T.cs[:], ["bo", "cs"])], ["P6"], first=False)
+
+    ms(T.hd1[:], 0.0, ["hd1"])
+    ranks_old()
+    ranks()
+    cp(T.hh[:], T.hni[:], ["hni"], ["hh"])
+    tt(T.pk[:, 0:B], ps[:, 0:B], T.fti[:], A.add, ["P0", "P1", "fti"], ["pk"])
+    dma("y", "ld6", T.pk[:, B:B + 512], T.pk[:, 0:512], ["pk"], ["pk2"])
+
+    def late_constants():
+        for t in range(2):
+            ms(T["aw%d" % t][:, W:W + 8], 0.0, ["aw%dz" % t])
+        ms(T.km[:], 1.0, ["km"])
+        ts(T.tmp[:], T.dm[:], 0.0, -2.0, A.is_equal, A.mult, ["dm"], ["tmp"])
+        ms(T.km[:, 0:512:16], 0.0, ["km"])
+        tt(T.n2[:], T.tmp[:], T.bo[:], A.add, ["tmp", "bo"], ["n2"])
+        TL = ps[:, 2048:2096]
+        cp(T.xs[0:8, :], T.hbi[0:8, :], ["hbi"], ["xs"])
+        ms(T.lu[:], 0, ["lu"])
+        ms(T.xrow[:, L:L + 8], 0.5, ["xrz"])
+        for t in range(2):
+            ms(T["ev%d" % t][:, 480:488], 0.0, ["ev%dz" % t])
+        return [(TL, T.x4f[0:8, 15 - r:143 - r], T.xs[0:8, r:B:16], ["x4f", "xs"]) for r in range(16)]
+
+    def scalar_constants():
+        act(col(WE), col(R), F.Exp, ["c0"], ["c22"], bias=76 * math.log(2.0), scale=-math.log(4.0))
+        lin(WO, WE, -2.0 ** -32, 0.0)
+        lin(NE_, WE, -1.0, 0.0)
+        lin(EB, R, -LN, -129.0 * LN)
+        lin(KW, R, 256.0, 0.0)
+        lin(T0, O7, 160.0, 496.0)
+        lin(T3, O7, 48.0, 48.0)
+        lin(EW, UP, 2.0, -1.0)
+        lin(NS, UP, -32767.0, -1.0)
+        lin(NV, UP, -24576.0, 0.0)
+        lin(CA, UP, 48.0, 0.0)
+        lin(CB, UP, -975.0, 1024.0)
+        lin(SS, UP, -1.0, 1.0)
+        lin(PF, UP, 1.0, -1.0)
+        lin(RH, R, 1.0, 0.5)
+        for c in range(3):
+            lin(D0 + c, R, -1.0 / 1024, (360.0 - 16 * c) / 1024)
+        lin(R1, S1, 1.0 / 524288, 0.0)
+        lin(R0, S0, 1.0 / 524288, 0.0)
+        act(T.bo4[:], T.bo[:], F.Identity, ["bo"], ["bo4"], scale=0.4)
+        act(T.x1g[:], T.bo[:], F.Identity, ["bo"], ["x1g"])
+        act(col(ZW), col(T0), F.Identity, ["c26", "c27", "c3"], ["c16"], bias=col(PF), scale=col(T1))
+        act(col(T2), col(T2), F.Identity, ["c28", "c29"], ["c28"], bias=col(T3))
+        act(col(NW), col(R1), F.Identity, ["c18", "c19"], ["c20"], bias=col(R0), scale=32.0)
+        act(col(NC), col(R0), F.Identity, ["c18", "c19"], ["c21"], bias=col(R1), scale=float(B * me))
+        act(T.jl[:], T.crow[:, 0:16], F.Identity, ["crow", "c0"], ["jl"], bias=col(R), scale=16.0)
+        act(col(IW), col(T2), F.Identity, ["c28", "c12"], ["c17"], scale=col(SS))
+        act(T.xk[:], T.x1[:], F.Identity, ["x1", "c10"], ["xk"], scale=col(KW))
+        for nm, c in (("boz", ZW), ("wn", NW), ("wc", NC), ("bow", IW)):
+            act(T[nm][:], T.bo[:], F.Identity, ["bo", "c%d" % c], [nm], scale=col(c))
+        double(T.cpk, 16, 512, "cpk")
+
+    def scalar_constants2():
+        CD = ["cdd0", "cdd1", "cdd2"]
+        act(T.eqb[:], T.cdd[:], F.Sign, CD + ["c30"], ["eqb"] + ["eq%d" % s for s in range(18)], bias=col(RH), scale=-1.0)
+        act(T.tw[:, 0:N * CAP], T.mark[:], F.Identity, ["mark"], ["tw"])
+        act(T.cdd[:], T.eqb[:], F.Relu, ["eqb"], CD)
+        for c in range(3):
+            x = T.cdd[:, SB[c] + SEG[c] - 1:SB[c] + N * SEG[c]:SEG[c]]
+            act(x, T.crow[:, 0:N], F.Identity, ["crow", "c%d" % (D0 + c)], [CD[c]], bias=col(D0 + c), scale=0.0)
+        act(T.x8[:], T.x1[:], F.Identity, ["x1"], ["x8"], scale=8192.0)
+        act(T.x1f[:], T.x1[:], F.Identity, ["x1"], ["x1f"])
+        act(T.xe[:], T.x1[:], F.Identity, ["x1", "c11"], ["xe"], scale=col(EW))
+        act(T.cpk[:, 512:B], T.cpk[:, 0:B - 512], F.Identity, ["cpk"], ["cpk"])
+        double(T.c8, 8, 320, "c8t")
+
+    def keys():
+        act(T.r2[:], T.hh[:], F.Sign, ["hh"], ["r2"])
+        act(T.ka[:], T.hh[:], F.Abs, ["hh"], ["ka"])
+        act(T.kb[:], T.r2[:], F.Relu, ["r2", "c23"], ["kb"], scale=col(WO))
+        act(T.ka[:], T.ka[:], F.Relu, ["ka", "c22", "c31"], ["ka"], bias=col(WE), scale=col(NE_))
+
+    P45, P67, P01, N23 = ps[:, 2048:2048 + V], ps[:, 3072:3072 + V], ps[:, 0:V], ps[:, 1216:1216 + V]
+    K0 = float(48 * sum(496 + 160 * o for o in range(N)))
+    tgc = ("tg0", "tg1")
+    scalar_constants()
+    act(T.o1[:], T.hh[:], F.Sign, ["hh"], ["o1"], bias=-4608.5)
+    act(T.x4f[:], T.x4[:], F.Identity, ["x4"], ["x4f"])
+    keys()
+
+    for t in range(RO):
+        u, un = t % 2, (t + 1) % 2
+        aw, awn, ev, tb, lb = T["aw%d" % u], T["aw%d" % un], T["ev%d" % u], T["tb%d" % u], T["lb%d" % u]
+        AW = ["aw%dm" % u, "aw%dr" % u, "aw%dz" % u]
+        s0 = (L * t) % B
+        ts(T.offu[:], X2, col(RM1), None, A.add, None, ["P6", "c8"], ["offu"])
+        ts(T.offc[:], X2, col(RM1), float(L), A.add, A.min, ["P6", "c8"], ["offc"])
+        cp(T.lw[:, :].indirect(T.offu[:, :]), T.pk[:, s0:s0 + B], ["offu", "pk"] + (["pk2"] if t else []), ["lw"])
+        act(T.xb[:, 0:N * CAP], T.mark[:], F.Identity, ["mark"], ["xb"])
+
+        def spread(c):
+            b0 = 512 * (c % 4)
+            for k in range(16):
+                o = ps[:, b0 + k:b0 + 512:16]
+                op("p", lambda: g.tensor.matmul(o, T.sel[:, 128 * k:128 * k + 128], T.utl[:, 32 * c:32 * c + 32], True, True),
+                   ["sel%d" % k, "utl%d" % (c > 1)], ["P%d" % (c % 4)], inc=(k == 15))
+
+        for j, (a, b) in enumerate(((0, 64), (64, L))):
+            ts(T.xi[:, a:b], T.lw[:, a:b], 4095, None, A.bitwise_and, None, ["lw"], ["xi%d" % j])
+            ts(T.uti[:, a:b], T.lw[:, a:b], 12, 15, A.logical_shift_right, A.bitwise_and, ["lw"], ["uti%d" % j])
+            cp(T.gl[:, a:b], T.xi[:, a:b], ["xi%d" % j], ["gl%d" % j])
+            cp(T.utl[:, a:b], T.uti[:, a:b], ["uti%d" % j], ["utl%d" % j])
+            spread(2 * j)
+            spread(2 * j + 1)
+        if t == 0:
+            mm(late_constants(), ["P4"])
+        for c in range(8):
+            act(T.ag[:, 512 * c:512 * c + 512], aw[:, :].indirect(T.gl[:, 32 * c:32 * c + 32]), F.Identity,
+                AW + ["gl%d" % (c > 1)], ["ag%d" % c])
+
+        def largest(c):
+            scan(T.ms[:, 512 * c:512 * c + 512], T.km[:], T.ag[:, 512 * c:512 * c + 512], 0.0, A.mult, A.max,
+                 ["km", "ag%d" % c], ["ms%d" % c])
+
+        for c in range(8):
+            x = T.ag[:, 512 * c:512 * c + 512]
+            tt(x, x, ps[:, 512 * (c % 4):512 * (c % 4) + 512], A.mult, ["ag%d" % c, "P%d" % (c % 4)], ["ag%d" % c])
+            if c < 4:
+                spread(c + 4)
+            if c > 0:
+                largest(c - 1)
+            if t == 0 and c == 2:
+                ts(T.tg0[:], ps[:, 2048:2096], -1.0, -1.0, A.mult, A.add, ["P4"], ["tg0"])
+        wide(2048, [(T.n2[:], T.ka, ["n2", "ka"]), (T.n2[:], T.kb, ["n2", "kb"])], ["P4", "P5"])
+        wide(3072, [(T.idb[:], T.o1, ["idb", "o1"]), (T.bo[:], T.ka, ["bo", "ka"]), (T.bo[:], T.kb, ["bo", "kb"])], ["P6", "P7"])
+        act(T.ntg[:], P45, F.Sign, ["P4", "P5"], ["ntg"])
+        act(ps[:, 0:192], T.ms[:, 15:3072:16], F.Identity, ["ms%d" % c for c in range(6)], ["P0"])
+        largest(7)
+        cp(ps[:, 192:256], T.ms[:, 3072 + 15:4096:16], ["ms6", "ms7"], ["P0"])
+        if t == 0:
+            scalar_constants2()
+        else:
+            act(T.tgt[:], T.ntg[:], F.Relu, ["ntg"], ["tgt"], scale=-1.0)
+            act(T.he[:], P67, F.Sign, ["P6", "P7"], ["he"], bias=-2.0)
+            act(T.r2[:], P67, F.Relu, ["P6", "P7"], ["r2"], scale=-2.0)
+            act(T.ff[:], T.he[:], F.Identity, ["he"], ["ff"], bias=0.96875, scale=0.03125)
+        AG = ["ag%d" % c for c in range(8)]
+        for k in range(16):
+            x = T.top[:, L * k:L * k + L]
+            tt(x, T.ag[:, k:4096:16], ps[:, 0:L], A.is_equal, AG + ["P0"], ["top%d" % k])
+            mm([(ps[:, 512:768], sh(T.x1, k), x, ["x1", "top%d" % k])], ["P1"], first=(k == 0), last=(k == 15))
+        act(T.wv[:], ps[:, 512:768], F.Exp, ["P1", "c9"], ["wv"], bias=col(EB), scale=16.0 * LN)
+        ts(T.owi[:], T.lw[:, 0:L], 16, 7, A.logical_shift_right, A.bitwise_and, ["lw"], ["owi"])
+        ts(T.pci[:], T.lw[:, 0:L], 19, None, A.logical_shift_right, None, ["lw"], ["pci"])
+        mm([(ps[:, 1024:1280], T.bo4[:], T.wv[:], ["bo4", "wv"])], ["P2"])
+        cp(T.pcb[:], T.pci[:], ["pci"], ["pcb"])
+        CH, KL, OL = ps[:, 1280:1536], ps[:, 256:272], ps[:, 1792:2048]
+        tt(CH, T.wv[:], ps[:, 1024:1280], A.is_ge, ["wv", "P2"], ["P2"])
+        tt(T.y2[:], CH, T.owi[:], A.mult, ["P2", "owi"], ["y2"])
+        mm([(ps[:, 1536:1792], T.bo[:], T.y2[:], ["bo", "y2"])], ["P3"])
+        tt(T.y1[:], CH, T.xi[:], A.mult, ["P2", "xi0", "xi1"], ["y1"])
+        act(T.ch[:], CH, F.Identity, ["P2"], ["ch"])
+        mm([(ps[:, 512:768], T.x1g[:], T.y1[:], ["x1g", "y1"])], ["P1"])
+        act(T.xrow[:, 0:L], ps[:, 512:768], F.Identity, ["P1"], ["xrow"], bias=1.0)
+        if t == 0:
+            act(T.tgt[:], T.ntg[:], F.Relu, ["ntg"], ["tgt"], scale=-1.0)
+            act(T.he[:], P67, F.Sign, ["P6", "P7"], ["he"], bias=-2.0)
+        ts(T.ind[:], ps[:, 1536:1792], col(O7), None, A.is_equal, None, ["P3", "c2"], ["ind"])
+        scan(ps[:, 1024:1280], T.ones[:], T.ind[:], 0.0, A.mult, A.add, ["ones", "ind"], ["P2"])
+        mm([(OL, T.bow[:], T.ind[:], ["bow", "ind"])], ["P3"], last=False)
+        kl = [(KL, T.idb[:], T.jl[:], ["idb", "jl"])] + [(KL, sh(T.xk, r), T.ch[:, r:L:16], ["xk", "ch"]) for r in range(16)]
+        mm(kl[:9], ["P0"], last=False)
+        tt(T.zz[:], T.ind[:], ps[:, 1024:1280], A.mult, ["ind", "P2"], ["zz"])
+        ts(T.zc[:], T.zz[:], col(CA), col(CB), A.max, A.min, ["zz", "c14", "c15"], ["zc"])
+        mm([(OL, T.boz[:], T.zc[:], ["boz", "zc"])], ["P3"], first=False)
+        mm(kl[9:], ["P0"], first=False)
+        mm([(ps[:, 768:1024], T.wc[:], T.ones[:], ["wc", "ones"]), (ps[:, 768:1024], T.wn[:], T.pcb[:], ["wn", "pcb"])], ["P1"])
+        scan(T.lsc[:, 0:L], OL, T.cpk[:, 0:L], 0.0, A.max, A.mult, ["P3", "cpk"], ["lsc"])
+        ts(T.bu[:], T.lsc[:, 15:L:16], -1.0, -K0, A.mult, A.add, ["lsc"], ["bu"])
+        cp(T.ku[:], KL, ["P0"], ["ku"])
+        act(T.sgn[:], T.top[:, :].indirect(T.ku[:, :]), F.Identity, ["ku"] + ["top%d" % k for k in range(16)], ["sgn"], bias=1.0, scale=-2.0)
+        cp(T.xb[:, :].indirect(T.bu[:, :]), T.xrow[:, 0:L], ["bu", "xrow"], ["xb"])
+        tt(T.vb[:], T.sgn[:], ps[:, 768:1024], A.mult, ["sgn", "P1"], ["vb"])
+        scan(T.lsc[:], T.xb[:, 0:N * CAP], T.cpk[:, 0:N * CAP], 0.0, A.max, A.mult, ["xb", "cpk"], ["lsc"])
+        cp(T.tw[:, :].indirect(T.bu[:, :]), T.vb[:], ["bu", "vb"], ["tw"])
+        order("g", ["tw"], [])
+        dl = deal(me)
+        g.remote_dma_fused([RemoteDMATransfer(dst_ids=[did(q)], dma_engine_mask=bits(dl[q]), remote_sem=T.sem["ab%d" % t],
+                                              srcs=[T.tw[:, CAP * q:CAP * q + CAP]], dsts=[tb[:, CAP * me:CAP * me + CAP]])
+                            for q in others], local_sem=T.sem["lt%d" % t])
+        nl = sum(len(dl[q]) for q in others)
+        mark(("lt%d" % t, nl, "d"), ["tw"], [])
+        ends["lt%d" % t] = nl
+        tt(T.w18[:], T.lsc[:, 15:N * CAP:16], T.wc18[:], A.add, ["lsc", "wc18"], ["w18"])
+        for s in range(18):
+            o, c = divmod(s, 3)
+            e0 = SB[c] + SEG[c] * o
+            x, y, z = T.eqb[:, e0:e0 + SEG[c] - 1], T.xb[:, CAP * o + 16 * c:CAP * o + CAP], T.lsc[:, 16 * s + 15:16 * s + 16]
+            if s < 14:
+                act(x, y, F.Abs, ["xb", "lsc"], ["eq%d" % s], bias=z)
+            else:
+                ts(x, y, z, 0.0, A.add, A.not_equal, ["xb", "lsc"], ["eq%d" % s])
+        for c in range(3):
+            ts(T.eqb[:, SB[c] + SEG[c] - 1:SB[c] + N * SEG[c]:SEG[c]], T.w18[:, c:18:3], 1.0 / 1024, None, A.mult, None,
+               ["w18"], ["eqb%d" % c] + (["eqb"] if c == 0 else []))
+        scan(T.eqs[:], T.eqb[:], T.cdd[:], 1.0, A.min, A.max,
+             ["eqb", "eqb0", "eqb1", "eqb2", "cdd0", "cdd1", "cdd2"] + ["eq%d" % s for s in range(18)], ["eqs"])
+        for c in range(3):
+            ts(T.lu[:, c:24:4], T.eqs[:, SB[c] + SEG[c] - 1:SB[c] + N * SEG[c]:SEG[c]], -1024.0, 1000.0, A.mult, A.add,
+               ["eqs"], ["lu%d" % c] + (["lu"] if c == 0 else []))
+        LU = ["lu", "lu0", "lu1", "lu2"]
+        bcast(T.lu[:], lb[:, 24 * me:24 * me + 24], "ab%d" % t, "ll%d" % t, LU)
+        arrive("bids", "ab%d" % t, nb + sum(len(deal(q)[me]) for q in others))
+        tt(T.uu[:], T.hh[:], P45, A.max, ["hh", "P4", "P5"], ["uu"])
+        act(T.xg[:], T.xrow[:, :].indirect(T.offc[:, :]), F.Identity, ["xrow", "xrz", "offc"], ["xg"])
+        act(T.tn[:], T.uu[:], F.Relu, ["uu"], ["tn"], scale=-1.0)
+        act(T.tt[:], T.nam[:, 0:688], F.Identity, ["nam"], ["tt"], bias=1.5, scale=0.0)
+        if t == 0:
+            act(T.r2[:], P67, F.Relu, ["P6", "P7"], ["r2"], scale=-2.0)
+            act(T.ff[:], T.he[:], F.Identity, ["he"], ["ff"], bias=0.96875, scale=0.03125)
+        act(P45, aw[:, mine], F.Identity, ["aw%dm" % u], ["P4", "P5"])
+        act(T.ntg[:], T.tgt[:], F.Identity, ["tgt"], ["ntg"], bias=1.0, scale=-1.0)
+        KF = ps[:, 0:80]
+        mm([(KF, sh(T.x8, r), T.tgt[:, r:V:8], ["x8", "tgt"]) for r in range(8)]
+           + [(KF, sh(T.x1f, 8 + r), T.tn[:, r:V:8], ["x1f", "tn"]) for r in range(8)], ["P0"])
+        scan(T.xs[:], T.xg[:], T.cpk[:], 0.0, A.max, A.mult, ["xg", "cpk"], ["xs"])
+        ko, kn = tgc[t % 2], tgc[(t + 1) % 2]
+        ts(T.m48[:], T.xs[:, 15:B:16], -0.75, None, A.is_gt, None, ["xs"], ["m48"])
+        if t + 1 < RO:
+            ms(T.lw[:, 0:L], W + (N << 16), ["lw"])
+        tt(T.t48[:], T.m48[:], T[ko][:], A.mult, ["m48", ko], ["t48"])
+        rot = ((0, 32, 16), (32, 48, -32)) if t + 1 < RO else ((0, 48, 0),)
+        for a, b, d in rot:
+            tt(T[kn][:, a:b], T.xs[:, 16 * (a + d) + 15:16 * (b + d):16], T.t48[:, a + d:b + d], A.min, ["xs", "t48"], [kn + str(a)])
+        wr[kn] = wr[kn + str(rot[-1][0])]
+        rd[kn] = []
+        ts(T.tgi[:], T[kn][:], -1.0, -1.0, A.mult, A.add, [kn], ["tgi"])
+        ts(T.tg8[:], T.tgi[:], 3, None, A.logical_shift_right, None, ["tgi"], ["tg8"])
+        for a, b, d in rot:
+            cp(T.h1[:, a:b], T.h0[:, a + d:b + d], ["h0"], ["h1"])
+        cp(T.tgu[:], T.tg8[:], ["tg8"], ["tgu"])
+        if t + 1 < RO:
+            tt(T.hd1[:], T.h1[:], T.dc[:], A.mult, ["h1", "dc"], ["hd1"])
+        tt(P67, T.ff[:], P45, A.mult, ["ff", "P4", "P5"], ["P6", "P7"])
+        for q in range(N - 1, -1, -1):
+            if q == me:
+                x, y, r = T.tw[:, CAP * me:CAP * me + CAP], T.lu[:, 4 * me:4 * me + 3], ["tw"] + LU
+            else:
+                x, y, r = tb[:, CAP * q:CAP * q + CAP], lb[:, 24 * q + 4 * me:24 * q + 4 * me + 3], ["bids"]
+            ts(T.tt[:, :].indirect(y), x, 1.0, 1.0, A.mult, A.add, r, ["tt"])
+        for j in range(2):
+            act(ps[:, 1216 + 320 * j:1536 + 320 * j], T.tt[:, 320 * j:320 * j + 320], F.Abs, ["tt"], ["P%d" % (2 + j)], bias=-1.0)
+        tt(T.he[:, 0:320], T.tt[:, 0:320], ps[:, 2048:2368], A.min, ["tt", "P4"], ["he"])
+        for j in range(2):
+            scan(T.uu[:, 320 * j:320 * j + 320], ps[:, 1216 + 320 * j:1536 + 320 * j], T.c8[:], 0.0, A.max, A.mult,
+                 ["P%d" % (2 + j), "c8t"], ["uu%d" % j] + (["uu"] if j == 0 else []))
+        ts(T.nab[:], T.uu[:, 7:V:8], col(NS), col(NV), A.mult, A.add, ["uu", "uu0", "uu1", "c13", "c6"], ["nab"])
+        evm = ev[:, 80 * me:80 * me + 80]
+        tt(evm, T.nab[:], KF, A.min, ["nab", "P0"], ["evm%d" % u])
+        bcast(evm, evm, "ae%d" % t, "le%d" % t, ["evm%d" % u])
+        arrive("evr", "ae%d" % t, nb)
+        act(T.en[:], N23, F.Identity, ["P2", "P3"], ["en"], bias=3.0, scale=-4.0)
+        act(T.tn[:], N23, F.Identity, ["P2", "P3"], ["tn"], bias=MAGIC)
+        act(N23, T.tn[:], F.Identity, ["tn"], ["P2", "P3"], bias=-MAGIC)
+        wide(0, [(T.idb[:], T.ntg, ["idb", "ntg"]), (T.nid[:], T.r2, ["nid", "r2"])], ["P0", "P1"])
+        tt(T.he[:, 320:V], T.tt[:, 320:V], ps[:, 2368:2048 + V], A.min, ["tt", "P4", "P5"], ["he2"])
+        tt(awn[:, mine], T.he[:], P67, A.max, ["he", "he2", "P6", "P7"], ["aw%dm" % un])
+        bcast(awn[:, mine], awn[:, mine], "aa%d" % (t + 1), "la%d" % (t + 1), ["aw%dm" % un])
+        arrive("aw%dr" % un, "aa%d" % (t + 1), nb)
+        if t + 1 == RO:
+            dma("y", "st0", T.yal[:], awn[:, mine], ["aw%dm" % un], [])
+
+        def codes():
+            tt(P01, P01, T.en[:], A.max, ["P0", "P1", "en"], ["P0", "P1"])
+            tt(T.he[:], T.hh[:], P01, A.mult, ["hh", "P0", "P1"], ["he", "he2"])
+            tt(N23, N23, T.tgt[:], A.mult, ["P2", "P3", "tgt"], ["P2", "P3"])
+            yield
+            tt(T.hh[:], T.he[:], N23, A.add, ["he", "P2", "P3"], ["hh"])
+            yield
+            yield
+
+        cd = codes()
+        if t + 1 < RO:
+            ranks_old()
+        next(cd)
+        s1 = (L * (t + 1)) % B if t + 1 < RO else 0
+        tt(T.tog[:], ev[:, :].indirect(T.tgu[:, :]), T.nam[:, s1:s1 + B], A.is_equal,
+           ["evm%d" % u, "evr", "ev%dz" % u, "tgu", "nam"], ["tog"])
+        mm([(XL, sh(T.xe, r), T.tog[:, r:B:16], ["xe", "tog"]) for r in range(16)], ["P7"])
+        next(cd)
+        if t + 1 < RO:
+            ranks()
+        else:
+            tt(T.h0[:], T.h1[:], XL, A.add, ["h1", "P7"], ["h0"])
+        next(cd)
+        if t + 1 < RO:
+            keys()
+        else:
+            dma("s", "st1", T.yh[:], T.hh[:], ["hh"], [])
+
+    hf = "h0"
+    ts(T.m48[:], T[hf][:], float(W), None, A.mult, None, [hf], ["m48"])
+    tt(T.t48[:], T.m48[:], T.tgi[:], A.max, ["m48", "tgi"], ["t48"])
+    cp(T.finu[:], T.t48[:], ["t48"], ["finu"])
+    aw = T["aw%d" % (RO % 2)]
+    AW = ["aw%d%s" % (RO % 2, x) for x in "mrz"]
+    for j, e in ((0, "y"), (1, "s")):
+        a = 384 * j
+        tt(T.xg[:, a:a + 384], aw[:, :].indirect(T.finu[:, 24 * j:24 * j + 24]), T.monb[:, a:a + 384], A.mult,
+           AW + ["finu", "monb"], ["yp%d" % j])
+        dma(e, "st%d" % (2 + j), T.yp[:, a:a + 384], T.xg[:, a:a + 384], ["yp%d" % j], [])
+    for e in ("v", "s", "p", "g"):
+        ends[SEM[e]] = cnt[e]
+    for sem in ends:
+        if all(seen[e].get(sem, 0) < ends[sem] for e in Q):
+            g.wait_ge(T.sem[sem], ends[sem])

@@ -4,9 +4,15 @@ from concourse.mybir import AluOpType as A, ActivationFunctionType as F
 
 N, V, B, L, CAP, RO = 6, 640, 768, 256, 48, 4
 W = N * V
-SEG = (49, 33, 17)
-SB = (0, N * 49, N * 82)
-NE = N * 99
+RG = 272
+STEP = 30
+CH = [0] + list(range(16, L, STEP)) + [L]
+NC = len(CH) - 1
+SPLIT = 384
+BEHIND = 1
+EARLY = 320
+HALF = ((0, 64), (64, L))
+PARTS = ((0, 192), (192, L))
 f32, bf, i32, u16 = "float32", "bfloat16", "int32", "uint16"
 SCRATCH = {"ps": ("psum", [128, 4096], f32)}
 
@@ -21,21 +27,22 @@ for _t in range(2):
     SCRATCH["ev%d" % _t] = ("sbuf", [128, 488], f32)
     SCRATCH["tb%d" % _t] = ("sbuf", [128, N * CAP], f32)
     SCRATCH["lb%d" % _t] = ("sbuf", [128, N * 24], u16)
-_sb(i32, fti=B, hni=V, hbi=B, pcol=4, ci=8, pk=B + 512, lw=2304, uti=L, xi=L, owi=L, pci=L, tgi=48, tg8=48)
-_sb(u16, offu=48, offc=48, gl=L, ku=16, bu=16, lu=24, tgu=48, finu=48)
-_sb(bf, utb=B, monb=B, ownb=B, lob=B, hib=B, idb=128, nid=128, bo=128, bo4=128, n2=128, m2=128, wn=128, wc=128,
-    d0=128, d1=128, d2=128, d3=128, sel=2048, x1=144, xe=144, xk=144, boz=128, bow=128, x8=144, x4=144, dc=48, jl=16,
-    h0=48, h1=48, cs=48, hd=48, hd1=48, ones=L, km=512, utl=L, pcb=L, top=4096, wv=L, ch=L, y2=L, ind=L, zz=L, zc=L,
-    tog=B, ka=V, kb=V, tgt=V, ntg=V, o1=V, r2=V)
-_sb(f32, cf=40, dm=128, tmp=128, tm2=128, crow=152, grow=128, r16=16, dg=16, pw=16, q16=16, z16=16, x1f=144, x4f=144,
-    x1g=128, c8=320, nam=2 * B, cpk=B, cdd=NE, eqb=NE, eqs=NE, mark=N * CAP, wc18=18, w18=18,
-    ag=4096, ms=4096, y1=L, xrow=264, sgn=L, vb=L, xb=1792, tw=1792, lsc=N * CAP, xg=B, xs=B, m48=48, t48=48, tg0=48,
-    tg1=48, tt=688, nab=80, hh=V, he=V, uu=V, tn=V, en=V, ff=V)
-SEMAPHORES = (["cv", "cs_", "cp", "cg"] + ["ld%d" % k for k in range(7)] + ["st%d" % k for k in range(4)]
+_sb(i32, fti=B + 8, hni=V, hbi=B, ci=8)
+_sb(u16, offu=48, offc=48, gl=L, bl=16, ku=16, bu=16, lu=24, tgu=48, finu=48)
+_sb(bf, utb=B + 16, monb=B, fac=4112, zer=128, idb=128, nid=128, ndr=128, bo=128, nbo=128, tri=128, m2=128, ta=128, nta=128, i32=128, tq=128,
+    gq=128, dq=128, i8k=128, n94=128, bo16=128, mxa=128, mxb=128, olm=128, sel=2048, x1=144, xe=144, xk0=144, xk1=144, x8=144, x4=144,
+    dc=48, jl=16, h0=48, h1=48, cs=48, hd=48, hd1=48, nones=V, low=L, sa=L, sb_=L, scl=L, utl=L, top=4096, wv=L, ch=L, ind=L,
+    zz=L, tog=B, em=V, ol=V, opn=V, dsb=V, tgt=V, gg=V, nsw=V, rl=V, cdd=144, eqb=1152, eqs=1152)
+_sb(f32, cf=32, dm=128, zef=128, crow=152, grow=128, dg=16, pw=16, x1f=144, x4f=144, idf=128, bof=128,
+    bov=128, c8=320, nam=B + 512, rev=B + 512, lx=2304, nml=L, cpk=L, wc24=24, w24=24, lf=24, ftf=B + 8, lw=2304, ag=4096, ms=2048, xc=L, y1=L,
+    xrow=264, sgn=L, dsc=L, xb=7 * RG, tw=7 * RG, lsc=N * 64, xg=B, xs=B, m48=48, t48=48, tg0=48, tg1=48, tt=840, uu=V, nab=80,
+    hh=V, mag=V, tm=V, mv=V)
+SEMAPHORES = (["cv", "cs_", "cp", "cg"] + ["ld%d" % k for k in range(6)] + ["st%d" % k for k in range(4)]
               + ["%s%d" % (p, t) for p in ("ab", "ae", "lt", "ll", "le") for t in range(RO)]
+              + ["%s%d" % (p, t) for p in ("ah", "lx", "lf") for t in range(RO)]
               + ["%s%d" % (p, t) for p in ("aa", "la") for t in range(RO + 1)])
+CYCLE, T_CYCLE, V_CALL, S_CALL, SIGNAL, GATHER, SCATTER, AHEAD, SPARE = 0.00083, 0.00055, 0.03, 0.2, 0.1, 1.5, 3.5, -0.5, 0.05
 MAGIC = 12582912.0
-LN = math.log(1.8)
 
 
 def rank_program(g, core, T, topo):
@@ -44,85 +51,164 @@ def rank_program(g, core, T, topo):
         return
     Q = {"v": g.vector, "s": g.scalar, "p": g.tensor, "g": g, "y": g.sync}
     SEM = {"v": "cv", "s": "cs_", "p": "cp", "g": "cg"}
-    cnt = {"v": 0, "s": 0, "p": 0, "g": 0}
-    seen = {e: {} for e in Q}
-    wr, rd, ends = {}, {}, {}
+    calls, wr, rd, aside = [], {}, {}, [False]
 
-    def need(e, tok):
-        if tok[2] == "p" and e == "p":
-            return
-        if seen[e].get(tok[0], 0) < tok[1]:
-            Q[e].wait_ge(T.sem[tok[0]], tok[1])
-            seen[e][tok[0]] = tok[1]
+    def side(on):
+        aside[0] = on
 
-    def order(e, r, w):
+    def note(e, fn, r, w, busy, after=0.0, tok=None):
+        dep = set()
         for k in r:
             if k in wr:
-                need(e, wr[k])
+                dep.add(wr[k])
             if k[0] == "P":
-                for tok in rd.get(k, []):
-                    if tok[2] != e:
-                        need(e, tok)
+                dep.update(i for i in rd.get(k, []) if calls[i]["e"] != e)
         for k in w:
             if k in wr:
-                need(e, wr[k])
-            for tok in rd.get(k, []):
-                need(e, tok)
-
-    def mark(tok, r, w):
+                dep.add(wr[k])
+            dep.update(rd.get(k, []))
+        calls.append({"e": e, "fn": fn, "dep": dep, "busy": busy, "after": after, "tok": tok, "side": aside[0]})
         for k in r:
-            rd.setdefault(k, []).append(tok)
+            rd.setdefault(k, []).append(len(calls) - 1)
         for k in w:
-            wr[k] = tok
+            wr[k] = len(calls) - 1
             rd[k] = []
 
-    def op(e, fn, r, w, inc=True):
-        order(e, r, w)
-        ins = fn()
-        if inc:
-            cnt[e] += 1
-            ins.then_inc(T.sem[SEM[e]], 1)
-            mark((SEM[e], cnt[e], e), r, w)
-        else:
-            mark((SEM[e], cnt[e] + 1, e), r, w)
+    def width(x):
+        return x.shape[1] if len(x.shape) > 1 else 1
 
-    def dma(e, sem, out, in_, r, w):
-        order(e, r, w)
-        Q[e].dma_start(out, in_).then_inc(T.sem[sem], 16)
-        mark((sem, 16, "d"), r, w)
-        ends[sem] = 16
+    def short(*xs):
+        return all(str(x.dtype).endswith("16") for x in xs)
 
-    def ts(out, in0, s1, s2, o0, o1, r, w):
+    def vec(fn, r, w, n, per):
+        note("v", fn, r, w, V_CALL + CYCLE * max(64, n * per))
+
+    def dma(e, sem, out, in_, r, w, after):
+        note(e, lambda: Q[e].dma_start(out, in_).then_inc(T.sem[sem], 16), r, w, 0.05, after, (sem, 16))
+
+    def ts(out, in0, s1, s2, o0, o1, r, w, per=None):
+        n, per = width(in0), per or (0.5 if short(out, in0) else 1)
         if o1 is None:
-            op("v", lambda: g.vector.tensor_scalar(out, in0, s1, None, o0), r, w)
+            vec(lambda: g.vector.tensor_scalar(out, in0, s1, None, o0), r, w, n, per)
         else:
-            op("v", lambda: g.vector.tensor_scalar(out, in0, s1, s2, o0, o1), r, w)
+            vec(lambda: g.vector.tensor_scalar(out, in0, s1, s2, o0, o1), r, w, n, per)
 
-    def tt(out, a, b, o, r, w):
-        op("v", lambda: g.vector.tensor_tensor(out, a, b, o), r, w)
+    def tt(out, a, b, o, r, w, per=None):
+        vec(lambda: g.vector.tensor_tensor(out, a, b, o), r, w, width(b), per or (1 if any(k[0] == "P" for k in r) else 2))
 
-    def cp(out, a, r, w):
-        op("v", lambda: g.vector.tensor_copy(out, a), r, w)
+    def cp(out, a, r, w, per=None, n=None):
+        vec(lambda: g.vector.tensor_copy(out, a), r, w, n or width(a), per or (0.5 if short(out, a) else 1))
 
     def ms(out, c, w):
-        op("v", lambda: g.vector.memset(out, c), [], w)
+        vec(lambda: g.vector.memset(out, c), [], w, width(out), 0.5 if short(out) else 1)
 
     def scan(out, a, b, init, o0, o1, r, w):
-        op("v", lambda: g.vector.tensor_tensor_scan(out, a, b, init, o0, o1), r, w)
+        vec(lambda: g.vector.tensor_tensor_scan(out, a, b, init, o0, o1), r, w, width(out), 0.5 if short(out, a, b) else 1)
 
-    def act(out, a, func, r, w, bias=0.0, scale=1.0):
-        op("s", lambda: g.scalar.activation(out, a, func, bias=bias, scale=scale), r, w)
+    def act(out, a, func, r, w, bias=0.0, scale=1.0, per=None, n=None):
+        fn = (lambda: g.scalar.activation(out, a, func)) if n else (lambda: g.scalar.activation(out, a, func, bias=bias, scale=scale))
+        note("s", fn, r, w, 0.07 + CYCLE * (n or width(out)) * per if per else S_CALL + CYCLE * width(out))
 
-    def mm(items, w, first=True, last=True):
-        for i, (o, l, x, r) in enumerate(items):
-            st, sp = first and i == 0, last and i == len(items) - 1
-            op("p", lambda: g.tensor.matmul(o, l, x, st, sp), r, w, inc=sp)
+    def mm(items, w, first=True, last=True, alone=False):
+        def fn():
+            for i, (o, l, x, r) in enumerate(items):
+                ins = g.tensor.matmul(o, l, x, alone or (first and i == 0), alone or (last and i == len(items) - 1))
+            return ins
+        note("p", fn, [k for it in items for k in it[3]], w,
+             sum(T_CYCLE * max(64, width(it[2])) * (1 if short(it[2]) else 4) for it in items))
 
-    def iota(out, pat, base, mult, w, small=True):
+    def iota(out, pat, base, mult, w, small=True, r=()):
+        busy = 0.13 + 2 * CYCLE * width(out)
         if small:
-            op("g", lambda: g.iota(out, pat, base, mult, allow_small_or_imprecise_dtypes=True), [], w)
+            note("g", lambda: g.iota(out, pat, base, mult, allow_small_or_imprecise_dtypes=True), list(r), w, busy)
         else:
-            op("g", lambda: g.iota(out, pat, base, mult), [], w)
+            note("g", lambda: g.iota(out, pat, base, mult), list(r), w, busy)
+
+    def fill(out, n, c, w, r=()):
+        iota(out, [[0, n]], c, 0, w, r=r)
+
+    def keep(nm, src, pat, cmp, other, base, mult):
+        note("g", lambda: g.affine_select(T[nm][:], T[src][:], pat, cmp, other, base, mult), [src], [nm], 0.17 + 256 * CYCLE)
+
+    def issue():
+        n = len(calls)
+        succ, left, way = [[] for _ in calls], [len(c["dep"]) for c in calls], [0.0] * n
+        for i, c in enumerate(calls):
+            for d in c["dep"]:
+                succ[d].append(i)
+
+        def lag(d, i):
+            return calls[d]["after"] + (0.0 if calls[d]["e"] == calls[i]["e"] == "p" else SIGNAL)
+
+        for i in range(n - 1, -1, -1):
+            way[i] = calls[i]["busy"] + max([calls[i]["after"]] + [lag(i, j) + way[j] for j in succ[i]])
+        free, end, ready = {e: 0.0 for e in list(Q) + [None]}, [None] * n, {e: {} for e in list(Q) + [None]}
+        cnt, seen, ends = {e: 0 for e in SEM}, {e: {} for e in Q}, {}
+        main = {e: [i for i in range(n - 1, -1, -1) if calls[i]["e"] == e and not calls[i]["side"]] for e in ready}
+        for i in range(n):
+            if not left[i]:
+                ready[calls[i]["e"]][i] = 0.0
+
+        before = {}
+        for e in main:
+            before.update(zip(main[e][:-1], main[e][1:]))
+
+        def soonest(i, memo, now):
+            if i not in memo:
+                if way[i] < now - 8.0:
+                    return 1e6
+                x = [(end[d] if end[d] is not None else soonest(d, memo, 0) + calls[d]["busy"]) + lag(d, i) for d in calls[i]["dep"]]
+                d = before.get(i)
+                memo[i] = max(x + [free[calls[i]["e"]] if d is None or end[d] is not None else soonest(d, memo, 0) + calls[d]["busy"]])
+            return memo[i]
+
+        for _ in range(n):
+            pick, memo = None, {}
+            now = max(way[m[-1]] for m in main.values() if m) if any(main.values()) else 0.0
+            for e in ready:
+                top = main[e][-1] if main[e] else None
+                due, far = (soonest(top, memo, now), way[top]) if main[e] else (1e9, 0.0)
+                side = [(max(free[e], r), -way[i], i) for i, r in ready[e].items()
+                        if calls[i]["side"] and (max(free[e], r) + calls[i]["busy"] <= due + SPARE or ((way[i] > far + AHEAD or calls[i]["side"] == 2) and r <= due) or top not in ready[e] and way[i] > far)]
+                i = min(side)[2] if side else top if top in ready[e] else None
+                if i is not None and (pick is None or max(free[e], ready[e][i]) < pick[0]):
+                    pick = (max(free[e], ready[e][i]), i)
+            at, i = pick
+            c, e = calls[i], calls[i]["e"]
+            del ready[e][i]
+            if not c["side"]:
+                main[e].pop()
+            end[i] = at + c["busy"]
+            if e is not None:
+                free[e] = end[i]
+                for d in sorted(c["dep"], key=lambda j: -calls[j]["tok"][1]):
+                    sem, val = calls[d]["tok"]
+                    if not (e == "p" and calls[d]["e"] == "p") and seen[e].get(sem, 0) < val:
+                        Q[e].wait_ge(T.sem[sem], val)
+                        seen[e][sem] = val
+                ins = c["fn"]()
+                if c["tok"] is None:
+                    cnt[e] += 1
+                    ins.then_inc(T.sem[SEM[e]], 1)
+                    c["tok"] = (SEM[e], cnt[e])
+            ends[c["tok"][0]] = c["tok"][1]
+            for j in succ[i]:
+                left[j] -= 1
+                if not left[j]:
+                    ready[calls[j]["e"]][j] = max(end[d] + lag(d, j) for d in calls[j]["dep"])
+        for sem in ends:
+            if all(seen[e].get(sem, 0) < ends[sem] for e in Q):
+                g.wait_ge(T.sem[sem], ends[sem])
+
+    def diag(nm, src, c):
+        keep(nm, src, [[-1, 128]], A.not_equal, c, 0, 1)
+
+    def above(nm, src):
+        keep(nm, src, [[1, 128]], A.is_gt, 0.0, 0, -1)
+
+    def block(nm, zero, c):
+        keep(nm, zero, [[16, 8], [0, 16]], A.is_gt, c, 0, -1)
+        keep(nm, nm, [[16, 8], [0, 16]], A.is_ge, 0.0, 15, -1)
 
     others = [q for q in range(N) if q != me]
 
@@ -154,23 +240,44 @@ def rank_program(g, core, T, topo):
     def bits(es):
         return sum(1 << e for e in es)
 
-    def bcast(src, dst, rsem, lsem, r):
-        order("g", r, [])
+    def bcast(src, dst, rsem, lsem, r, after, busy=0.4):
         es = common(me)
-        g.remote_dma_fused([RemoteDMATransfer(dst_ids=[did(q) for q in others], dma_engine_mask=bits(es),
-                                              remote_sem=T.sem[rsem], srcs=[src], dsts=[dst] * len(others))],
-                           local_sem=T.sem[lsem])
-        mark((lsem, len(es), "d"), r, [])
-        ends[lsem] = len(es)
+        note("g", lambda: g.remote_dma_fused([RemoteDMATransfer(dst_ids=[did(q) for q in others], dma_engine_mask=bits(es), remote_sem=T.sem[rsem],
+                                                                srcs=[src], dsts=[dst] * len(others))], local_sem=T.sem[lsem]),
+             r, [lsem], busy, after, (lsem, len(es)))
 
     nb = sum(len(common(q)) for q in others)
 
-    def arrive(key, sem, n):
-        wr[key] = (sem, n, "d")
-        ends[sem] = n
+    def arrive(key, sem, n, sent):
+        note(None, None, sent, [], 0.0, 0.0, (sem, n))
+        wr[key] = len(calls) - 1
 
     ps = T.ps
     mine = slice(me * V, (me + 1) * V)
+
+    def near(q):
+        return [p for p in range(N) if topo.die(T.cores[p]) == topo.die(T.cores[q])]
+
+    def crossing(q):
+        far = [p for p in range(N) if p not in near(q)]
+        return [(q * V + h * (V // 2), far[(2 * near(q).index(q) + h) % len(far)]) for h in range(2)]
+
+    def send(parts, rsem, lsem, r, after, busy=0.4):
+        es = common(me)
+        n = len(es) // len(parts)
+        note("g", lambda: g.remote_dma_fused([RemoteDMATransfer(dst_ids=[did(q) for q in to], dma_engine_mask=bits(es[n * i:n * i + n]),
+                                                                remote_sem=T.sem[rsem], srcs=[x], dsts=[x] * len(to))
+                                              for i, (x, to) in enumerate(parts)], local_sem=T.sem[lsem]),
+             r, [lsem], busy, after, (lsem, n * len(parts)))
+
+    def share_alpha(u, t, busy=0.4):
+        x, mates_, e = T["aw%d" % u], [q for q in near(me) if q != me], len(common(me))
+        taken = {p: [c for q in range(N) for c, to in crossing(q) if to == p] for p in range(N)}
+        send([(x[:, c:c + V // 2], [to]) for c, to in crossing(me)], "ah%d" % t, "lx%d" % t, ["aw%dm" % u], 2.5, busy)
+        send([(x[:, mine], mates_)], "aa%d" % t, "la%d" % t, ["aw%dm" % u], 3.5)
+        arrive("aw%dh" % u, "ah%d" % t, len(taken[me]) * (e // 2), ["lx%d" % t])
+        send([(x[:, c:c + V // 2], mates_) for c in taken[me]], "aa%d" % t, "lf%d" % t, ["aw%dh" % u], 2.5)
+        arrive("aw%dr" % u, "aa%d" % t, 2 * e * len(mates_), ["la%d" % t, "lf%d" % t])
 
     def col(j):
         return T.cf[:, j:j + 1]
@@ -178,412 +285,503 @@ def rank_program(g, core, T, topo):
     def sh(x, r):
         return x[:, 15 - r:143 - r]
 
-    def wide(base, items, w):
-        for a, b, k in ((0, 512, w[0]), (512, V, w[1])):
-            mm([(ps[:, base + a:base + b], l, x[:, a:b], r) for (l, x, r) in items], [k])
+    def wide(base, items, first=True, last=True):
+        for j, (a, b) in enumerate(((0, 512), (512, V))):
+            for i, (l, x) in enumerate(items):
+                step = 512 if short(T[x]) else 128
+                for c in range(a, b, step):
+                    d = min(b, c + step)
+                    mm([(ps[:, 512 * base + c:512 * base + d], T[l][:], T[x][:, c:d], [l, x])], ["P%d" % (base + j)],
+                       first and i == 0, last and i == len(items) - 1)
 
-    def double(x, n, end, key):
-        while n < end:
-            m = min(n, end - n)
-            act(x[:, n:n + m], x[:, 0:m], F.Identity, [key], [key])
-            n += m
+    def pieces(items, w, n):
+        for i in range(0, len(items), n):
+            mm(items[i:i + n], w, i == 0, i + n >= len(items))
 
-    dma("y", "ld0", T.aw0[:, mine], T.al[:], [], ["aw0m"])
-    dma("s", "ld1", T.hbi[0:8, :], T.hb[:], [], ["hbi"])
-    dma("s", "ld2", T.fti[:], T.ft[:], [], ["fti"])
-    dma("y", "ld3", T.utb[:], T.ut[:], [], ["utb"])
-    dma("y", "ld4", T.hni[:], T.hn[:], [], ["hni"])
-    dma("y", "ld5", T.monb[:], T.mon[:], [], ["monb"])
-    iota(T.pcol[:, 0:1], [[0, 1]], 0, 1, ["pcol"], small=False)
+    def bucket(x, o):
+        return x[:, RG * o + RG - CAP:RG * o + RG]
+
+    XB, TW = ["xb%d" % o for o in range(N)], ["tw%d" % o for o in range(N)]
+
+    def bids(tb, t):
+        dl = deal(me)
+        note("g", lambda: g.remote_dma_fused([RemoteDMATransfer(dst_ids=[did(q)], dma_engine_mask=bits(dl[q]), remote_sem=T.sem["ab%d" % t],
+                                                                srcs=[bucket(T.tw, q)], dsts=[tb[:, CAP * me:CAP * me + CAP]])
+                                              for q in others], local_sem=T.sem["lt%d" % t]),
+             TW, ["lt%d" % t], 0.4, 3.0, ("lt%d" % t, sum(len(dl[q]) for q in others)))
+
+    def empty_buckets(r):
+        for o in range(N):
+            fill(bucket(T.xb, o), CAP, V * o + V + 1, [XB[o]], r)
+
+    dma("y", "ld0", T.aw0[:, mine], T.al[:], [], ["aw0m", "q0"], 2.6)
+    dma("s", "ld1", T.hbi[0:8, :], T.hb[:], [], ["hbi", "q1"], 2.0)
+    dma("s", "ld4", T.hni[:], T.hn[:], [], ["hni"], 3.5)
+    dma("y", "ld2", T.fti[:, 0:B], T.ft[:], [], ["fti"], 4.3)
+    dma("y", "ld3", T.utb[:, 0:B], T.ut[:], [], ["utb"], 4.8)
+    iota(T.ci[:, 4:5], [[0, 1]], 0, 1, ["pcol"], small=False)
     iota(T.crow[:], [[1, 152]], 0, 0, ["crow"])
     iota(T.dm[:], [[-1, 128]], 0, 1, ["dm"])
     iota(T.grow[:], [[16, 8], [0, 16]], 0, 0, ["grow"])
-    iota(T.hib[:], [[1, 24], [0, 32]], 0, 0, ["hib"])
-    bcast(T.aw0[:, mine], T.aw0[:, mine], "aa0", "la0", ["aw0m"])
-    arrive("aw0r", "aa0", nb)
-    act(T.lob[:, 0:32], T.crow[:, 0:32], F.Identity, ["crow"], ["lob"])
-    double(T.lob, 32, B, "lob")
-    iota(T.mark[:], [[V, N], [1, CAP]], V + 1, 0, ["mark"])
-    iota(T.wc18[:], [[V, N], [0, 3]], 1001, 0, ["wc18"])
-    for c in range(3):
-        iota(T.cdd[:, SB[c]:SB[c] + N * SEG[c]], [[0, N], [1, SEG[c]]], 0, 0, ["cdd%d" % c])
-    iota(T.nam[:], [[0, 2], [1, B]], me * B + 1, 0, ["nam"])
+    iota(T.rev[:, 0:B], [[-1, B]], B + 33, 0, ["rev"])
+    share_alpha(0, 0, 3.5)
 
-    (R, G16, O7, PF, UP, C15, NV, P15, RM1, EB, KW, EW, SS, NS, CA, CB, ZW, IW, R0, R1, NW, NC, WE, WO, S0, S1, T0, T1,
-     T2, T3, RH, NE_, D0, D1, D2) = range(35)
+    (R, G16, O7, PF, UP, C15, P15, RM1, KW, EW, NS, NV, OM, LOW, OW, GB, T0, D0, D1, D2, NR, VW, KX) = range(23)
 
     def lin(j, src, a, b):
         act(col(j), col(src), F.Identity, ["c%d" % src], ["c%d" % j], bias=b, scale=a)
 
-    ts(T.ci[:, 0:1], T.pcol[:, 0:1], 15, None, A.bitwise_and, None, ["pcol"], ["ci0"])
-    ts(T.ci[:, 1:2], T.pcol[:, 0:1], 7, None, A.bitwise_and, None, ["pcol"], ["ci1"])
-    cp(col(PF), T.pcol[:, 0:1], ["pcol"], ["c3"])
-    ms(T.ones[:], 1.0, ["ones"])
+    def scaled(nm, src, c):
+        ts(T[nm][:], T[src][:], c if isinstance(c, float) else col(c), None, A.mult, None,
+           [src] + ([] if isinstance(c, float) else ["c%d" % c]), [nm])
+
+    side(True)
+    ms(T.lw[:, 0:L], 0.25, ["lw"])
+    ms(T.lx[:, 0:L], 0.25, ["lx"])
+    ms(T.h1[:], 0.0, ["h1"])
+    ms(T.zer[:], 0.0, ["zer"])
+    ts(T.ci[:, 0:1], T.ci[:, 4:5], 15, None, A.bitwise_and, None, ["pcol"], ["ci0"])
+    ts(T.ci[:, 1:2], T.ci[:, 4:5], 7, None, A.bitwise_and, None, ["pcol"], ["ci1"])
+    cp(col(PF), T.ci[:, 4:5], ["pcol"], ["c3"])
     cp(col(R), T.ci[:, 0:1], ["ci0"], ["c0"])
     cp(col(O7), T.ci[:, 1:2], ["ci1"], ["c2"])
-    ts(col(P15), col(PF), 16.0, 15.0, A.mult, A.add, ["c3"], ["c7"])
-    ts(T.idb[:], T.dm[:], 0.0, None, A.is_equal, None, ["dm"], ["idb"])
+    ts(col(P15), col(PF), 16.0, 15.0, A.mult, A.add, ["c3"], ["c6"])
     tt(col(G16), col(PF), col(R), A.subtract, ["c3", "c0"], ["c1"])
-    ts(T.x4[:], T.crow[:, 0:144], col(P15), None, A.is_equal, None, ["crow", "c7"], ["x4"])
-    ts(T.dg[:], T.crow[:, 0:16], col(R), None, A.is_equal, None, ["crow", "c0"], ["dg"])
-    ts(T.bo[:], T.grow[:], col(G16), None, A.is_equal, None, ["grow", "c1"], ["bo"])
-    ts(T.tmp[:], T.dm[:], 0.0, -1.0, A.is_gt, A.mult, ["dm"], ["tmp"])
-    ts(T.tm2[:], T.dm[:], 0.0, col(R), A.is_equal, A.mult, ["dm", "c0"], ["tm2"])
-    ts(col(S0), col(R), 0.0, 524288.0, A.is_equal, A.mult, ["c0"], ["c24"])
-    ts(col(S1), col(R), 1.0, 524288.0, A.is_equal, A.mult, ["c0"], ["c25"])
     ts(col(UP), col(R), 7.5, None, A.is_gt, None, ["c0"], ["c4"])
-    tt(T.tmp[:], T.tmp[:], T.bo[:], A.mult, ["tmp", "bo"], ["tmp"])
-    act(T.dc[:], T.crow[:, 0:48], F.Identity, ["crow"], ["dc"], bias=768.0, scale=16.0)
-    act(T.nid[:], T.idb[:], F.Identity, ["idb"], ["nid"], scale=-1.0)
-    lin(RM1, R, 1.0, -1.0)
-    act(T.d2[:], T.idb[:], F.Identity, ["idb"], ["d2"], scale=4096.0)
-    act(T.d3[:], T.idb[:], F.Identity, ["idb"], ["d3"], scale=65536.0)
-    act(T.d0[:], T.idb[:], F.Identity, ["idb", "c24"], ["d0"], scale=col(S0))
-    act(T.d1[:], T.idb[:], F.Identity, ["idb", "c25"], ["d1"], scale=col(S1))
-    lin(C15, G16, 1.0, 15.0)
-    for k in range(16):
-        act(T.sel[:, 128 * k:128 * k + 128], T.bo[:], F.Identity, ["bo", "dg"], ["sel%d" % k], scale=T.dg[:, k:k + 1])
-    ts(T.tog[0:8, :], T.hbi[0:8, :], float(W), None, A.is_equal, None, ["hbi"], ["tog"])
-    XL = ps[:, 3584:3632]
-    mm([(XL, T.x4[0:8, 15 - r:143 - r], T.tog[0:8, r:B:16], ["x4", "tog"]) for r in range(16)], ["P7"])
-    ts(T.xg[:], T.fti[:], 1.0 / V, -0.4992, A.mult, A.add, ["fti"], ["xg"])
-    tt(T.m2[:], T.tmp[:], T.tm2[:], A.subtract, ["tmp", "tm2"], ["m2"])
-    ts(T.ownb[:], T.xg[:], MAGIC, -MAGIC, A.add, A.add, ["xg"], ["ownb"])
-    for a, b, k in ((0, 512, "P0"), (512, B, "P1")):
-        mm([(ps[:, a:b], T.d0[:], T.lob[:, a:b], ["d0", "lob"]), (ps[:, a:b], T.d2[:], T.utb[:, a:b], ["d2", "utb"]),
-            (ps[:, a:b], T.d1[:], T.hib[:, a:b], ["d1", "hib"]), (ps[:, a:b], T.d3[:], T.ownb[:, a:b], ["d3", "ownb"])], [k])
-    ts(T.x1[:], T.crow[:, 0:144], col(C15), None, A.is_equal, None, ["crow", "c5"], ["x1"])
-    ts(col(T1), col(O7), 5.5, col(UP), A.is_lt, A.mult, ["c2", "c4"], ["c27"])
-    ts(col(T2), col(O7), 6.0, 1456.0, A.is_equal, A.mult, ["c2"], ["c28"])
-    ts(T.r16[:], T.crow[:, 0:16], col(R), None, A.is_gt, None, ["crow", "c0"], ["r16"])
-    ts(T.c8[:, 0:8], T.crow[:, 0:8], col(O7), None, A.is_gt, None, ["crow", "c2"], ["c8t"])
-    ts(T.z16[:, 0:8], T.crow[:, 0:8], col(O7), 16384.0, A.is_equal, A.mult, ["crow", "c2"], ["z16"])
+    ts(T.x4[:], T.crow[:, 0:144], col(P15), None, A.is_equal, None, ["crow", "c6"], ["x4"])
+    ts(T.dg[:], T.crow[:, 0:16], col(R), None, A.is_equal, None, ["crow", "c0"], ["dg"])
+    ts(T.lf[:, 0:16], T.crow[:, 0:16], col(R), None, A.is_gt, None, ["crow", "c0"], ["lf"])
+    ts(T.idb[:], T.dm[:], 0.0, None, A.is_equal, None, ["dm"], ["idb"])
     ts(T.pw[:], T.dg[:], 8192.0, None, A.mult, None, ["dg"], ["pw"])
-    ms(T.h1[:], 0.0, ["h1"])
-    tt(T.c8[:, 0:8], T.c8[:, 0:8], T.z16[:, 0:8], A.add, ["c8t", "z16"], ["c8t"])
-    tt(T.cpk[:, 0:16], T.r16[:], T.pw[:], A.add, ["r16", "pw"], ["cpk"])
-    ts(T.c8[:, 7:8], T.c8[:, 7:8], -1.0 / 16384, None, A.mult, None, ["c8t"], ["c8t"])
+    ts(T.bo[:], T.grow[:], col(G16), None, A.is_equal, None, ["grow", "c1"], ["bo"])
+    ts(T.m2[:], T.dm[:], 0.0, -1.0, A.is_gt, A.mult, ["dm"], ["m2"])
+    tt(T.cpk[:, 0:16], T.lf[:, 0:16], T.pw[:], A.add, ["lf", "pw"], ["cpk"])
+    act(T.dc[:], T.crow[:, 0:48], F.Identity, ["crow"], ["dc"], bias=768.0, scale=16.0)
+    lin(RM1, R, 1.0, -1.0)
+    lin(NR, R, -1.0, 0.0)
+    act(T.nid[:], T.idb[:], F.Identity, ["idb"], ["nid"], scale=-1.0)
+    act(T.ndr[:], T.idb[:], F.Identity, ["idb", "c20"], ["ndr"], scale=col(NR))
+    act(T.nbo[:], T.bo[:], F.Identity, ["bo"], ["nbo"], scale=-1.0)
+    for j, src, a, b in ((C15, G16, 1.0, 15.0), (KW, R, float(PARTS[0][1]), 0.0), (KX, R, float(L - PARTS[0][1]), 0.0), (OM, O7, 1.0, MAGIC), (T0, O7, float(RG), RG + 1.0), (LOW, UP, -1.0, 1.0),
+                         (GB, R, 1.0 / 128, -0.125), (D0, R, 4.0, 644.0), (D1, R, 4.0, 708.0), (D2, R, 4.0, 772.0)):
+        lin(j, src, a, b)
+    act(col(OW), col(T0), F.Identity, ["c16", "c4"], ["c14"], bias=-1.0, scale=col(UP))
+    side(False)
+    ts(T.tog[0:8, :], T.hbi[0:8, :], float(W), None, A.is_equal, None, ["hbi"], ["tog"])
+    XL, X2 = ps[:, 1536:1584], ps[:, 1024:1072]
+    mm([(XL, T.x4[0:8, 15 - r:143 - r], T.tog[0:8, r:B:16], ["x4", "tog"]) for r in range(16)], ["P3"])
+    side(True)
     ts(T.cpk[:, 15:16], T.cpk[:, 15:16], -1.0 / 8192, None, A.mult, None, ["cpk"], ["cpk"])
-    ms(T.lw[:, 0:L], W + (N << 16), ["lw"])
+    tt(T.m2[:], T.m2[:], T.bo[:], A.mult, ["m2", "bo"], ["m2"])
+    cp(T.cpk[:, 16:32], T.cpk[:, 0:16], ["cpk"], ["cpk"])
+    ms(T.sa[:], 256.0, ["sa"])
+    cp(T.cpk[:, 32:64], T.cpk[:, 0:32], ["cpk"], ["cpk"])
 
-    X2 = ps[:, 3072:3120]
-
-    def ranks_old():
-        mm([(X2, T.idb[:], T.dc[:], ["idb", "dc"]), (X2, T.nid[:], T.hd1[:], ["nid", "hd1"])], ["P6"], last=False)
+    def ranks_old(first=False):
+        mm([(X2, T.idb[:], T.dc[:], ["idb", "dc"])] + ([] if first else [(X2, T.nid[:], T.hd1[:], ["nid", "hd1"])]), ["P2"], last=False)
 
     def ranks():
-        tt(T.h0[:], T.h1[:], XL, A.add, ["h1", "P7"], ["h0"])
-        tt(T.hd[:], T.dc[:], XL, A.mult, ["dc", "P7"], ["hd"])
-        scan(T.cs[:], T.h1[:], XL, 0.0, A.add, A.add, ["h1", "P7"], ["cs"])
-        mm([(X2, T.m2[:], T.h0[:], ["m2", "h0"]), (X2, T.nid[:], T.hd[:], ["nid", "hd"]),
-            (X2, T.bo[:], T.cs[:], ["bo", "cs"])], ["P6"], first=False)
+        scan(T.cs[:], T.h1[:], XL, 0.0, A.add, A.add, ["h1", "h1b", "P3"], ["cs"])
+        tt(T.h0[:], T.h1[:], XL, A.add, ["h1", "h1b", "P3"], ["h0"])
+        tt(T.hd[:], T.dc[:], XL, A.mult, ["dc", "P3"], ["hd"])
+        mm([(X2, T.bo[:], T.cs[:], ["bo", "cs"]), (X2, T.m2[:], T.h0[:], ["m2", "h0"]), (X2, T.ndr[:], T.h0[:], ["ndr", "h0"]),
+            (X2, T.nid[:], T.hd[:], ["nid", "hd"])], ["P2"], first=False)
 
-    ms(T.hd1[:], 0.0, ["hd1"])
-    ranks_old()
+    ranks_old(True)
+    side(False)
     ranks()
-    cp(T.hh[:], T.hni[:], ["hni"], ["hh"])
-    tt(T.pk[:, 0:B], ps[:, 0:B], T.fti[:], A.add, ["P0", "P1", "fti"], ["pk"])
-    dma("y", "ld6", T.pk[:, B:B + 512], T.pk[:, 0:512], ["pk"], ["pk2"])
+    side(True)
+    ms(T.sb_[:], 0.0, ["sb"])
+    cp(T.cpk[:, 64:128], T.cpk[:, 0:64], ["cpk"], ["cpk"])
+    ms(T.sa[:, 16:L:STEP], 0.0, ["sa"])
+    cp(T.cpk[:, 128:L], T.cpk[:, 0:128], ["cpk"], ["cpk"])
+    ms(T.sb_[:, 16:L:STEP], 2.0 ** -116, ["sb"])
+    scan(T.scl[:], T.sa[:], T.sb_[:], 2.0 ** -72, A.mult, A.add, ["sa", "sb"], ["scl"])
+    for k in range(16):
+        ts(T.sel[:, 128 * k:128 * k + 128], T.bo[:], T.dg[:, k:k + 1], None, A.mult, None, ["bo", "dg"], ["sel%d" % k])
+    dma("y", "ld5", T.monb[:], T.mon[:], ["aw0r"], ["monb"], 2.5)
+    iota(T.fti[:, B:B + 8], [[0, 8]], W, 0, ["ftz"], small=False)
+    fill(T.utb[:, B:B + 16], 16, 1, ["utz"])
+    for t in range(2):
+        iota(T["aw%d" % t][:, W:W + 2], [[-1, 2]], 1, 0, ["aw%dz" % t])
+    above("tri", "bo")
+    above("nta", "nbo")
+    diag("ta", "tri", -16.0)
+    diag("mxa", "nta", 0.5)
+    diag("nta", "nta", 16.0)
+    diag("i32", "zer", 32.0)
+    fill(T.zef[:], 128, 0, ["zef"])
+    fill(T.ftf[:, B:B + 8], 8, W, ["ftfz"])
+    block("bof", "zef", 1.0)
+    block("bov", "zef", 1.0 / V)
+    empty_buckets([])
+    fill(T.xrow[:, L:L + 8], 8, 0, ["xrz"])
+    block("dq", "zer", 0.5)
+    above("tq", "dq")
+    diag("tq", "tq", 8.0)
+    diag("dq", "dq", 32.5)
+    block("gq", "zer", -64.0)
+    diag("gq", "gq", 2.0 ** 20)
+    iota(T.uu[:, 0:144], [[-16, 3], [1, 48]], 0, 0, ["uu0"])
+    iota(T.wc24[:], [[-V, N], [0, 4]], -1, 0, ["wc24"])
+    for o in range(N):
+        fill(bucket(T.tw, o), CAP, 1, [TW[o]])
+    diag("idf", "zef", 1.0)
+    diag("i8k", "zer", 8192.0)
+    diag("n94", "zer", -0.9375)
+    block("bo16", "zer", 0.0625)
+    fill(T.nones[:], V, -1, ["nones"], ["lf0"])
+
+    def slots():
+        cp(T.hh[:], T.hni[:], ["hni"], ["hh"])
+        act(T.mag[:], T.hh[:], F.Abs, ["hh"], ["mag"])
+        act(T.nsw[:], T.hh[:], F.Sign, ["hh"], ["nsw"], scale=-1.0)
+        act(T.em[:], T.mag[:], F.Relu, ["mag"], ["em"], bias=1.0, scale=-1.0)
+        act(T.ol[:], T.nsw[:], F.Relu, ["nsw"], ["ol"])
+        act(T.opn[:], T.mag[:], F.Sign, ["mag"], ["opn"], bias=4608.5, scale=-1.0)
+        wide(4, [("ta", "em"), ("nbo", "em"), ("nta", "ol")])
+        act(T.rl[:], ps[:, 2048:2048 + V], F.Relu, ["P4", "P5"], ["rl"])
+        wide(6, [("ta", "em"), ("i32", "em"), ("i32", "ol"), ("nid", "rl")])
 
     def late_constants():
-        for t in range(2):
-            ms(T["aw%d" % t][:, W:W + 8], 0.0, ["aw%dz" % t])
-        ms(T.km[:], 1.0, ["km"])
-        ts(T.tmp[:], T.dm[:], 0.0, -2.0, A.is_equal, A.mult, ["dm"], ["tmp"])
-        ms(T.km[:, 0:512:16], 0.0, ["km"])
-        tt(T.n2[:], T.tmp[:], T.bo[:], A.add, ["tmp", "bo"], ["n2"])
-        TL = ps[:, 2048:2096]
-        cp(T.xs[0:8, :], T.hbi[0:8, :], ["hbi"], ["xs"])
-        ms(T.lu[:], 0, ["lu"])
-        ms(T.xrow[:, L:L + 8], 0.5, ["xrz"])
-        for t in range(2):
-            ms(T["ev%d" % t][:, 480:488], 0.0, ["ev%dz" % t])
-        return [(TL, T.x4f[0:8, 15 - r:143 - r], T.xs[0:8, r:B:16], ["x4f", "xs"]) for r in range(16)]
+        ts(T.x1[:], T.crow[:, 0:144], col(C15), None, A.is_equal, None, ["crow", "c5"], ["x1"])
+        cp(T.ftf[:, 0:B], T.fti[:, 0:B], ["fti"], ["ftf"])
+        scaled("mxb", "m2", 1.0 / 64)
+        scaled("olm", "bo", OW)
+        scaled("xk0", "x1", KW)
+        scaled("xk1", "x1", KX)
+        ts(T.low[:], T.sa[:], 0.0, col(LOW), A.mult, A.add, ["sa", "c13"], ["low"])
+        ts(T.jl[:], T.crow[:, 0:16], 16.0, col(R), A.mult, A.add, ["crow", "c0"], ["jl"])
 
-    def scalar_constants():
-        act(col(WE), col(R), F.Exp, ["c0"], ["c22"], bias=76 * math.log(2.0), scale=-math.log(4.0))
-        lin(WO, WE, -2.0 ** -32, 0.0)
-        lin(NE_, WE, -1.0, 0.0)
-        lin(EB, R, -LN, -129.0 * LN)
-        lin(KW, R, 256.0, 0.0)
-        lin(T0, O7, 160.0, 496.0)
-        lin(T3, O7, 48.0, 48.0)
-        lin(EW, UP, 2.0, -1.0)
-        lin(NS, UP, -32767.0, -1.0)
-        lin(NV, UP, -24576.0, 0.0)
-        lin(CA, UP, 48.0, 0.0)
-        lin(CB, UP, -975.0, 1024.0)
-        lin(SS, UP, -1.0, 1.0)
-        lin(PF, UP, 1.0, -1.0)
-        lin(RH, R, 1.0, 0.5)
+    def gap_constants():
+        ts(T.cdd[:], T.uu[:, 0:144], col(R), None, A.is_gt, None, ["uu0", "c0"], ["cdd"])
+        ms(T.lsc[:, 63:N * 64:64], 0.0, ["lsc%d" % o for o in range(N)])
+        ms(T.eqs[:, 191:1152:192], 0.0, ["eqs%d" % o for o in range(N)])
         for c in range(3):
-            lin(D0 + c, R, -1.0 / 1024, (360.0 - 16 * c) / 1024)
-        lin(R1, S1, 1.0 / 524288, 0.0)
-        lin(R0, S0, 1.0 / 524288, 0.0)
-        act(T.bo4[:], T.bo[:], F.Identity, ["bo"], ["bo4"], scale=0.4)
-        act(T.x1g[:], T.bo[:], F.Identity, ["bo"], ["x1g"])
-        act(col(ZW), col(T0), F.Identity, ["c26", "c27", "c3"], ["c16"], bias=col(PF), scale=col(T1))
-        act(col(T2), col(T2), F.Identity, ["c28", "c29"], ["c28"], bias=col(T3))
-        act(col(NW), col(R1), F.Identity, ["c18", "c19"], ["c20"], bias=col(R0), scale=32.0)
-        act(col(NC), col(R0), F.Identity, ["c18", "c19"], ["c21"], bias=col(R1), scale=float(B * me))
-        act(T.jl[:], T.crow[:, 0:16], F.Identity, ["crow", "c0"], ["jl"], bias=col(R), scale=16.0)
-        act(col(IW), col(T2), F.Identity, ["c28", "c12"], ["c17"], scale=col(SS))
-        act(T.xk[:], T.x1[:], F.Identity, ["x1", "c10"], ["xk"], scale=col(KW))
-        for nm, c in (("boz", ZW), ("wn", NW), ("wc", NC), ("bow", IW)):
-            act(T[nm][:], T.bo[:], F.Identity, ["bo", "c%d" % c], [nm], scale=col(c))
-        double(T.cpk, 16, 512, "cpk")
+            x = T.cdd[:, CAP * c + CAP - 1:CAP * c + CAP]
+            ts(x, x, col(D0 + c), None, A.mult, None, ["cdd", "c%d" % (D0 + c)], ["cdd%d" % c])
+        scaled("x8", "x1", 8192.0)
+        scaled("x1f", "x1", 1.0)
 
-    def scalar_constants2():
-        CD = ["cdd0", "cdd1", "cdd2"]
-        act(T.eqb[:], T.cdd[:], F.Sign, CD + ["c30"], ["eqb"] + ["eq%d" % s for s in range(18)], bias=col(RH), scale=-1.0)
-        act(T.tw[:, 0:N * CAP], T.mark[:], F.Identity, ["mark"], ["tw"])
-        act(T.cdd[:], T.eqb[:], F.Relu, ["eqb"], CD)
-        for c in range(3):
-            x = T.cdd[:, SB[c] + SEG[c] - 1:SB[c] + N * SEG[c]:SEG[c]]
-            act(x, T.crow[:, 0:N], F.Identity, ["crow", "c%d" % (D0 + c)], [CD[c]], bias=col(D0 + c), scale=0.0)
-        act(T.x8[:], T.x1[:], F.Identity, ["x1"], ["x8"], scale=8192.0)
-        act(T.x1f[:], T.x1[:], F.Identity, ["x1"], ["x1f"])
-        act(T.xe[:], T.x1[:], F.Identity, ["x1", "c11"], ["xe"], scale=col(EW))
-        act(T.cpk[:, 512:B], T.cpk[:, 0:B - 512], F.Identity, ["cpk"], ["cpk"])
-        double(T.c8, 8, 320, "c8t")
+    def last_constants():
+        fill(T.tt[:], 840, 1, ["tt"], ["lf0"])
+        for t in range(2):
+            fill(T["ev%d" % t][:, 480:488], 8, 0, ["ev%dz" % t])
+        iota(T.nam[:, 0:B], [[1, B]], me * B + 1, 0, ["nam"], r=["lf0"])
+        iota(T.nam[:, B:B + 512], [[1, 512]], me * B + 1, 0, ["nam2"], r=["lf0"])
+        iota(T.rev[:, B:B + 512], [[-1, 512]], B + 33, 0, ["rev2"], r=["lf0"])
+        for j, src, a, b in ((EW, UP, 2.0, -1.0), (NS, UP, -32767.0, -1.0), (NV, UP, -24576.0, 0.0)):
+            lin(j, src, a, b)
+        ts(T.c8[:, 0:8], T.crow[:, 0:8], col(O7), None, A.is_gt, None, ["crow", "c2"], ["c8t"])
+        ts(T.pw[:, 0:8], T.crow[:, 0:8], col(O7), 16384.0, A.is_equal, A.mult, ["crow", "c2"], ["pw"])
+        scaled("x4f", "x4", 16.0)
+        tt(T.c8[:, 0:8], T.c8[:, 0:8], T.pw[:, 0:8], A.add, ["c8t", "pw"], ["c8t"])
+        ts(T.xs[0:8, :], T.hbi[0:8, :], 1.0, None, A.add, None, ["hbi"], ["xs"])
+        ts(T.c8[:, 7:8], T.c8[:, 7:8], -1.0 / 16384, None, A.mult, None, ["c8t"], ["c8t"])
+        scaled("xe", "x1", EW)
+        n = 8
+        while n < 320:
+            m = min(n, 320 - n)
+            cp(T.c8[:, n:n + m], T.c8[:, 0:m], ["c8t"], ["c8t"])
+            n += m
 
-    def keys():
-        act(T.r2[:], T.hh[:], F.Sign, ["hh"], ["r2"])
-        act(T.ka[:], T.hh[:], F.Abs, ["hh"], ["ka"])
-        act(T.kb[:], T.r2[:], F.Relu, ["r2", "c23"], ["kb"], scale=col(WO))
-        act(T.ka[:], T.ka[:], F.Relu, ["ka", "c22", "c31"], ["ka"], bias=col(WE), scale=col(NE_))
+    P45, P67, NN = ps[:, 2048:2048 + V], ps[:, 3072:3072 + V], ps[:, 192:192 + V]
 
-    P45, P67, P01, N23 = ps[:, 2048:2048 + V], ps[:, 3072:3072 + V], ps[:, 0:V], ps[:, 1216:1216 + V]
-    K0 = float(48 * sum(496 + 160 * o for o in range(N)))
+    KF, TL, TL0 = ps[:, 3968:4048], ps[:, 2560:2608], ps[:, 3712:3760]
+
+    def target(bias):
+        act(T.em[:], P67, F.Abs, ["P6", "P7"], ["em"], bias=bias)
+        act(T.dsb[:], P67, F.Identity, ["P6", "P7"], ["dsb"], bias=bias)
+        act(T.tgt[:], T.em[:], F.Relu, ["em"], ["tgt"], bias=1.0, scale=-1.0)
+        wide(6, [("tq", "opn"), ("nid", "dsb"), ("gq", "tgt")])
+        act(T.gg[:], P67, F.Relu, ["P6", "P7", "c15"], ["gg"], bias=col(GB), scale=1.0 / 64)
+        wide(6, [("i8k", "nones"), ("idf", "mag"), ("i8k", "tgt")])
+        act(T.tm[:], P67, F.Relu, ["P6", "P7"], ["tm"])
+        wide(6, [("bo16", "tgt"), ("n94", "nones")])
+        pieces([(KF, sh(T.x8, r), T.tgt[:, r:V:8], ["x8", "tgt"]) for r in range(8)]
+               + [(KF, sh(T.x1f, 8 + r), T.tm[:, r:V:8], ["x1f", "tm"]) for r in range(8)], ["P7"], 2)
+
     tgc = ("tg0", "tg1")
-    scalar_constants()
-    act(T.o1[:], T.hh[:], F.Sign, ["hh"], ["o1"], bias=-4608.5)
-    act(T.x4f[:], T.x4[:], F.Identity, ["x4"], ["x4f"])
-    keys()
+    slots()
+    late_constants()
+    gap_constants()
+    last_constants()
+    pieces([(TL0, T.x4f[0:8, 15 - r:143 - r], T.xs[0:8, r:B:16], ["x4f", "xs"]) for r in range(16)], ["P7"], 2)
+    cp(T.tg0[:], TL0, ["P7"], ["tg0"])
+    target(-16.0)
+    side(False)
 
     for t in range(RO):
         u, un = t % 2, (t + 1) % 2
         aw, awn, ev, tb, lb = T["aw%d" % u], T["aw%d" % un], T["ev%d" % u], T["tb%d" % u], T["lb%d" % u]
-        AW = ["aw%dm" % u, "aw%dr" % u, "aw%dz" % u]
+        AW = ["aw%dm" % u, "aw%dr" % u, "aw%dz" % u, "aw%dh" % u]
         s0 = (L * t) % B
-        ts(T.offu[:], X2, col(RM1), None, A.add, None, ["P6", "c8"], ["offu"])
-        ts(T.offc[:], X2, col(RM1), float(L), A.add, A.min, ["P6", "c8"], ["offc"])
-        cp(T.lw[:, :].indirect(T.offu[:, :]), T.pk[:, s0:s0 + B], ["offu", "pk"] + (["pk2"] if t else []), ["lw"])
-        act(T.xb[:, 0:N * CAP], T.mark[:], F.Identity, ["mark"], ["xb"])
+        ts(T.offu[:], X2, col(RM1), None, A.add, None, ["P2", "c7"], ["offu"])
+        r = ["offu", "rev"] + (["rev2"] if t else [])
+        act(T.lx[:, :].indirect(T.offu[:, SPLIT // 16:48]), T.rev[:, s0 + SPLIT:s0 + B], F.Silu, r, ["lx"], per=SCATTER, n=B - SPLIT)
+        cp(T.lw[:, :].indirect(T.offu[:, 0:SPLIT // 16]), T.rev[:, s0:s0 + SPLIT], r, ["lw"], SCATTER)
+        side(True)
+        ts(T.offc[:], X2, col(RM1), float(L), A.add, A.min, ["P2", "c7"], ["offc"])
+        side(False)
+
+        def rows(j):
+            a, b = HALF[j]
+            scan(T.dsc[:, a:b], T.lw[:, a:b], T.cpk[:, 0:b - a], 0.0, A.max, A.mult, ["lw", "cpk"], ["dsc%d" % j])
+            scan(T.y1[:, a:b], T.lx[:, a:b], T.cpk[:, 0:b - a], 0.0, A.max, A.mult, ["lx", "cpk"], ["y1%d" % j] + (["y10"] if j else []))
+
+        def buyers(j):
+            a, b = HALF[j]
+            tt(T.w24[:, a // 16:b // 16], T.dsc[:, a + 15:b:16], T.y1[:, a + 15:b:16], A.min, ["dsc%d" % j, "y1%d" % j], ["w24"])
+            ts(T.bl[:, a // 16:b // 16], T.w24[:, a // 16:b // 16], B + 33.3, float(B), A.add, A.min, ["w24"], ["bl%d" % j])
+
+        def lists(j):
+            a, b = HALF[j]
+            x = T.bl[:, a // 16:b // 16]
+            cp(T.gl[:, a:b], T.fti[:, :].indirect(x), ["fti", "ftz", "bl%d" % j], ["gl%d" % j], GATHER, b - a)
+            tt(T.utl[:, a:b], T.utb[:, :].indirect(x), T.scl[:, a:b], A.mult, ["utb", "utz", "scl", "bl%d" % j], ["utl%d" % j], GATHER)
 
         def spread(c):
-            b0 = 512 * (c % 4)
-            for k in range(16):
-                o = ps[:, b0 + k:b0 + 512:16]
-                op("p", lambda: g.tensor.matmul(o, T.sel[:, 128 * k:128 * k + 128], T.utl[:, 32 * c:32 * c + 32], True, True),
-                   ["sel%d" % k, "utl%d" % (c > 1)], ["P%d" % (c % 4)], inc=(k == 15))
+            a, b, b0 = CH[c], CH[c + 1], 512 * (c % 3)
+            mm([(ps[:, b0 + k:b0 + 16 * (b - a):16], T.sel[:, 128 * k:128 * k + 128], T.utl[:, a:b],
+                 ["sel%d" % k, "utl0"] + (["utl1"] if b > HALF[0][1] else [])) for k in range(16)], ["P%d" % (c % 3)], alone=True)
 
-        for j, (a, b) in enumerate(((0, 64), (64, L))):
-            ts(T.xi[:, a:b], T.lw[:, a:b], 4095, None, A.bitwise_and, None, ["lw"], ["xi%d" % j])
-            ts(T.uti[:, a:b], T.lw[:, a:b], 12, 15, A.logical_shift_right, A.bitwise_and, ["lw"], ["uti%d" % j])
-            cp(T.gl[:, a:b], T.xi[:, a:b], ["xi%d" % j], ["gl%d" % j])
-            cp(T.utl[:, a:b], T.uti[:, a:b], ["uti%d" % j], ["utl%d" % j])
-            spread(2 * j)
-            spread(2 * j + 1)
-        if t == 0:
-            mm(late_constants(), ["P4"])
-        for c in range(8):
-            act(T.ag[:, 512 * c:512 * c + 512], aw[:, :].indirect(T.gl[:, 32 * c:32 * c + 32]), F.Identity,
-                AW + ["gl%d" % (c > 1)], ["ag%d" % c])
+        def gather(c):
+            a, b = CH[c], CH[c + 1]
+            act(T.ag[:, 16 * a:16 * b], aw[:, :].indirect(T.gl[:, a:b]), F.Identity,
+                AW + ["gl0"] + (["gl1"] if b > HALF[0][1] else []), ["ag%d" % c], per=GATHER)
+
+        def product(c):
+            a, b, b0 = CH[c], CH[c + 1], 512 * (c % 3)
+            x = T.ag[:, 16 * a:16 * b]
+            tt(x, x, ps[:, b0:b0 + 16 * (b - a)], A.mult, ["ag%d" % c, "P%d" % (c % 3)], ["ag%d" % c])
+            if c + 3 < NC:
+                spread(c + 3)
 
         def largest(c):
-            scan(T.ms[:, 512 * c:512 * c + 512], T.km[:], T.ag[:, 512 * c:512 * c + 512], 0.0, A.mult, A.max,
-                 ["km", "ag%d" % c], ["ms%d" % c])
+            a, b = CH[c], CH[c + 1]
+            scan(T.ms[:, 8 * a:8 * b], T.ag[:, 16 * a:16 * b:2], T.ag[:, 16 * a + 1:16 * b:2], 0.0, A.max, A.max,
+                 ["ag%d" % c], ["ms%d" % c])
 
-        for c in range(8):
-            x = T.ag[:, 512 * c:512 * c + 512]
-            tt(x, x, ps[:, 512 * (c % 4):512 * (c % 4) + 512], A.mult, ["ag%d" % c, "P%d" % (c % 4)], ["ag%d" % c])
-            if c < 4:
-                spread(c + 4)
-            if c > 0:
-                largest(c - 1)
-            if t == 0 and c == 2:
-                ts(T.tg0[:], ps[:, 2048:2096], -1.0, -1.0, A.mult, A.add, ["P4"], ["tg0"])
-        wide(2048, [(T.n2[:], T.ka, ["n2", "ka"]), (T.n2[:], T.kb, ["n2", "kb"])], ["P4", "P5"])
-        wide(3072, [(T.idb[:], T.o1, ["idb", "o1"]), (T.bo[:], T.ka, ["bo", "ka"]), (T.bo[:], T.kb, ["bo", "kb"])], ["P6", "P7"])
-        act(T.ntg[:], P45, F.Sign, ["P4", "P5"], ["ntg"])
-        act(ps[:, 0:192], T.ms[:, 15:3072:16], F.Identity, ["ms%d" % c for c in range(6)], ["P0"])
-        largest(7)
-        cp(ps[:, 192:256], T.ms[:, 3072 + 15:4096:16], ["ms6", "ms7"], ["P0"])
-        if t == 0:
-            scalar_constants2()
-        else:
-            act(T.tgt[:], T.ntg[:], F.Relu, ["ntg"], ["tgt"], scale=-1.0)
-            act(T.he[:], P67, F.Sign, ["P6", "P7"], ["he"], bias=-2.0)
-            act(T.r2[:], P67, F.Relu, ["P6", "P7"], ["r2"], scale=-2.0)
-            act(T.ff[:], T.he[:], F.Identity, ["he"], ["ff"], bias=0.96875, scale=0.03125)
-        AG = ["ag%d" % c for c in range(8)]
+        BV, BM, BX = (3, 1), (4, 0), (5, 2)
+
+        def chunks(j):
+            a, b = PARTS[j]
+            return [c for c in range(NC) if CH[c] < b and CH[c + 1] > a]
+
+        def maxima(j):
+            a, b = PARTS[j]
+            cp(ps[:, 512 * BM[j]:512 * BM[j] + b - a], T.ms[:, 8 * a + 7:8 * b:8], ["ms%d" % c for c in chunks(j)], ["P%d" % BM[j]])
+
+        def vote(j, k):
+            a, b = PARTS[j]
+            mm([(ps[:, 512 * BV[j]:512 * BV[j] + b - a], sh(T.x1, k), T.top[:, 16 * a + (b - a) * k:16 * a + (b - a) * (k + 1)],
+                 ["x1", "top%d_%d" % (j, k)])], ["P%d" % BV[j]], first=(k == 0), last=(k == 15))
+
+        def best(j, k):
+            a, b = PARTS[j]
+            tt(T.top[:, 16 * a + (b - a) * k:16 * a + (b - a) * (k + 1)], T.ag[:, 16 * a + k:16 * b:16], ps[:, 512 * BM[j]:512 * BM[j] + b - a],
+               A.not_equal, ["ag%d" % c for c in chunks(j)] + ["P%d" % BM[j]], ["top%d_%d" % (j, k)])
+            vote(j, k)
+
+        def choice(j):
+            a, b = PARTS[j]
+            n, s = b - a, str(j)
+            pv, pm, px = "P%d" % BV[j], "P%d" % BM[j], "P%d" % BX[j]
+            v0, v1 = ps[:, 512 * BV[j]:512 * BV[j] + n], ps[:, 512 * BV[j] + 256:512 * BV[j] + 256 + n]
+            m0, m1 = ps[:, 512 * BM[j]:512 * BM[j] + n], ps[:, 512 * BM[j] + 256:512 * BM[j] + 256 + n]
+            x0 = ps[:, 512 * BX[j]:512 * BX[j] + n]
+            act(T.wv[:, a:b], v0, F.Silu, [pv], ["wv" + s], bias=-16.0, scale=-4.0)
+            mm([(m0, T.mxa[:], T.wv[:, a:b], ["mxa", "wv" + s]), (m0, T.mxb[:], T.wv[:, a:b], ["mxb", "wv" + s])], [pm])
+            ts(m0, m0, 0.0, None, A.is_lt, None, [pm], [pm])
+            tt(T.y1[:, a:b], T.xc[:, a:b], m0, A.mult, ["xc", pm], ["y1" + s])
+            mm([(v0, T.bov[:], T.y1[:, a:b], ["bov", "y1" + s])], [pv])
+            act(T.ch[:, a:b], m0, F.Identity, [pm], ["ch" + s])
+            mm([(x0, T.bof[:], T.y1[:, a:b], ["bof", "y1" + s])], [px])
+            act(T.xrow[:, a:b], x0, F.Identity, [px], ["xrow" + s], bias=320.5)
+            ts(T.ind[:, a:b], v0, MAGIC, col(OM), A.add, A.is_equal, [pv, "c12"], ["ind" + s])
+            init = 0.0 if j == 0 else ps[:, 512 * BV[j - 1] + 255 + a - PARTS[j - 1][0]:512 * BV[j - 1] + 256 + a - PARTS[j - 1][0]]
+            scan(v1, T.low[:, a:b], T.ind[:, a:b], init, A.mult, A.add, ["low", "ind" + s] + (["P%d" % BV[j - 1]] if j else []), [pv])
+            tt(T.zz[:, a:b], T.ind[:, a:b], v1, A.mult, ["ind" + s, pv], ["zz" + s])
+            mm([(m1, T.olm[:], T.zz[:, a:b], ["olm", "zz" + s])], [pm])
+            scan(T.dsc[:, a:b], m1, T.cpk[:, 0:n], 0.0, A.max, A.mult, [pm, "cpk"], ["dsc0", "dsc1"] if j == 0 else ["dsd"])
+            ts(T.bu[:, a // 16:b // 16], T.dsc[:, a + 15:b:16], -1.0, None, A.mult, None, ["dsc0"] if j == 0 else ["dsd"], ["bu" + s])
+            cp(T.xb[:, :].indirect(T.bu[:, a // 16:b // 16]), T.xrow[:, a:b], ["bu" + s, "xrow" + s], XB, SCATTER)
+
+        def masks(j):
+            a, b = PARTS[j]
+            s, px, x1 = str(j), "P%d" % BX[j], ps[:, 512 * BX[j] + 256:512 * BX[j] + 256 + (b - a) // 16]
+            pieces([(x1, T.idb[:], T.jl[:, 0:(b - a) // 16], ["idb", "jl"])]
+                   + [(x1, sh(T["xk" + s], r), T.ch[:, a + r:b:16], ["xk" + s, "ch" + s]) for r in range(16)], [px], 6)
+            cp(T.ku[:, a // 16:b // 16], x1, [px], ["ku" + s])
+            act(T.sgn[:, a:b], T.top[:, 16 * a:16 * b].indirect(T.ku[:, a // 16:b // 16]), F.Identity,
+                ["ku" + s] + ["top%d_%d" % (j, k) for k in range(16)], ["sgn" + s], bias=-1.0, scale=2.0, per=GATHER)
+            tt(T.tw[:, :].indirect(T.bu[:, a // 16:b // 16]), T.sgn[:, a:b], T.nml[:, a:b], A.mult, ["bu" + s, "sgn" + s, "nml"], TW, SCATTER)
+
+        rows(0)
+        buyers(0)
+        side(True)
+        rows(1)
+        side(False)
+        lists(0)
+        for c in range(2):
+            spread(c)
+            gather(c)
+        buyers(1)
+        lists(1)
+        spread(2)
+        for c in range(2, NC):
+            gather(c)
+        act(T.xc[:], T.ftf[:, :].indirect(T.bl[:, :]), F.Identity, ["ftf", "ftfz", "bl0", "bl1"], ["xc"], bias=-319.5, per=GATHER)
+        side(True)
+        act(T.nml[:], T.nam[:, 0:B + 8].indirect(T.bl[:, :]), F.Identity, ["nam", "nam2", "bl0", "bl1"], ["nml"], per=GATHER)
+        side(False)
+        product(0)
+        c0 = chunks(0)[-1] + 1
+        for c in range(1, c0 + 1):
+            product(c)
+            largest(c - 1)
+        maxima(0)
         for k in range(16):
-            x = T.top[:, L * k:L * k + L]
-            tt(x, T.ag[:, k:4096:16], ps[:, 0:L], A.is_equal, AG + ["P0"], ["top%d" % k])
-            mm([(ps[:, 512:768], sh(T.x1, k), x, ["x1", "top%d" % k])], ["P1"], first=(k == 0), last=(k == 15))
-        act(T.wv[:], ps[:, 512:768], F.Exp, ["P1", "c9"], ["wv"], bias=col(EB), scale=16.0 * LN)
-        ts(T.owi[:], T.lw[:, 0:L], 16, 7, A.logical_shift_right, A.bitwise_and, ["lw"], ["owi"])
-        ts(T.pci[:], T.lw[:, 0:L], 19, None, A.logical_shift_right, None, ["lw"], ["pci"])
-        mm([(ps[:, 1024:1280], T.bo4[:], T.wv[:], ["bo4", "wv"])], ["P2"])
-        cp(T.pcb[:], T.pci[:], ["pci"], ["pcb"])
-        CH, KL, OL = ps[:, 1280:1536], ps[:, 256:272], ps[:, 1792:2048]
-        tt(CH, T.wv[:], ps[:, 1024:1280], A.is_ge, ["wv", "P2"], ["P2"])
-        tt(T.y2[:], CH, T.owi[:], A.mult, ["P2", "owi"], ["y2"])
-        mm([(ps[:, 1536:1792], T.bo[:], T.y2[:], ["bo", "y2"])], ["P3"])
-        tt(T.y1[:], CH, T.xi[:], A.mult, ["P2", "xi0", "xi1"], ["y1"])
-        act(T.ch[:], CH, F.Identity, ["P2"], ["ch"])
-        mm([(ps[:, 512:768], T.x1g[:], T.y1[:], ["x1g", "y1"])], ["P1"])
-        act(T.xrow[:, 0:L], ps[:, 512:768], F.Identity, ["P1"], ["xrow"], bias=1.0)
-        if t == 0:
-            act(T.tgt[:], T.ntg[:], F.Relu, ["ntg"], ["tgt"], scale=-1.0)
-            act(T.he[:], P67, F.Sign, ["P6", "P7"], ["he"], bias=-2.0)
-        ts(T.ind[:], ps[:, 1536:1792], col(O7), None, A.is_equal, None, ["P3", "c2"], ["ind"])
-        scan(ps[:, 1024:1280], T.ones[:], T.ind[:], 0.0, A.mult, A.add, ["ones", "ind"], ["P2"])
-        mm([(OL, T.bow[:], T.ind[:], ["bow", "ind"])], ["P3"], last=False)
-        kl = [(KL, T.idb[:], T.jl[:], ["idb", "jl"])] + [(KL, sh(T.xk, r), T.ch[:, r:L:16], ["xk", "ch"]) for r in range(16)]
-        mm(kl[:9], ["P0"], last=False)
-        tt(T.zz[:], T.ind[:], ps[:, 1024:1280], A.mult, ["ind", "P2"], ["zz"])
-        ts(T.zc[:], T.zz[:], col(CA), col(CB), A.max, A.min, ["zz", "c14", "c15"], ["zc"])
-        mm([(OL, T.boz[:], T.zc[:], ["boz", "zc"])], ["P3"], first=False)
-        mm(kl[9:], ["P0"], first=False)
-        mm([(ps[:, 768:1024], T.wc[:], T.ones[:], ["wc", "ones"]), (ps[:, 768:1024], T.wn[:], T.pcb[:], ["wn", "pcb"])], ["P1"])
-        scan(T.lsc[:, 0:L], OL, T.cpk[:, 0:L], 0.0, A.max, A.mult, ["P3", "cpk"], ["lsc"])
-        ts(T.bu[:], T.lsc[:, 15:L:16], -1.0, -K0, A.mult, A.add, ["lsc"], ["bu"])
-        cp(T.ku[:], KL, ["P0"], ["ku"])
-        act(T.sgn[:], T.top[:, :].indirect(T.ku[:, :]), F.Identity, ["ku"] + ["top%d" % k for k in range(16)], ["sgn"], bias=1.0, scale=-2.0)
-        cp(T.xb[:, :].indirect(T.bu[:, :]), T.xrow[:, 0:L], ["bu", "xrow"], ["xb"])
-        tt(T.vb[:], T.sgn[:], ps[:, 768:1024], A.mult, ["sgn", "P1"], ["vb"])
-        scan(T.lsc[:], T.xb[:, 0:N * CAP], T.cpk[:, 0:N * CAP], 0.0, A.max, A.mult, ["xb", "cpk"], ["lsc"])
-        cp(T.tw[:, :].indirect(T.bu[:, :]), T.vb[:], ["bu", "vb"], ["tw"])
-        order("g", ["tw"], [])
-        dl = deal(me)
-        g.remote_dma_fused([RemoteDMATransfer(dst_ids=[did(q)], dma_engine_mask=bits(dl[q]), remote_sem=T.sem["ab%d" % t],
-                                              srcs=[T.tw[:, CAP * q:CAP * q + CAP]], dsts=[tb[:, CAP * me:CAP * me + CAP]])
-                            for q in others], local_sem=T.sem["lt%d" % t])
-        nl = sum(len(dl[q]) for q in others)
-        mark(("lt%d" % t, nl, "d"), ["tw"], [])
-        ends["lt%d" % t] = nl
-        tt(T.w18[:], T.lsc[:, 15:N * CAP:16], T.wc18[:], A.add, ["lsc", "wc18"], ["w18"])
-        for s in range(18):
-            o, c = divmod(s, 3)
-            e0 = SB[c] + SEG[c] * o
-            x, y, z = T.eqb[:, e0:e0 + SEG[c] - 1], T.xb[:, CAP * o + 16 * c:CAP * o + CAP], T.lsc[:, 16 * s + 15:16 * s + 16]
-            if s < 14:
-                act(x, y, F.Abs, ["xb", "lsc"], ["eq%d" % s], bias=z)
-            else:
-                ts(x, y, z, 0.0, A.add, A.not_equal, ["xb", "lsc"], ["eq%d" % s])
-        for c in range(3):
-            ts(T.eqb[:, SB[c] + SEG[c] - 1:SB[c] + N * SEG[c]:SEG[c]], T.w18[:, c:18:3], 1.0 / 1024, None, A.mult, None,
-               ["w18"], ["eqb%d" % c] + (["eqb"] if c == 0 else []))
-        scan(T.eqs[:], T.eqb[:], T.cdd[:], 1.0, A.min, A.max,
-             ["eqb", "eqb0", "eqb1", "eqb2", "cdd0", "cdd1", "cdd2"] + ["eq%d" % s for s in range(18)], ["eqs"])
-        for c in range(3):
-            ts(T.lu[:, c:24:4], T.eqs[:, SB[c] + SEG[c] - 1:SB[c] + N * SEG[c]:SEG[c]], -1024.0, 1000.0, A.mult, A.add,
-               ["eqs"], ["lu%d" % c] + (["lu"] if c == 0 else []))
-        LU = ["lu", "lu0", "lu1", "lu2"]
-        bcast(T.lu[:], lb[:, 24 * me:24 * me + 24], "ab%d" % t, "ll%d" % t, LU)
-        arrive("bids", "ab%d" % t, nb + sum(len(deal(q)[me]) for q in others))
-        tt(T.uu[:], T.hh[:], P45, A.max, ["hh", "P4", "P5"], ["uu"])
-        act(T.xg[:], T.xrow[:, :].indirect(T.offc[:, :]), F.Identity, ["xrow", "xrz", "offc"], ["xg"])
-        act(T.tn[:], T.uu[:], F.Relu, ["uu"], ["tn"], scale=-1.0)
-        act(T.tt[:], T.nam[:, 0:688], F.Identity, ["nam"], ["tt"], bias=1.5, scale=0.0)
-        if t == 0:
-            act(T.r2[:], P67, F.Relu, ["P6", "P7"], ["r2"], scale=-2.0)
-            act(T.ff[:], T.he[:], F.Identity, ["he"], ["ff"], bias=0.96875, scale=0.03125)
-        act(P45, aw[:, mine], F.Identity, ["aw%dm" % u], ["P4", "P5"])
-        act(T.ntg[:], T.tgt[:], F.Identity, ["tgt"], ["ntg"], bias=1.0, scale=-1.0)
-        KF = ps[:, 0:80]
-        mm([(KF, sh(T.x8, r), T.tgt[:, r:V:8], ["x8", "tgt"]) for r in range(8)]
-           + [(KF, sh(T.x1f, 8 + r), T.tn[:, r:V:8], ["x1f", "tn"]) for r in range(8)], ["P0"])
-        scan(T.xs[:], T.xg[:], T.cpk[:], 0.0, A.max, A.mult, ["xg", "cpk"], ["xs"])
-        ko, kn = tgc[t % 2], tgc[(t + 1) % 2]
-        ts(T.m48[:], T.xs[:, 15:B:16], -0.75, None, A.is_gt, None, ["xs"], ["m48"])
+            best(0, k)
+            if (k + 1) % (16 // (NC - c0)) == 0 and c0 + 1 < NC - BEHIND:
+                c0 += 1
+                product(c0)
+                largest(c0 - 1)
+        side(2)
+        choice(0)
+        side(True)
+        masks(0)
+        side(False)
+        for c in range(c0 + 1, NC):
+            product(c)
+            largest(c - 1)
+        largest(NC - 1)
+        maxima(1)
+        for k in range(16):
+            best(1, k)
+        choice(1)
+        side(True)
+        masks(1)
+        bids(tb, t)
+        act(T.xg[:], T.xrow[:, :].indirect(T.offc[:, :]), F.Identity, ["xrow0", "xrow1", "xrz", "offc"], ["xg"], per=GATHER)
+        pieces([(TL, sh(T.x1f, r), T.xg[:, r:B:16], ["x1f", "xg"]) for r in range(16)], ["P5"], 2)
+        side(False)
+
+        def entries(o):
+            scan(T.lsc[:, 64 * o:64 * o + CAP], bucket(T.xb, o), T.cpk[:, 0:CAP], 0.0, A.max, A.mult, [XB[o], "cpk"], ["lsc%d" % o])
+
+        def compare(o):
+            for c in range(3):
+                e0 = 192 * o + CAP * c
+                ts(T.eqb[:, e0:e0 + CAP], bucket(T.xb, o), T.lsc[:, 64 * o + 16 * c + 15:64 * o + 16 * c + 16], 0.0,
+                   A.add, A.is_equal, [XB[o], "lsc%d" % o], ["eqb%d_%d" % (o, c)])
+
+        def repeated(o):
+            scan(T.eqs[:, 192 * o:192 * o + 144], T.eqb[:, 192 * o:192 * o + 144], T.cdd[:], 0.0, A.max, A.mult,
+                 ["eqb%d_%d" % (o, c) for c in range(3)] + ["cdd0", "cdd1", "cdd2"], ["eqs%d" % o])
+
+        for o in range(N):
+            entries(o)
+        for o in range(N):
+            compare(o)
+            if o > 0:
+                repeated(o - 1)
+        tt(T.w24[:], T.wc24[:], T.lsc[:, 15:N * 64:16], A.subtract, ["wc24"] + ["lsc%d" % o for o in range(N)], ["w24"])
+        repeated(N - 1)
+        tt(T.lf[:], T.eqs[:, 47:1152:48], T.w24[:], A.max, ["w24"] + ["eqs%d" % o for o in range(N)], ["lf"])
+        cp(T.lu[:], T.lf[:], ["lf"], ["lu"])
+        bcast(T.lu[:], lb[:, 24 * me:24 * me + 24], "ab%d" % t, "ll%d" % t, ["lu", "lf%d" % t], 2.2)
+        arrive("bids", "ab%d" % t, nb + sum(len(deal(q)[me]) for q in others), ["lt%d" % t, "ll%d" % t])
+        side(True)
         if t + 1 < RO:
-            ms(T.lw[:, 0:L], W + (N << 16), ["lw"])
-        tt(T.t48[:], T.m48[:], T[ko][:], A.mult, ["m48", ko], ["t48"])
+            ms(T.lw[:, 0:L], 0.25, ["lw"])
+            act(T.lx[:, 0:L], T.nml[:], F.Identity, ["nml"], ["lx"], bias=0.25, scale=0.0)
+            for o in range(N):
+                ms(bucket(T.xb, o), float(V * o + V + 1), [XB[o]])
+            tt(P67, aw[:, mine], P67, A.mult, ["aw%dm" % u, "P6", "P7"], ["P6", "P7"])
         rot = ((0, 32, 16), (32, 48, -32)) if t + 1 < RO else ((0, 48, 0),)
         for a, b, d in rot:
-            tt(T[kn][:, a:b], T.xs[:, 16 * (a + d) + 15:16 * (b + d):16], T.t48[:, a + d:b + d], A.min, ["xs", "t48"], [kn + str(a)])
-        wr[kn] = wr[kn + str(rot[-1][0])]
-        rd[kn] = []
-        ts(T.tgi[:], T[kn][:], -1.0, -1.0, A.mult, A.add, [kn], ["tgi"])
-        ts(T.tg8[:], T.tgi[:], 3, None, A.logical_shift_right, None, ["tgi"], ["tg8"])
-        for a, b, d in rot:
-            cp(T.h1[:, a:b], T.h0[:, a + d:b + d], ["h0"], ["h1"])
-        cp(T.tgu[:], T.tg8[:], ["tg8"], ["tgu"])
+            cp(T.h1[:, a:b], T.h0[:, a + d:b + d], ["h0"], ["h1"] if a == 0 else ["h1b"])
         if t + 1 < RO:
-            tt(T.hd1[:], T.h1[:], T.dc[:], A.mult, ["h1", "dc"], ["hd1"])
-        tt(P67, T.ff[:], P45, A.mult, ["ff", "P4", "P5"], ["P6", "P7"])
+            tt(T.hd1[:], T.h1[:], T.dc[:], A.mult, ["h1", "h1b", "dc"], ["hd1"])
+        ko, kn = tgc[t % 2], tgc[(t + 1) % 2]
+        ts(T.m48[:], TL, 0.5, None, A.is_lt, None, ["P5"], ["m48"])
+        tt(T.t48[:], T.m48[:], T[ko][:], A.mult, ["m48", ko, ko + "b"], ["t48"])
+        for a, b, d in rot:
+            tt(T[kn][:, a:b], T.t48[:, a + d:b + d], ps[:, 2560 + a + d:2560 + b + d], A.max, ["P5", "t48"], [kn if a == 0 else kn + "b"])
+        ts(T.m48[:], T[kn][:], 1.0 / 128, -0.5625, A.mult, A.add, [kn, kn + "b"], ["m48"])
+        ts(T.tgu[:], T.m48[:], MAGIC, -MAGIC, A.add, A.add, ["m48"], ["tgu"])
+        if t + 1 == RO:
+            ts(T.offu[:], T[kn][:], 1.0 / 16, -1.0, A.mult, A.add, [kn], ["offu"])
+            ts(T.t48[:], T[kn][:], 2.0 ** -16, -2.0 ** -12, A.mult, A.add, [kn], ["t48"])
+            tt(T.xs[:], aw[:, :].indirect(T.offu[:, :]), T.monb[:], A.mult, AW + ["offu", "monb"], ["xs"], GATHER)
+        side(False)
         for q in range(N - 1, -1, -1):
             if q == me:
-                x, y, r = T.tw[:, CAP * me:CAP * me + CAP], T.lu[:, 4 * me:4 * me + 3], ["tw"] + LU
+                x, y, r = bucket(T.tw, me), T.lu[:, 4 * me:4 * me + 3], [TW[me], "lu"]
             else:
                 x, y, r = tb[:, CAP * q:CAP * q + CAP], lb[:, 24 * q + 4 * me:24 * q + 4 * me + 3], ["bids"]
-            ts(T.tt[:, :].indirect(y), x, 1.0, 1.0, A.mult, A.add, r, ["tt"])
+            ts(T.tt[:, :].indirect(y), x, 1.0, 1.0, A.mult, A.add, r, ["tt"], SCATTER)
         for j in range(2):
-            act(ps[:, 1216 + 320 * j:1536 + 320 * j], T.tt[:, 320 * j:320 * j + 320], F.Abs, ["tt"], ["P%d" % (2 + j)], bias=-1.0)
-        tt(T.he[:, 0:320], T.tt[:, 0:320], ps[:, 2048:2368], A.min, ["tt", "P4"], ["he"])
+            act(ps[:, 192 + 320 * j:512 + 320 * j], T.tt[:, 320 * j:320 * j + 320], F.Abs, ["tt"], ["P%d" % j], bias=-1.0)
+        tt(P67, T.tt[:, 0:V], P67, A.max, ["tt", "P6", "P7"], ["P6", "P7"])
+
+        def new_alpha(a, b, w):
+            if t + 1 < RO:
+                tt(awn[:, me * V + a:me * V + b], aw[:, me * V + a:me * V + b], ps[:, 3072 + a:3072 + b], A.min, ["aw%dm" % u, "P6", "P7"], w)
+            else:
+                ts(T.fac[:, me * V + a:me * V + b], ps[:, 3072 + a:3072 + b], 1.0, None, A.min, None, ["P6", "P7"], ["facm"])
+
         for j in range(2):
-            scan(T.uu[:, 320 * j:320 * j + 320], ps[:, 1216 + 320 * j:1536 + 320 * j], T.c8[:], 0.0, A.max, A.mult,
-                 ["P%d" % (2 + j), "c8t"], ["uu%d" % j] + (["uu"] if j == 0 else []))
-        ts(T.nab[:], T.uu[:, 7:V:8], col(NS), col(NV), A.mult, A.add, ["uu", "uu0", "uu1", "c13", "c6"], ["nab"])
+            scan(T.uu[:, 320 * j:320 * j + 320], ps[:, 192 + 320 * j:512 + 320 * j], T.c8[:], 0.0, A.max, A.mult,
+                 ["P%d" % j, "c8t"], ["uu%d" % j])
+            if j == 0:
+                new_alpha(0, EARLY, ["aw%dm" % un])
+        ts(T.nab[:], T.uu[:, 7:V:8], col(NS), col(NV), A.mult, A.add, ["uu0", "uu1", "c10", "c11"], ["nab"])
         evm = ev[:, 80 * me:80 * me + 80]
-        tt(evm, T.nab[:], KF, A.min, ["nab", "P0"], ["evm%d" % u])
-        bcast(evm, evm, "ae%d" % t, "le%d" % t, ["evm%d" % u])
-        arrive("evr", "ae%d" % t, nb)
-        act(T.en[:], N23, F.Identity, ["P2", "P3"], ["en"], bias=3.0, scale=-4.0)
-        act(T.tn[:], N23, F.Identity, ["P2", "P3"], ["tn"], bias=MAGIC)
-        act(N23, T.tn[:], F.Identity, ["tn"], ["P2", "P3"], bias=-MAGIC)
-        wide(0, [(T.idb[:], T.ntg, ["idb", "ntg"]), (T.nid[:], T.r2, ["nid", "r2"])], ["P0", "P1"])
-        tt(T.he[:, 320:V], T.tt[:, 320:V], ps[:, 2368:2048 + V], A.min, ["tt", "P4", "P5"], ["he2"])
-        tt(awn[:, mine], T.he[:], P67, A.max, ["he", "he2", "P6", "P7"], ["aw%dm" % un])
-        bcast(awn[:, mine], awn[:, mine], "aa%d" % (t + 1), "la%d" % (t + 1), ["aw%dm" % un])
-        arrive("aw%dr" % un, "aa%d" % (t + 1), nb)
-        if t + 1 == RO:
-            dma("y", "st0", T.yal[:], awn[:, mine], ["aw%dm" % un], [])
-
-        def codes():
-            tt(P01, P01, T.en[:], A.max, ["P0", "P1", "en"], ["P0", "P1"])
-            tt(T.he[:], T.hh[:], P01, A.mult, ["hh", "P0", "P1"], ["he", "he2"])
-            tt(N23, N23, T.tgt[:], A.mult, ["P2", "P3", "tgt"], ["P2", "P3"])
-            yield
-            tt(T.hh[:], T.he[:], N23, A.add, ["he", "P2", "P3"], ["hh"])
-            yield
-            yield
-
-        cd = codes()
+        tt(evm, T.nab[:], KF, A.min, ["nab", "P7"], ["evm%d" % u])
+        bcast(evm, evm, "ae%d" % t, "le%d" % t, ["evm%d" % u], 1.8)
+        arrive("evr", "ae%d" % t, nb, ["le%d" % t])
+        new_alpha(EARLY, V, ["aw%dm" % un])
+        if t + 1 < RO:
+            share_alpha(un, t + 1)
+        else:
+            bcast(T.fac[:, mine], T.fac[:, mine], "aa%d" % RO, "la%d" % RO, ["facm"], 3.5)
+            arrive("facr", "aa%d" % RO, nb, ["la%d" % RO])
+        side(True)
+        tt(T.mv[:], T.gg[:], NN, A.min, ["gg", "P0", "P1"], ["mv"])
+        act(T.nsw[:], T.mv[:], F.Sign, ["mv"], ["nsw"], bias=0.75, scale=-1.0)
+        act(T.rl[:], T.mv[:], F.Relu, ["mv"], ["rl"], bias=64.0, scale=-64.0)
         if t + 1 < RO:
             ranks_old()
-        next(cd)
+            fill(T.tt[:, 0:V], V, 1, ["tt"], ["lf%d" % (t + 1)])
+        wide(4, [("i8k", "nones"), ("idf", "mag"), ("i8k", "nsw")])
+        wide(6, [("idb", "dsb"), ("dq", "nsw"), ("nid", "rl")])
+        tt(T.mag[:], T.mv[:], P45, A.max, ["mv", "P4", "P5"], ["mag"])
+        if t + 1 < RO:
+            target(24.0)
+        side(False)
         s1 = (L * (t + 1)) % B if t + 1 < RO else 0
         tt(T.tog[:], ev[:, :].indirect(T.tgu[:, :]), T.nam[:, s1:s1 + B], A.is_equal,
-           ["evm%d" % u, "evr", "ev%dz" % u, "tgu", "nam"], ["tog"])
-        mm([(XL, sh(T.xe, r), T.tog[:, r:B:16], ["xe", "tog"]) for r in range(16)], ["P7"])
-        next(cd)
+           ["evm%d" % u, "evr", "ev%dz" % u, "tgu", "nam", "nam2"], ["tog"], GATHER)
+        mm([(XL, sh(T.xe, r), T.tog[:, r:B:16], ["xe", "tog"]) for r in range(16)], ["P3"])
         if t + 1 < RO:
             ranks()
-        else:
-            tt(T.h0[:], T.h1[:], XL, A.add, ["h1", "P7"], ["h0"])
-        next(cd)
-        if t + 1 < RO:
-            keys()
-        else:
-            dma("s", "st1", T.yh[:], T.hh[:], ["hh"], [])
 
-    hf = "h0"
-    ts(T.m48[:], T[hf][:], float(W), None, A.mult, None, [hf], ["m48"])
-    tt(T.t48[:], T.m48[:], T.tgi[:], A.max, ["m48", "tgi"], ["t48"])
-    cp(T.finu[:], T.t48[:], ["t48"], ["finu"])
-    aw = T["aw%d" % (RO % 2)]
-    AW = ["aw%d%s" % (RO % 2, x) for x in "mrz"]
+    side(True)
+    ms(T.fac[:, 4096:4112], 0.0, ["facz"])
+    tt(T.tm[:], aw[:, mine], T.fac[:, mine], A.mult, ["aw%dm" % u, "facm"], ["tm"])
+    dma("s", "st0", T.yal[:], T.tm[:], ["tm"], [], 2.5)
+    act(P67, P67, F.Sign, ["P6", "P7"], ["P6", "P7"], bias=-24.5, scale=-1.0)
+    tt(T.hh[:], T.mag[:], P67, A.mult, ["mag", "P6", "P7"], ["hh"])
+    dma("y", "st1", T.yh[:], T.hh[:], ["hh"], [], 2.5)
+    side(False)
+    tt(T.m48[:], T.h1[:], XL, A.add, ["h1", "P3"], ["m48"])
+    tt(T.t48[:], T.m48[:], T.t48[:], A.max, ["m48", "t48"], ["t48"])
+    ts(T.finu[:], T.t48[:], 4096.0, None, A.mult, None, ["t48"], ["finu"])
     for j, e in ((0, "y"), (1, "s")):
         a = 384 * j
-        tt(T.xg[:, a:a + 384], aw[:, :].indirect(T.finu[:, 24 * j:24 * j + 24]), T.monb[:, a:a + 384], A.mult,
-           AW + ["finu", "monb"], ["yp%d" % j])
-        dma(e, "st%d" % (2 + j), T.yp[:, a:a + 384], T.xg[:, a:a + 384], ["yp%d" % j], [])
-    for e in ("v", "s", "p", "g"):
-        ends[SEM[e]] = cnt[e]
-    for sem in ends:
-        if all(seen[e].get(sem, 0) < ends[sem] for e in Q):
-            g.wait_ge(T.sem[sem], ends[sem])
+        tt(T.xg[:, a:a + 384], T.fac[:, :].indirect(T.finu[:, 24 * j:24 * j + 24]), T.xs[:, a:a + 384], A.mult,
+           ["facm", "facr", "facz", "finu", "xs"], ["yp%d" % j] + (["xg"] if j == 0 else []), GATHER)
+        dma(e, "st%d" % (2 + j), T.yp[:, a:a + 384], T.xg[:, a:a + 384], ["yp%d" % j], [], 2.5)
+    issue()

import math
from concourse.bass import DstId, RemoteDMATransfer
from concourse.mybir import AluOpType as A, ActivationFunctionType as F

N, V, B, L, CAP, RO = 6, 640, 768, 256, 48, 4
W = N * V
RG = 272
STEP = 30
CH = [0] + list(range(16, L, STEP)) + [L]
NC = len(CH) - 1
SPLIT = 384
BEHIND = 1
EARLY = 320
HALF = ((0, 64), (64, L))
PARTS = ((0, 192), (192, L))
f32, bf, i32, u16 = "float32", "bfloat16", "int32", "uint16"
SCRATCH = {"ps": ("psum", [128, 4096], f32)}


def _sb(dtype, **kw):
    for k in kw:
        SCRATCH[k] = ("sbuf", [128, kw[k]], dtype)


for _t in range(2):
    SCRATCH["aw%d" % _t] = ("sbuf", [128, W + 8], f32)
    SCRATCH["ev%d" % _t] = ("sbuf", [128, 488], f32)
    SCRATCH["tb%d" % _t] = ("sbuf", [128, N * CAP], f32)
    SCRATCH["lb%d" % _t] = ("sbuf", [128, N * 24], u16)
_sb(i32, fti=B + 8, hni=V, hbi=B, ci=8)
_sb(u16, offu=48, offc=48, gl=L, bl=16, ku=16, bu=16, lu=24, tgu=48, finu=48)
_sb(bf, utb=B + 16, monb=B, fac=4112, zer=128, idb=128, nid=128, ndr=128, bo=128, nbo=128, tri=128, m2=128, ta=128, nta=128, i32=128, tq=128,
    gq=128, dq=128, i8k=128, n94=128, bo16=128, mxa=128, mxb=128, olm=128, sel=2048, x1=144, xe=144, xk0=144, xk1=144, x8=144, x4=144,
    dc=48, jl=16, h0=48, h1=48, cs=48, hd=48, hd1=48, nones=V, low=L, sa=L, sb_=L, scl=L, utl=L, top=4096, wv=L, ch=L, ind=L,
    zz=L, tog=B, em=V, ol=V, opn=V, dsb=V, tgt=V, gg=V, nsw=V, rl=V, cdd=144, eqb=1152, eqs=1152)
_sb(f32, cf=32, dm=128, zef=128, crow=152, grow=128, dg=16, pw=16, x1f=144, x4f=144, idf=128, bof=128,
    bov=128, c8=320, nam=B + 512, rev=B + 512, lx=2304, nml=L, cpk=L, wc24=24, w24=24, lf=24, ftf=B + 8, lw=2304, ag=4096, ms=2048, xc=L, y1=L,
    xrow=264, sgn=L, dsc=L, xb=7 * RG, tw=7 * RG, lsc=N * 64, xg=B, xs=B, m48=48, t48=48, tg0=48, tg1=48, tt=840, uu=V, nab=80,
    hh=V, mag=V, tm=V, mv=V)
SEMAPHORES = (["cv", "cs_", "cp", "cg"] + ["ld%d" % k for k in range(6)] + ["st%d" % k for k in range(4)]
              + ["%s%d" % (p, t) for p in ("ab", "ae", "lt", "ll", "le") for t in range(RO)]
              + ["%s%d" % (p, t) for p in ("ah", "lx", "lf") for t in range(RO)]
              + ["%s%d" % (p, t) for p in ("aa", "la") for t in range(RO + 1)])
CYCLE, T_CYCLE, V_CALL, S_CALL, SIGNAL, GATHER, SCATTER, AHEAD, SPARE = 0.00083, 0.00055, 0.03, 0.2, 0.1, 1.5, 3.5, -0.5, 0.05
MAGIC = 12582912.0


def rank_program(g, core, T, topo):
    me = T.rank_of(core)
    if me is None:
        return
    Q = {"v": g.vector, "s": g.scalar, "p": g.tensor, "g": g, "y": g.sync}
    SEM = {"v": "cv", "s": "cs_", "p": "cp", "g": "cg"}
    calls, wr, rd, aside = [], {}, {}, [False]

    def side(on):
        aside[0] = on

    def note(e, fn, r, w, busy, after=0.0, tok=None):
        dep = set()
        for k in r:
            if k in wr:
                dep.add(wr[k])
            if k[0] == "P":
                dep.update(i for i in rd.get(k, []) if calls[i]["e"] != e)
        for k in w:
            if k in wr:
                dep.add(wr[k])
            dep.update(rd.get(k, []))
        calls.append({"e": e, "fn": fn, "dep": dep, "busy": busy, "after": after, "tok": tok, "side": aside[0]})
        for k in r:
            rd.setdefault(k, []).append(len(calls) - 1)
        for k in w:
            wr[k] = len(calls) - 1
            rd[k] = []

    def width(x):
        return x.shape[1] if len(x.shape) > 1 else 1

    def short(*xs):
        return all(str(x.dtype).endswith("16") for x in xs)

    def vec(fn, r, w, n, per):
        note("v", fn, r, w, V_CALL + CYCLE * max(64, n * per))

    def dma(e, sem, out, in_, r, w, after):
        note(e, lambda: Q[e].dma_start(out, in_).then_inc(T.sem[sem], 16), r, w, 0.05, after, (sem, 16))

    def ts(out, in0, s1, s2, o0, o1, r, w, per=None):
        n, per = width(in0), per or (0.5 if short(out, in0) else 1)
        if o1 is None:
            vec(lambda: g.vector.tensor_scalar(out, in0, s1, None, o0), r, w, n, per)
        else:
            vec(lambda: g.vector.tensor_scalar(out, in0, s1, s2, o0, o1), r, w, n, per)

    def tt(out, a, b, o, r, w, per=None):
        vec(lambda: g.vector.tensor_tensor(out, a, b, o), r, w, width(b), per or (1 if any(k[0] == "P" for k in r) else 2))

    def cp(out, a, r, w, per=None, n=None):
        vec(lambda: g.vector.tensor_copy(out, a), r, w, n or width(a), per or (0.5 if short(out, a) else 1))

    def ms(out, c, w):
        vec(lambda: g.vector.memset(out, c), [], w, width(out), 0.5 if short(out) else 1)

    def scan(out, a, b, init, o0, o1, r, w):
        vec(lambda: g.vector.tensor_tensor_scan(out, a, b, init, o0, o1), r, w, width(out), 0.5 if short(out, a, b) else 1)

    def act(out, a, func, r, w, bias=0.0, scale=1.0, per=None, n=None):
        fn = (lambda: g.scalar.activation(out, a, func)) if n else (lambda: g.scalar.activation(out, a, func, bias=bias, scale=scale))
        note("s", fn, r, w, 0.07 + CYCLE * (n or width(out)) * per if per else S_CALL + CYCLE * width(out))

    def mm(items, w, first=True, last=True, alone=False):
        def fn():
            for i, (o, l, x, r) in enumerate(items):
                ins = g.tensor.matmul(o, l, x, alone or (first and i == 0), alone or (last and i == len(items) - 1))
            return ins
        note("p", fn, [k for it in items for k in it[3]], w,
             sum(T_CYCLE * max(64, width(it[2])) * (1 if short(it[2]) else 4) for it in items))

    def iota(out, pat, base, mult, w, small=True, r=()):
        busy = 0.13 + 2 * CYCLE * width(out)
        if small:
            note("g", lambda: g.iota(out, pat, base, mult, allow_small_or_imprecise_dtypes=True), list(r), w, busy)
        else:
            note("g", lambda: g.iota(out, pat, base, mult), list(r), w, busy)

    def fill(out, n, c, w, r=()):
        iota(out, [[0, n]], c, 0, w, r=r)

    def keep(nm, src, pat, cmp, other, base, mult):
        note("g", lambda: g.affine_select(T[nm][:], T[src][:], pat, cmp, other, base, mult), [src], [nm], 0.17 + 256 * CYCLE)

    def issue():
        n = len(calls)
        succ, left, way = [[] for _ in calls], [len(c["dep"]) for c in calls], [0.0] * n
        for i, c in enumerate(calls):
            for d in c["dep"]:
                succ[d].append(i)

        def lag(d, i):
            return calls[d]["after"] + (0.0 if calls[d]["e"] == calls[i]["e"] == "p" else SIGNAL)

        for i in range(n - 1, -1, -1):
            way[i] = calls[i]["busy"] + max([calls[i]["after"]] + [lag(i, j) + way[j] for j in succ[i]])
        free, end, ready = {e: 0.0 for e in list(Q) + [None]}, [None] * n, {e: {} for e in list(Q) + [None]}
        cnt, seen, ends = {e: 0 for e in SEM}, {e: {} for e in Q}, {}
        main = {e: [i for i in range(n - 1, -1, -1) if calls[i]["e"] == e and not calls[i]["side"]] for e in ready}
        for i in range(n):
            if not left[i]:
                ready[calls[i]["e"]][i] = 0.0

        before = {}
        for e in main:
            before.update(zip(main[e][:-1], main[e][1:]))

        def soonest(i, memo, now):
            if i not in memo:
                if way[i] < now - 8.0:
                    return 1e6
                x = [(end[d] if end[d] is not None else soonest(d, memo, 0) + calls[d]["busy"]) + lag(d, i) for d in calls[i]["dep"]]
                d = before.get(i)
                memo[i] = max(x + [free[calls[i]["e"]] if d is None or end[d] is not None else soonest(d, memo, 0) + calls[d]["busy"]])
            return memo[i]

        for _ in range(n):
            pick, memo = None, {}
            now = max(way[m[-1]] for m in main.values() if m) if any(main.values()) else 0.0
            for e in ready:
                top = main[e][-1] if main[e] else None
                due, far = (soonest(top, memo, now), way[top]) if main[e] else (1e9, 0.0)
                side = [(max(free[e], r), -way[i], i) for i, r in ready[e].items()
                        if calls[i]["side"] and (max(free[e], r) + calls[i]["busy"] <= due + SPARE or ((way[i] > far + AHEAD or calls[i]["side"] == 2) and r <= due) or top not in ready[e] and way[i] > far)]
                i = min(side)[2] if side else top if top in ready[e] else None
                if i is not None and (pick is None or max(free[e], ready[e][i]) < pick[0]):
                    pick = (max(free[e], ready[e][i]), i)
            at, i = pick
            c, e = calls[i], calls[i]["e"]
            del ready[e][i]
            if not c["side"]:
                main[e].pop()
            end[i] = at + c["busy"]
            if e is not None:
                free[e] = end[i]
                for d in sorted(c["dep"], key=lambda j: -calls[j]["tok"][1]):
                    sem, val = calls[d]["tok"]
                    if not (e == "p" and calls[d]["e"] == "p") and seen[e].get(sem, 0) < val:
                        Q[e].wait_ge(T.sem[sem], val)
                        seen[e][sem] = val
                ins = c["fn"]()
                if c["tok"] is None:
                    cnt[e] += 1
                    ins.then_inc(T.sem[SEM[e]], 1)
                    c["tok"] = (SEM[e], cnt[e])
            ends[c["tok"][0]] = c["tok"][1]
            for j in succ[i]:
                left[j] -= 1
                if not left[j]:
                    ready[calls[j]["e"]][j] = max(end[d] + lag(d, j) for d in calls[j]["dep"])
        for sem in ends:
            if all(seen[e].get(sem, 0) < ends[sem] for e in Q):
                g.wait_ge(T.sem[sem], ends[sem])

    def diag(nm, src, c):
        keep(nm, src, [[-1, 128]], A.not_equal, c, 0, 1)

    def above(nm, src):
        keep(nm, src, [[1, 128]], A.is_gt, 0.0, 0, -1)

    def block(nm, zero, c):
        keep(nm, zero, [[16, 8], [0, 16]], A.is_gt, c, 0, -1)
        keep(nm, nm, [[16, 8], [0, 16]], A.is_ge, 0.0, 15, -1)

    others = [q for q in range(N) if q != me]

    def did(q):
        a = topo.addr(T.cores[q])
        return DstId(rid=a[0], pnc=a[1])

    def common(src):
        return [e for e in topo.engines(T.cores[src], T.cores[(src + 1) % N])
                if all(e in topo.engines(T.cores[src], T.cores[q]) for q in range(N) if q != src)]

    def deal(src):
        eng, dst = common(src), [q for q in range(N) if q != src]
        n = {q: 1 for q in dst}
        grow = True
        while grow:
            grow = False
            for q in sorted(dst, key=lambda x: n[x]):
                if sum(n.values()) + n[q] <= len(eng):
                    n[q] *= 2
                    grow = True
                    break
        out, at = {}, 0
        for q in dst:
            out[q] = eng[at:at + n[q]]
            at += n[q]
        return out

    def bits(es):
        return sum(1 << e for e in es)

    def bcast(src, dst, rsem, lsem, r, after, busy=0.4):
        es = common(me)
        note("g", lambda: g.remote_dma_fused([RemoteDMATransfer(dst_ids=[did(q) for q in others], dma_engine_mask=bits(es), remote_sem=T.sem[rsem],
                                                                srcs=[src], dsts=[dst] * len(others))], local_sem=T.sem[lsem]),
             r, [lsem], busy, after, (lsem, len(es)))

    nb = sum(len(common(q)) for q in others)

    def arrive(key, sem, n, sent):
        note(None, None, sent, [], 0.0, 0.0, (sem, n))
        wr[key] = len(calls) - 1

    ps = T.ps
    mine = slice(me * V, (me + 1) * V)

    def near(q):
        return [p for p in range(N) if topo.die(T.cores[p]) == topo.die(T.cores[q])]

    def crossing(q):
        far = [p for p in range(N) if p not in near(q)]
        return [(q * V + h * (V // 2), far[(2 * near(q).index(q) + h) % len(far)]) for h in range(2)]

    def send(parts, rsem, lsem, r, after, busy=0.4):
        es = common(me)
        n = len(es) // len(parts)
        note("g", lambda: g.remote_dma_fused([RemoteDMATransfer(dst_ids=[did(q) for q in to], dma_engine_mask=bits(es[n * i:n * i + n]),
                                                                remote_sem=T.sem[rsem], srcs=[x], dsts=[x] * len(to))
                                              for i, (x, to) in enumerate(parts)], local_sem=T.sem[lsem]),
             r, [lsem], busy, after, (lsem, n * len(parts)))

    def share_alpha(u, t, busy=0.4):
        x, mates_, e = T["aw%d" % u], [q for q in near(me) if q != me], len(common(me))
        taken = {p: [c for q in range(N) for c, to in crossing(q) if to == p] for p in range(N)}
        send([(x[:, c:c + V // 2], [to]) for c, to in crossing(me)], "ah%d" % t, "lx%d" % t, ["aw%dm" % u], 2.5, busy)
        send([(x[:, mine], mates_)], "aa%d" % t, "la%d" % t, ["aw%dm" % u], 3.5)
        arrive("aw%dh" % u, "ah%d" % t, len(taken[me]) * (e // 2), ["lx%d" % t])
        send([(x[:, c:c + V // 2], mates_) for c in taken[me]], "aa%d" % t, "lf%d" % t, ["aw%dh" % u], 2.5)
        arrive("aw%dr" % u, "aa%d" % t, 2 * e * len(mates_), ["la%d" % t, "lf%d" % t])

    def col(j):
        return T.cf[:, j:j + 1]

    def sh(x, r):
        return x[:, 15 - r:143 - r]

    def wide(base, items, first=True, last=True):
        for j, (a, b) in enumerate(((0, 512), (512, V))):
            for i, (l, x) in enumerate(items):
                step = 512 if short(T[x]) else 128
                for c in range(a, b, step):
                    d = min(b, c + step)
                    mm([(ps[:, 512 * base + c:512 * base + d], T[l][:], T[x][:, c:d], [l, x])], ["P%d" % (base + j)],
                       first and i == 0, last and i == len(items) - 1)

    def pieces(items, w, n):
        for i in range(0, len(items), n):
            mm(items[i:i + n], w, i == 0, i + n >= len(items))

    def bucket(x, o):
        return x[:, RG * o + RG - CAP:RG * o + RG]

    XB, TW = ["xb%d" % o for o in range(N)], ["tw%d" % o for o in range(N)]

    def bids(tb, t):
        dl = deal(me)
        note("g", lambda: g.remote_dma_fused([RemoteDMATransfer(dst_ids=[did(q)], dma_engine_mask=bits(dl[q]), remote_sem=T.sem["ab%d" % t],
                                                                srcs=[bucket(T.tw, q)], dsts=[tb[:, CAP * me:CAP * me + CAP]])
                                              for q in others], local_sem=T.sem["lt%d" % t]),
             TW, ["lt%d" % t], 0.4, 3.0, ("lt%d" % t, sum(len(dl[q]) for q in others)))

    def empty_buckets(r):
        for o in range(N):
            fill(bucket(T.xb, o), CAP, V * o + V + 1, [XB[o]], r)

    dma("y", "ld0", T.aw0[:, mine], T.al[:], [], ["aw0m", "q0"], 2.6)
    dma("s", "ld1", T.hbi[0:8, :], T.hb[:], [], ["hbi", "q1"], 2.0)
    dma("s", "ld4", T.hni[:], T.hn[:], [], ["hni"], 3.5)
    dma("y", "ld2", T.fti[:, 0:B], T.ft[:], [], ["fti"], 4.3)
    dma("y", "ld3", T.utb[:, 0:B], T.ut[:], [], ["utb"], 4.8)
    iota(T.ci[:, 4:5], [[0, 1]], 0, 1, ["pcol"], small=False)
    iota(T.crow[:], [[1, 152]], 0, 0, ["crow"])
    iota(T.dm[:], [[-1, 128]], 0, 1, ["dm"])
    iota(T.grow[:], [[16, 8], [0, 16]], 0, 0, ["grow"])
    iota(T.rev[:, 0:B], [[-1, B]], B + 33, 0, ["rev"])
    share_alpha(0, 0, 3.5)

    (R, G16, O7, PF, UP, C15, P15, RM1, KW, EW, NS, NV, OM, LOW, OW, GB, T0, D0, D1, D2, NR, VW, KX) = range(23)

    def lin(j, src, a, b):
        act(col(j), col(src), F.Identity, ["c%d" % src], ["c%d" % j], bias=b, scale=a)

    def scaled(nm, src, c):
        ts(T[nm][:], T[src][:], c if isinstance(c, float) else col(c), None, A.mult, None,
           [src] + ([] if isinstance(c, float) else ["c%d" % c]), [nm])

    side(True)
    ms(T.lw[:, 0:L], 0.25, ["lw"])
    ms(T.lx[:, 0:L], 0.25, ["lx"])
    ms(T.h1[:], 0.0, ["h1"])
    ms(T.zer[:], 0.0, ["zer"])
    ts(T.ci[:, 0:1], T.ci[:, 4:5], 15, None, A.bitwise_and, None, ["pcol"], ["ci0"])
    ts(T.ci[:, 1:2], T.ci[:, 4:5], 7, None, A.bitwise_and, None, ["pcol"], ["ci1"])
    cp(col(PF), T.ci[:, 4:5], ["pcol"], ["c3"])
    cp(col(R), T.ci[:, 0:1], ["ci0"], ["c0"])
    cp(col(O7), T.ci[:, 1:2], ["ci1"], ["c2"])
    ts(col(P15), col(PF), 16.0, 15.0, A.mult, A.add, ["c3"], ["c6"])
    tt(col(G16), col(PF), col(R), A.subtract, ["c3", "c0"], ["c1"])
    ts(col(UP), col(R), 7.5, None, A.is_gt, None, ["c0"], ["c4"])
    ts(T.x4[:], T.crow[:, 0:144], col(P15), None, A.is_equal, None, ["crow", "c6"], ["x4"])
    ts(T.dg[:], T.crow[:, 0:16], col(R), None, A.is_equal, None, ["crow", "c0"], ["dg"])
    ts(T.lf[:, 0:16], T.crow[:, 0:16], col(R), None, A.is_gt, None, ["crow", "c0"], ["lf"])
    ts(T.idb[:], T.dm[:], 0.0, None, A.is_equal, None, ["dm"], ["idb"])
    ts(T.pw[:], T.dg[:], 8192.0, None, A.mult, None, ["dg"], ["pw"])
    ts(T.bo[:], T.grow[:], col(G16), None, A.is_equal, None, ["grow", "c1"], ["bo"])
    ts(T.m2[:], T.dm[:], 0.0, -1.0, A.is_gt, A.mult, ["dm"], ["m2"])
    tt(T.cpk[:, 0:16], T.lf[:, 0:16], T.pw[:], A.add, ["lf", "pw"], ["cpk"])
    act(T.dc[:], T.crow[:, 0:48], F.Identity, ["crow"], ["dc"], bias=768.0, scale=16.0)
    lin(RM1, R, 1.0, -1.0)
    lin(NR, R, -1.0, 0.0)
    act(T.nid[:], T.idb[:], F.Identity, ["idb"], ["nid"], scale=-1.0)
    act(T.ndr[:], T.idb[:], F.Identity, ["idb", "c20"], ["ndr"], scale=col(NR))
    act(T.nbo[:], T.bo[:], F.Identity, ["bo"], ["nbo"], scale=-1.0)
    for j, src, a, b in ((C15, G16, 1.0, 15.0), (KW, R, float(PARTS[0][1]), 0.0), (KX, R, float(L - PARTS[0][1]), 0.0), (OM, O7, 1.0, MAGIC), (T0, O7, float(RG), RG + 1.0), (LOW, UP, -1.0, 1.0),
                         (GB, R, 1.0 / 128, -0.125), (D0, R, 4.0, 644.0), (D1, R, 4.0, 708.0), (D2, R, 4.0, 772.0)):
        lin(j, src, a, b)
    act(col(OW), col(T0), F.Identity, ["c16", "c4"], ["c14"], bias=-1.0, scale=col(UP))
    side(False)
    ts(T.tog[0:8, :], T.hbi[0:8, :], float(W), None, A.is_equal, None, ["hbi"], ["tog"])
    XL, X2 = ps[:, 1536:1584], ps[:, 1024:1072]
    mm([(XL, T.x4[0:8, 15 - r:143 - r], T.tog[0:8, r:B:16], ["x4", "tog"]) for r in range(16)], ["P3"])
    side(True)
    ts(T.cpk[:, 15:16], T.cpk[:, 15:16], -1.0 / 8192, None, A.mult, None, ["cpk"], ["cpk"])
    tt(T.m2[:], T.m2[:], T.bo[:], A.mult, ["m2", "bo"], ["m2"])
    cp(T.cpk[:, 16:32], T.cpk[:, 0:16], ["cpk"], ["cpk"])
    ms(T.sa[:], 256.0, ["sa"])
    cp(T.cpk[:, 32:64], T.cpk[:, 0:32], ["cpk"], ["cpk"])

    def ranks_old(first=False):
        mm([(X2, T.idb[:], T.dc[:], ["idb", "dc"])] + ([] if first else [(X2, T.nid[:], T.hd1[:], ["nid", "hd1"])]), ["P2"], last=False)

    def ranks():
        scan(T.cs[:], T.h1[:], XL, 0.0, A.add, A.add, ["h1", "h1b", "P3"], ["cs"])
        tt(T.h0[:], T.h1[:], XL, A.add, ["h1", "h1b", "P3"], ["h0"])
        tt(T.hd[:], T.dc[:], XL, A.mult, ["dc", "P3"], ["hd"])
        mm([(X2, T.bo[:], T.cs[:], ["bo", "cs"]), (X2, T.m2[:], T.h0[:], ["m2", "h0"]), (X2, T.ndr[:], T.h0[:], ["ndr", "h0"]),
            (X2, T.nid[:], T.hd[:], ["nid", "hd"])], ["P2"], first=False)

    ranks_old(True)
    side(False)
    ranks()
    side(True)
    ms(T.sb_[:], 0.0, ["sb"])
    cp(T.cpk[:, 64:128], T.cpk[:, 0:64], ["cpk"], ["cpk"])
    ms(T.sa[:, 16:L:STEP], 0.0, ["sa"])
    cp(T.cpk[:, 128:L], T.cpk[:, 0:128], ["cpk"], ["cpk"])
    ms(T.sb_[:, 16:L:STEP], 2.0 ** -116, ["sb"])
    scan(T.scl[:], T.sa[:], T.sb_[:], 2.0 ** -72, A.mult, A.add, ["sa", "sb"], ["scl"])
    for k in range(16):
        ts(T.sel[:, 128 * k:128 * k + 128], T.bo[:], T.dg[:, k:k + 1], None, A.mult, None, ["bo", "dg"], ["sel%d" % k])
    dma("y", "ld5", T.monb[:], T.mon[:], ["aw0r"], ["monb"], 2.5)
    iota(T.fti[:, B:B + 8], [[0, 8]], W, 0, ["ftz"], small=False)
    fill(T.utb[:, B:B + 16], 16, 1, ["utz"])
    for t in range(2):
        iota(T["aw%d" % t][:, W:W + 2], [[-1, 2]], 1, 0, ["aw%dz" % t])
    above("tri", "bo")
    above("nta", "nbo")
    diag("ta", "tri", -16.0)
    diag("mxa", "nta", 0.5)
    diag("nta", "nta", 16.0)
    diag("i32", "zer", 32.0)
    fill(T.zef[:], 128, 0, ["zef"])
    fill(T.ftf[:, B:B + 8], 8, W, ["ftfz"])
    block("bof", "zef", 1.0)
    block("bov", "zef", 1.0 / V)
    empty_buckets([])
    fill(T.xrow[:, L:L + 8], 8, 0, ["xrz"])
    block("dq", "zer", 0.5)
    above("tq", "dq")
    diag("tq", "tq", 8.0)
    diag("dq", "dq", 32.5)
    block("gq", "zer", -64.0)
    diag("gq", "gq", 2.0 ** 20)
    iota(T.uu[:, 0:144], [[-16, 3], [1, 48]], 0, 0, ["uu0"])
    iota(T.wc24[:], [[-V, N], [0, 4]], -1, 0, ["wc24"])
    for o in range(N):
        fill(bucket(T.tw, o), CAP, 1, [TW[o]])
    diag("idf", "zef", 1.0)
    diag("i8k", "zer", 8192.0)
    diag("n94", "zer", -0.9375)
    block("bo16", "zer", 0.0625)
    fill(T.nones[:], V, -1, ["nones"], ["lf0"])

    def slots():
        cp(T.hh[:], T.hni[:], ["hni"], ["hh"])
        act(T.mag[:], T.hh[:], F.Abs, ["hh"], ["mag"])
        act(T.nsw[:], T.hh[:], F.Sign, ["hh"], ["nsw"], scale=-1.0)
        act(T.em[:], T.mag[:], F.Relu, ["mag"], ["em"], bias=1.0, scale=-1.0)
        act(T.ol[:], T.nsw[:], F.Relu, ["nsw"], ["ol"])
        act(T.opn[:], T.mag[:], F.Sign, ["mag"], ["opn"], bias=4608.5, scale=-1.0)
        wide(4, [("ta", "em"), ("nbo", "em"), ("nta", "ol")])
        act(T.rl[:], ps[:, 2048:2048 + V], F.Relu, ["P4", "P5"], ["rl"])
        wide(6, [("ta", "em"), ("i32", "em"), ("i32", "ol"), ("nid", "rl")])

    def late_constants():
        ts(T.x1[:], T.crow[:, 0:144], col(C15), None, A.is_equal, None, ["crow", "c5"], ["x1"])
        cp(T.ftf[:, 0:B], T.fti[:, 0:B], ["fti"], ["ftf"])
        scaled("mxb", "m2", 1.0 / 64)
        scaled("olm", "bo", OW)
        scaled("xk0", "x1", KW)
        scaled("xk1", "x1", KX)
        ts(T.low[:], T.sa[:], 0.0, col(LOW), A.mult, A.add, ["sa", "c13"], ["low"])
        ts(T.jl[:], T.crow[:, 0:16], 16.0, col(R), A.mult, A.add, ["crow", "c0"], ["jl"])

    def gap_constants():
        ts(T.cdd[:], T.uu[:, 0:144], col(R), None, A.is_gt, None, ["uu0", "c0"], ["cdd"])
        ms(T.lsc[:, 63:N * 64:64], 0.0, ["lsc%d" % o for o in range(N)])
        ms(T.eqs[:, 191:1152:192], 0.0, ["eqs%d" % o for o in range(N)])
        for c in range(3):
            x = T.cdd[:, CAP * c + CAP - 1:CAP * c + CAP]
            ts(x, x, col(D0 + c), None, A.mult, None, ["cdd", "c%d" % (D0 + c)], ["cdd%d" % c])
        scaled("x8", "x1", 8192.0)
        scaled("x1f", "x1", 1.0)

    def last_constants():
        fill(T.tt[:], 840, 1, ["tt"], ["lf0"])
        for t in range(2):
            fill(T["ev%d" % t][:, 480:488], 8, 0, ["ev%dz" % t])
        iota(T.nam[:, 0:B], [[1, B]], me * B + 1, 0, ["nam"], r=["lf0"])
        iota(T.nam[:, B:B + 512], [[1, 512]], me * B + 1, 0, ["nam2"], r=["lf0"])
        iota(T.rev[:, B:B + 512], [[-1, 512]], B + 33, 0, ["rev2"], r=["lf0"])
        for j, src, a, b in ((EW, UP, 2.0, -1.0), (NS, UP, -32767.0, -1.0), (NV, UP, -24576.0, 0.0)):
            lin(j, src, a, b)
        ts(T.c8[:, 0:8], T.crow[:, 0:8], col(O7), None, A.is_gt, None, ["crow", "c2"], ["c8t"])
        ts(T.pw[:, 0:8], T.crow[:, 0:8], col(O7), 16384.0, A.is_equal, A.mult, ["crow", "c2"], ["pw"])
        scaled("x4f", "x4", 16.0)
        tt(T.c8[:, 0:8], T.c8[:, 0:8], T.pw[:, 0:8], A.add, ["c8t", "pw"], ["c8t"])
        ts(T.xs[0:8, :], T.hbi[0:8, :], 1.0, None, A.add, None, ["hbi"], ["xs"])
        ts(T.c8[:, 7:8], T.c8[:, 7:8], -1.0 / 16384, None, A.mult, None, ["c8t"], ["c8t"])
        scaled("xe", "x1", EW)
        n = 8
        while n < 320:
            m = min(n, 320 - n)
            cp(T.c8[:, n:n + m], T.c8[:, 0:m], ["c8t"], ["c8t"])
            n += m

    P45, P67, NN = ps[:, 2048:2048 + V], ps[:, 3072:3072 + V], ps[:, 192:192 + V]

    KF, TL, TL0 = ps[:, 3968:4048], ps[:, 2560:2608], ps[:, 3712:3760]

    def target(bias):
        act(T.em[:], P67, F.Abs, ["P6", "P7"], ["em"], bias=bias)
        act(T.dsb[:], P67, F.Identity, ["P6", "P7"], ["dsb"], bias=bias)
        act(T.tgt[:], T.em[:], F.Relu, ["em"], ["tgt"], bias=1.0, scale=-1.0)
        wide(6, [("tq", "opn"), ("nid", "dsb"), ("gq", "tgt")])
        act(T.gg[:], P67, F.Relu, ["P6", "P7", "c15"], ["gg"], bias=col(GB), scale=1.0 / 64)
        wide(6, [("i8k", "nones"), ("idf", "mag"), ("i8k", "tgt")])
        act(T.tm[:], P67, F.Relu, ["P6", "P7"], ["tm"])
        wide(6, [("bo16", "tgt"), ("n94", "nones")])
        pieces([(KF, sh(T.x8, r), T.tgt[:, r:V:8], ["x8", "tgt"]) for r in range(8)]
               + [(KF, sh(T.x1f, 8 + r), T.tm[:, r:V:8], ["x1f", "tm"]) for r in range(8)], ["P7"], 2)

    tgc = ("tg0", "tg1")
    slots()
    late_constants()
    gap_constants()
    last_constants()
    pieces([(TL0, T.x4f[0:8, 15 - r:143 - r], T.xs[0:8, r:B:16], ["x4f", "xs"]) for r in range(16)], ["P7"], 2)
    cp(T.tg0[:], TL0, ["P7"], ["tg0"])
    target(-16.0)
    side(False)

    for t in range(RO):
        u, un = t % 2, (t + 1) % 2
        aw, awn, ev, tb, lb = T["aw%d" % u], T["aw%d" % un], T["ev%d" % u], T["tb%d" % u], T["lb%d" % u]
        AW = ["aw%dm" % u, "aw%dr" % u, "aw%dz" % u, "aw%dh" % u]
        s0 = (L * t) % B
        ts(T.offu[:], X2, col(RM1), None, A.add, None, ["P2", "c7"], ["offu"])
        r = ["offu", "rev"] + (["rev2"] if t else [])
        act(T.lx[:, :].indirect(T.offu[:, SPLIT // 16:48]), T.rev[:, s0 + SPLIT:s0 + B], F.Silu, r, ["lx"], per=SCATTER, n=B - SPLIT)
        cp(T.lw[:, :].indirect(T.offu[:, 0:SPLIT // 16]), T.rev[:, s0:s0 + SPLIT], r, ["lw"], SCATTER)
        side(True)
        ts(T.offc[:], X2, col(RM1), float(L), A.add, A.min, ["P2", "c7"], ["offc"])
        side(False)

        def rows(j):
            a, b = HALF[j]
            scan(T.dsc[:, a:b], T.lw[:, a:b], T.cpk[:, 0:b - a], 0.0, A.max, A.mult, ["lw", "cpk"], ["dsc%d" % j])
            scan(T.y1[:, a:b], T.lx[:, a:b], T.cpk[:, 0:b - a], 0.0, A.max, A.mult, ["lx", "cpk"], ["y1%d" % j] + (["y10"] if j else []))

        def buyers(j):
            a, b = HALF[j]
            tt(T.w24[:, a // 16:b // 16], T.dsc[:, a + 15:b:16], T.y1[:, a + 15:b:16], A.min, ["dsc%d" % j, "y1%d" % j], ["w24"])
            ts(T.bl[:, a // 16:b // 16], T.w24[:, a // 16:b // 16], B + 33.3, float(B), A.add, A.min, ["w24"], ["bl%d" % j])

        def lists(j):
            a, b = HALF[j]
            x = T.bl[:, a // 16:b // 16]
            cp(T.gl[:, a:b], T.fti[:, :].indirect(x), ["fti", "ftz", "bl%d" % j], ["gl%d" % j], GATHER, b - a)
            tt(T.utl[:, a:b], T.utb[:, :].indirect(x), T.scl[:, a:b], A.mult, ["utb", "utz", "scl", "bl%d" % j], ["utl%d" % j], GATHER)

        def spread(c):
            a, b, b0 = CH[c], CH[c + 1], 512 * (c % 3)
            mm([(ps[:, b0 + k:b0 + 16 * (b - a):16], T.sel[:, 128 * k:128 * k + 128], T.utl[:, a:b],
                 ["sel%d" % k, "utl0"] + (["utl1"] if b > HALF[0][1] else [])) for k in range(16)], ["P%d" % (c % 3)], alone=True)

        def gather(c):
            a, b = CH[c], CH[c + 1]
            act(T.ag[:, 16 * a:16 * b], aw[:, :].indirect(T.gl[:, a:b]), F.Identity,
                AW + ["gl0"] + (["gl1"] if b > HALF[0][1] else []), ["ag%d" % c], per=GATHER)

        def product(c):
            a, b, b0 = CH[c], CH[c + 1], 512 * (c % 3)
            x = T.ag[:, 16 * a:16 * b]
            tt(x, x, ps[:, b0:b0 + 16 * (b - a)], A.mult, ["ag%d" % c, "P%d" % (c % 3)], ["ag%d" % c])
            if c + 3 < NC:
                spread(c + 3)

        def largest(c):
            a, b = CH[c], CH[c + 1]
            scan(T.ms[:, 8 * a:8 * b], T.ag[:, 16 * a:16 * b:2], T.ag[:, 16 * a + 1:16 * b:2], 0.0, A.max, A.max,
                 ["ag%d" % c], ["ms%d" % c])

        BV, BM, BX = (3, 1), (4, 0), (5, 2)

        def chunks(j):
            a, b = PARTS[j]
            return [c for c in range(NC) if CH[c] < b and CH[c + 1] > a]

        def maxima(j):
            a, b = PARTS[j]
            cp(ps[:, 512 * BM[j]:512 * BM[j] + b - a], T.ms[:, 8 * a + 7:8 * b:8], ["ms%d" % c for c in chunks(j)], ["P%d" % BM[j]])

        def vote(j, k):
            a, b = PARTS[j]
            mm([(ps[:, 512 * BV[j]:512 * BV[j] + b - a], sh(T.x1, k), T.top[:, 16 * a + (b - a) * k:16 * a + (b - a) * (k + 1)],
                 ["x1", "top%d_%d" % (j, k)])], ["P%d" % BV[j]], first=(k == 0), last=(k == 15))

        def best(j, k):
            a, b = PARTS[j]
            tt(T.top[:, 16 * a + (b - a) * k:16 * a + (b - a) * (k + 1)], T.ag[:, 16 * a + k:16 * b:16], ps[:, 512 * BM[j]:512 * BM[j] + b - a],
               A.not_equal, ["ag%d" % c for c in chunks(j)] + ["P%d" % BM[j]], ["top%d_%d" % (j, k)])
            vote(j, k)

        def choice(j):
            a, b = PARTS[j]
            n, s = b - a, str(j)
            pv, pm, px = "P%d" % BV[j], "P%d" % BM[j], "P%d" % BX[j]
            v0, v1 = ps[:, 512 * BV[j]:512 * BV[j] + n], ps[:, 512 * BV[j] + 256:512 * BV[j] + 256 + n]
            m0, m1 = ps[:, 512 * BM[j]:512 * BM[j] + n], ps[:, 512 * BM[j] + 256:512 * BM[j] + 256 + n]
            x0 = ps[:, 512 * BX[j]:512 * BX[j] + n]
            act(T.wv[:, a:b], v0, F.Silu, [pv], ["wv" + s], bias=-16.0, scale=-4.0)
            mm([(m0, T.mxa[:], T.wv[:, a:b], ["mxa", "wv" + s]), (m0, T.mxb[:], T.wv[:, a:b], ["mxb", "wv" + s])], [pm])
            ts(m0, m0, 0.0, None, A.is_lt, None, [pm], [pm])
            tt(T.y1[:, a:b], T.xc[:, a:b], m0, A.mult, ["xc", pm], ["y1" + s])
            mm([(v0, T.bov[:], T.y1[:, a:b], ["bov", "y1" + s])], [pv])
            act(T.ch[:, a:b], m0, F.Identity, [pm], ["ch" + s])
            mm([(x0, T.bof[:], T.y1[:, a:b], ["bof", "y1" + s])], [px])
            act(T.xrow[:, a:b], x0, F.Identity, [px], ["xrow" + s], bias=320.5)
            ts(T.ind[:, a:b], v0, MAGIC, col(OM), A.add, A.is_equal, [pv, "c12"], ["ind" + s])
            init = 0.0 if j == 0 else ps[:, 512 * BV[j - 1] + 255 + a - PARTS[j - 1][0]:512 * BV[j - 1] + 256 + a - PARTS[j - 1][0]]
            scan(v1, T.low[:, a:b], T.ind[:, a:b], init, A.mult, A.add, ["low", "ind" + s] + (["P%d" % BV[j - 1]] if j else []), [pv])
            tt(T.zz[:, a:b], T.ind[:, a:b], v1, A.mult, ["ind" + s, pv], ["zz" + s])
            mm([(m1, T.olm[:], T.zz[:, a:b], ["olm", "zz" + s])], [pm])
            scan(T.dsc[:, a:b], m1, T.cpk[:, 0:n], 0.0, A.max, A.mult, [pm, "cpk"], ["dsc0", "dsc1"] if j == 0 else ["dsd"])
            ts(T.bu[:, a // 16:b // 16], T.dsc[:, a + 15:b:16], -1.0, None, A.mult, None, ["dsc0"] if j == 0 else ["dsd"], ["bu" + s])
            cp(T.xb[:, :].indirect(T.bu[:, a // 16:b // 16]), T.xrow[:, a:b], ["bu" + s, "xrow" + s], XB, SCATTER)

        def masks(j):
            a, b = PARTS[j]
            s, px, x1 = str(j), "P%d" % BX[j], ps[:, 512 * BX[j] + 256:512 * BX[j] + 256 + (b - a) // 16]
            pieces([(x1, T.idb[:], T.jl[:, 0:(b - a) // 16], ["idb", "jl"])]
                   + [(x1, sh(T["xk" + s], r), T.ch[:, a + r:b:16], ["xk" + s, "ch" + s]) for r in range(16)], [px], 6)
            cp(T.ku[:, a // 16:b // 16], x1, [px], ["ku" + s])
            act(T.sgn[:, a:b], T.top[:, 16 * a:16 * b].indirect(T.ku[:, a // 16:b // 16]), F.Identity,
                ["ku" + s] + ["top%d_%d" % (j, k) for k in range(16)], ["sgn" + s], bias=-1.0, scale=2.0, per=GATHER)
            tt(T.tw[:, :].indirect(T.bu[:, a // 16:b // 16]), T.sgn[:, a:b], T.nml[:, a:b], A.mult, ["bu" + s, "sgn" + s, "nml"], TW, SCATTER)

        rows(0)
        buyers(0)
        side(True)
        rows(1)
        side(False)
        lists(0)
        for c in range(2):
            spread(c)
            gather(c)
        buyers(1)
        lists(1)
        spread(2)
        for c in range(2, NC):
            gather(c)
        act(T.xc[:], T.ftf[:, :].indirect(T.bl[:, :]), F.Identity, ["ftf", "ftfz", "bl0", "bl1"], ["xc"], bias=-319.5, per=GATHER)
        side(True)
        act(T.nml[:], T.nam[:, 0:B + 8].indirect(T.bl[:, :]), F.Identity, ["nam", "nam2", "bl0", "bl1"], ["nml"], per=GATHER)
        side(False)
        product(0)
        c0 = chunks(0)[-1] + 1
        for c in range(1, c0 + 1):
            product(c)
            largest(c - 1)
        maxima(0)
        for k in range(16):
            best(0, k)
            if (k + 1) % (16 // (NC - c0)) == 0 and c0 + 1 < NC - BEHIND:
                c0 += 1
                product(c0)
                largest(c0 - 1)
        side(2)
        choice(0)
        side(True)
        masks(0)
        side(False)
        for c in range(c0 + 1, NC):
            product(c)
            largest(c - 1)
        largest(NC - 1)
        maxima(1)
        for k in range(16):
            best(1, k)
        choice(1)
        side(True)
        masks(1)
        bids(tb, t)
        act(T.xg[:], T.xrow[:, :].indirect(T.offc[:, :]), F.Identity, ["xrow0", "xrow1", "xrz", "offc"], ["xg"], per=GATHER)
        pieces([(TL, sh(T.x1f, r), T.xg[:, r:B:16], ["x1f", "xg"]) for r in range(16)], ["P5"], 2)
        side(False)

        def entries(o):
            scan(T.lsc[:, 64 * o:64 * o + CAP], bucket(T.xb, o), T.cpk[:, 0:CAP], 0.0, A.max, A.mult, [XB[o], "cpk"], ["lsc%d" % o])

        def compare(o):
            for c in range(3):
                e0 = 192 * o + CAP * c
                ts(T.eqb[:, e0:e0 + CAP], bucket(T.xb, o), T.lsc[:, 64 * o + 16 * c + 15:64 * o + 16 * c + 16], 0.0,
                   A.add, A.is_equal, [XB[o], "lsc%d" % o], ["eqb%d_%d" % (o, c)])

        def repeated(o):
            scan(T.eqs[:, 192 * o:192 * o + 144], T.eqb[:, 192 * o:192 * o + 144], T.cdd[:], 0.0, A.max, A.mult,
                 ["eqb%d_%d" % (o, c) for c in range(3)] + ["cdd0", "cdd1", "cdd2"], ["eqs%d" % o])

        for o in range(N):
            entries(o)
        for o in range(N):
            compare(o)
            if o > 0:
                repeated(o - 1)
        tt(T.w24[:], T.wc24[:], T.lsc[:, 15:N * 64:16], A.subtract, ["wc24"] + ["lsc%d" % o for o in range(N)], ["w24"])
        repeated(N - 1)
        tt(T.lf[:], T.eqs[:, 47:1152:48], T.w24[:], A.max, ["w24"] + ["eqs%d" % o for o in range(N)], ["lf"])
        cp(T.lu[:], T.lf[:], ["lf"], ["lu"])
        bcast(T.lu[:], lb[:, 24 * me:24 * me + 24], "ab%d" % t, "ll%d" % t, ["lu", "lf%d" % t], 2.2)
        arrive("bids", "ab%d" % t, nb + sum(len(deal(q)[me]) for q in others), ["lt%d" % t, "ll%d" % t])
        side(True)
        if t + 1 < RO:
            ms(T.lw[:, 0:L], 0.25, ["lw"])
            act(T.lx[:, 0:L], T.nml[:], F.Identity, ["nml"], ["lx"], bias=0.25, scale=0.0)
            for o in range(N):
                ms(bucket(T.xb, o), float(V * o + V + 1), [XB[o]])
            tt(P67, aw[:, mine], P67, A.mult, ["aw%dm" % u, "P6", "P7"], ["P6", "P7"])
        rot = ((0, 32, 16), (32, 48, -32)) if t + 1 < RO else ((0, 48, 0),)
        for a, b, d in rot:
            cp(T.h1[:, a:b], T.h0[:, a + d:b + d], ["h0"], ["h1"] if a == 0 else ["h1b"])
        if t + 1 < RO:
            tt(T.hd1[:], T.h1[:], T.dc[:], A.mult, ["h1", "h1b", "dc"], ["hd1"])
        ko, kn = tgc[t % 2], tgc[(t + 1) % 2]
        ts(T.m48[:], TL, 0.5, None, A.is_lt, None, ["P5"], ["m48"])
        tt(T.t48[:], T.m48[:], T[ko][:], A.mult, ["m48", ko, ko + "b"], ["t48"])
        for a, b, d in rot:
            tt(T[kn][:, a:b], T.t48[:, a + d:b + d], ps[:, 2560 + a + d:2560 + b + d], A.max, ["P5", "t48"], [kn if a == 0 else kn + "b"])
        ts(T.m48[:], T[kn][:], 1.0 / 128, -0.5625, A.mult, A.add, [kn, kn + "b"], ["m48"])
        ts(T.tgu[:], T.m48[:], MAGIC, -MAGIC, A.add, A.add, ["m48"], ["tgu"])
        if t + 1 == RO:
            ts(T.offu[:], T[kn][:], 1.0 / 16, -1.0, A.mult, A.add, [kn], ["offu"])
            ts(T.t48[:], T[kn][:], 2.0 ** -16, -2.0 ** -12, A.mult, A.add, [kn], ["t48"])
            tt(T.xs[:], aw[:, :].indirect(T.offu[:, :]), T.monb[:], A.mult, AW + ["offu", "monb"], ["xs"], GATHER)
        side(False)
        for q in range(N - 1, -1, -1):
            if q == me:
                x, y, r = bucket(T.tw, me), T.lu[:, 4 * me:4 * me + 3], [TW[me], "lu"]
            else:
                x, y, r = tb[:, CAP * q:CAP * q + CAP], lb[:, 24 * q + 4 * me:24 * q + 4 * me + 3], ["bids"]
            ts(T.tt[:, :].indirect(y), x, 1.0, 1.0, A.mult, A.add, r, ["tt"], SCATTER)
        for j in range(2):
            act(ps[:, 192 + 320 * j:512 + 320 * j], T.tt[:, 320 * j:320 * j + 320], F.Abs, ["tt"], ["P%d" % j], bias=-1.0)
        tt(P67, T.tt[:, 0:V], P67, A.max, ["tt", "P6", "P7"], ["P6", "P7"])

        def new_alpha(a, b, w):
            if t + 1 < RO:
                tt(awn[:, me * V + a:me * V + b], aw[:, me * V + a:me * V + b], ps[:, 3072 + a:3072 + b], A.min, ["aw%dm" % u, "P6", "P7"], w)
            else:
                ts(T.fac[:, me * V + a:me * V + b], ps[:, 3072 + a:3072 + b], 1.0, None, A.min, None, ["P6", "P7"], ["facm"])

        for j in range(2):
            scan(T.uu[:, 320 * j:320 * j + 320], ps[:, 192 + 320 * j:512 + 320 * j], T.c8[:], 0.0, A.max, A.mult,
                 ["P%d" % j, "c8t"], ["uu%d" % j])
            if j == 0:
                new_alpha(0, EARLY, ["aw%dm" % un])
        ts(T.nab[:], T.uu[:, 7:V:8], col(NS), col(NV), A.mult, A.add, ["uu0", "uu1", "c10", "c11"], ["nab"])
        evm = ev[:, 80 * me:80 * me + 80]
        tt(evm, T.nab[:], KF, A.min, ["nab", "P7"], ["evm%d" % u])
        bcast(evm, evm, "ae%d" % t, "le%d" % t, ["evm%d" % u], 1.8)
        arrive("evr", "ae%d" % t, nb, ["le%d" % t])
        new_alpha(EARLY, V, ["aw%dm" % un])
        if t + 1 < RO:
            share_alpha(un, t + 1)
        else:
            bcast(T.fac[:, mine], T.fac[:, mine], "aa%d" % RO, "la%d" % RO, ["facm"], 3.5)
            arrive("facr", "aa%d" % RO, nb, ["la%d" % RO])
        side(True)
        tt(T.mv[:], T.gg[:], NN, A.min, ["gg", "P0", "P1"], ["mv"])
        act(T.nsw[:], T.mv[:], F.Sign, ["mv"], ["nsw"], bias=0.75, scale=-1.0)
        act(T.rl[:], T.mv[:], F.Relu, ["mv"], ["rl"], bias=64.0, scale=-64.0)
        if t + 1 < RO:
            ranks_old()
            fill(T.tt[:, 0:V], V, 1, ["tt"], ["lf%d" % (t + 1)])
        wide(4, [("i8k", "nones"), ("idf", "mag"), ("i8k", "nsw")])
        wide(6, [("idb", "dsb"), ("dq", "nsw"), ("nid", "rl")])
        tt(T.mag[:], T.mv[:], P45, A.max, ["mv", "P4", "P5"], ["mag"])
        if t + 1 < RO:
            target(24.0)
        side(False)
        s1 = (L * (t + 1)) % B if t + 1 < RO else 0
        tt(T.tog[:], ev[:, :].indirect(T.tgu[:, :]), T.nam[:, s1:s1 + B], A.is_equal,
           ["evm%d" % u, "evr", "ev%dz" % u, "tgu", "nam", "nam2"], ["tog"], GATHER)
        mm([(XL, sh(T.xe, r), T.tog[:, r:B:16], ["xe", "tog"]) for r in range(16)], ["P3"])
        if t + 1 < RO:
            ranks()

    side(True)
    ms(T.fac[:, 4096:4112], 0.0, ["facz"])
    tt(T.tm[:], aw[:, mine], T.fac[:, mine], A.mult, ["aw%dm" % u, "facm"], ["tm"])
    dma("s", "st0", T.yal[:], T.tm[:], ["tm"], [], 2.5)
    act(P67, P67, F.Sign, ["P6", "P7"], ["P6", "P7"], bias=-24.5, scale=-1.0)
    tt(T.hh[:], T.mag[:], P67, A.mult, ["mag", "P6", "P7"], ["hh"])
    dma("y", "st1", T.yh[:], T.hh[:], ["hh"], [], 2.5)
    side(False)
    tt(T.m48[:], T.h1[:], XL, A.add, ["h1", "P3"], ["m48"])
    tt(T.t48[:], T.m48[:], T.t48[:], A.max, ["m48", "t48"], ["t48"])
    ts(T.finu[:], T.t48[:], 4096.0, None, A.mult, None, ["t48"], ["finu"])
    for j, e in ((0, "y"), (1, "s")):
        a = 384 * j
        tt(T.xg[:, a:a + 384], T.fac[:, :].indirect(T.finu[:, 24 * j:24 * j + 24]), T.xs[:, a:a + 384], A.mult,
           ["facm", "facr", "facz", "finu", "xs"], ["yp%d" % j] + (["xg"] if j == 0 else []), GATHER)
        dma(e, "st%d" % (2 + j), T.yp[:, a:a + 384], T.xg[:, a:a + 384], ["yp%d" % j], [], 2.5)
    issue()
